import numpy as np, ml_dtypes
CORES = [3,7,11,15,131,135,139,143]
N = 8
BF = ml_dtypes.bfloat16
W, C, CUT, VI, HE, EPS = 2048, 128, 64, 4, 12, 192
def parts(rng, p):
    m = len(p); ty = rng.integers(24, 248, (m, 16)); s = rng.choice(m, (N, 8, W), p=p); u = rng.choice(m, (N, 8, C), p=p)
    x = np.clip(ty[s].transpose(0, 1, 3, 2) + rng.integers(-2, 3, (N, 8, 16, W)), 16, 255)
    x = np.where(rng.random(x.shape) < 0.01, rng.integers(16, 256, x.shape), x)
    ta = rng.integers(0, W, (N, 8, C)); iv = rng.integers(1, W // 8 + 1, (N, 8, 16, C))
    iv = np.where(rng.random((N, 8, 1, C)) < 0.25, rng.integers(1, W, iv.shape), iv)
    e = rng.choice(np.array([EPS // 4, EPS // 2, EPS - EPS // 8, EPS + EPS // 4]), (N, 8, 1, C))
    d = np.clip(32 * ty[u].transpose(0, 1, 3, 2) + rng.integers(-e, e + 1, (N, 8, 16, C)), 512, 8160)
    d = np.where(rng.random(d.shape) < 0.03, rng.integers(512, 8161, d.shape), d)
    return x, ta, iv, d
def gains(rng):
    return 0.5 + rng.random((N, 8, 16, W), dtype=np.float32)
def pack(x, gain, ta, iv, d):
    return {"xs": np.ascontiguousarray(x.reshape(N, 128, W)).astype(np.float32).astype(BF), "gn": np.ascontiguousarray(gain.reshape(N, 128, W)).astype(np.float32).astype(BF),
            "tau": np.ascontiguousarray(ta).astype(np.int32), "iv": np.ascontiguousarray(iv.reshape(N, 128, C)).astype(np.int32), "pf": np.ascontiguousarray(d.reshape(N, 128, C)).astype(np.int32)}
def setup_inputs(rng):
    x, ta, iv, d = parts(rng, [0.4, 0.3, 0.3])
    return pack(x, gains(rng), ta, iv, d)
def setup_inputs_spread(rng):
    x, ta, iv, d = parts(rng, [0.45, 0.3, 0.15, 0.1])
    iv = np.clip(np.exp2((W.bit_length() - 1) * rng.random(iv.shape)).astype(np.int64), 1, W - 1)
    return pack(x, gains(rng) * np.exp2(rng.integers(-1, 2, (N, 8, 1, W))), ta, iv, d)
def setup_inputs_ends(rng):
    i = np.arange(16); v = i[:, None] & i; par = (v ^ (v >> 1) ^ (v >> 2) ^ (v >> 3)) & 1
    ty = par[rng.permutation(16)[:4]][:, rng.permutation(16)] ^ rng.integers(0, 2, 16)
    s = np.repeat(rng.integers(1, 4, (N, 8, W // 8)), 8, axis=2); s[..., 1:17] = 0; s[..., W - 17:W - 1] = 0
    nf = np.where((rng.random((N, 8, W)) < 0.08) & (s > 0), rng.integers(3, 6, (N, 8, W)), 0)[:, :, None, :]
    x = ty[s].transpose(0, 1, 3, 2) ^ (np.argsort(rng.random((N, 8, 16, W), dtype=np.float32), axis=2) < nf)
    u = rng.integers(1, 4, (N, 8, C)); nd = np.where(rng.random((N, 8, C)) < 0.3, rng.integers(1, 5, (N, 8, C)), 0)
    for q in range(N - 1, -1, -2):
        u[q, :, 0] = 0; u[q, :, C - 1] = 0; nd[q, :, 0] = 0; nd[q, :, C - 1] = 16 - HE
    d = ty[u].transpose(0, 1, 3, 2) ^ (np.argsort(rng.random((N, 8, 16, C)), axis=2) < nd[:, :, None, :])
    near = (np.sum(d != ty[0][:, None], axis=2) <= 16 - HE) & (u > 0)
    d = np.where(near[:, :, None, :], ty[u].transpose(0, 1, 3, 2), d)
    mode = rng.integers(0, 3, (N, 8, 1, C)); iv = np.where(mode == 2, rng.integers(0, 2, (N, 8, 16, C)), mode)
    iv = np.where(iv == 1, W - 1, 1); jump = rng.random((N, 8, C)) < 0.8
    iv[:, :, 0] = np.where(jump, rng.integers(1, W, (N, 8, C)), iv[:, :, 0])
    iv[:, :, 8] = np.where(jump & (rng.random((N, 8, C)) < 0.5), rng.integers(1, W, (N, 8, C)), iv[:, :, 8])
    ta = np.where(rng.random((N, 8, C)) < 0.7, (W - 1) * rng.integers(0, 2, (N, 8, C)), rng.integers(0, W, (N, 8, C)))
    iv[..., 0] = 1; iv[..., C - 1] = W - 1; ta[..., 0] = 0; ta[..., C - 1] = W - 1
    gain = np.where(rng.random((N, 8, 16, W)) < 0.3, 0.125, 4.0)
    return pack(np.where(x == 1, 255, 16), gain, ta, iv, np.where(d == 1, 8160, 512))
def setup_inputs_corners(rng):
    x, ta, iv, d = parts(rng, [0.4, 0.3, 0.3]); z = rng.integers(24, 248, 16); junk = 16 + (z - 16 + 100) % 240
    k = np.arange(16); e = k % 2; nb = W // 64
    for q in range(N):
        for g in range(8):
            st = (2, 1, 3, 2)[(g + q) % 4]
            cs = rng.permutation(np.concatenate([np.array([0, C - 1]), 1 + rng.permutation(C - 2)[:nb - 2]]))
            b = 64 * rng.permutation(nb) - 1; on = (b[:, None] + st * k) % W; lt = (on + 1) % W
            mode = rng.integers(0, 9, (nb, 1)); state = rng.integers(0, 4, (nb, 16))
            for j, pat in enumerate((3 + 0 * k, 2 + 0 * k, e, (k == 15) * 1, (k == 0) * 1, 1 - e, 2 * e)):
                state = np.where(mode == j, pat[None, :], state)
            hc = np.zeros(W, bool); hc[on[(state & 1) > 0]] = True; hc[lt[(state & 2) > 0]] = True
            al = np.zeros(W, bool); al[on.reshape(-1)] = True; al[lt.reshape(-1)] = True
            rest = np.where(al[None, :], junk[:, None], x[q, g])
            far = np.argsort(rng.random((16, W)), axis=0) < rng.choice(np.array([0, 16 - HE, 17 - HE]), W, p=[0.7, 0.2, 0.1])[None, :]
            x[q, g] = np.where(hc[None, :] & ~far, z[:, None], rest)
            ta[q, g, cs] = (b - st) % W; iv[q, g][:, cs] = st
            pick = rng.choice(4, nb, p=[0.4, 0.25, 0.25, 0.1]); n1 = np.array([16, 16, HE, HE - 1])[pick]
            size = np.where(np.argsort(rng.random((16, nb)), axis=0) < n1[None, :], EPS, EPS + 1) * (pick > 0)[None, :]
            d[q, g][:, cs] = 32 * z[:, None] + rng.choice(np.array([-1, 1]), (16, nb)) * size
    return pack(x, gains(rng), ta, iv, d)
def setup_inputs_crowd(rng):
    x, ta, iv, d = parts(rng, [0.4, 0.3, 0.3]); z = rng.integers(24, 248, 16); junk = 16 + (z - 16 + 100) % 240
    hop = np.where(np.arange(16) % 2 == 0, W - 1, 1); o = rng.permutation(8)
    for q in range(N):
        for i in range(8):
            g = int(o[i]); v = int(rng.choice(np.array([0, W - 1, int(rng.integers(1, W - 1))]))); cs = rng.permutation(C)
            if i == 6: v = int(rng.integers(1, W // 2))
            n = (C, C, 16, 16, 16, 0, (64, 32, 96)[q % 3], 0)[i]; one = (0, 0, 1, 0, 0, 2, 1, 0)[i]; a = cs[:n]; s = cs[n:n + one]
            if i == 7:
                h = 19 + rng.permutation(45)[:7]; s = np.concatenate([np.arange(9, 19), h, 127 - h, rng.choice(np.array([0, C - 1]), 1)])
            x[q, g, :, (v - 1) % W] = junk; x[q, g, :, v] = z
            ta[q, g, a] = v; iv[q, g][:, a] = hop[:, None]; d[q, g][:, a] = 32 * z[:, None]
            ta[q, g, s] = (v - W // 32) % W; iv[q, g][:, s] = W // 32; d[q, g][:, s] = 32 * z[:, None]
            if i in (1, 4):
                iv[q, g, 15, a[-1]] = W // 2; x[q, g, :, (v - 1 + W // 2) % W] = z
    return pack(x, gains(rng), ta, iv, d)
def setup_inputs_long(rng):
    x, ta, iv, d = parts(rng, [0.4, 0.3, 0.3]); gain = gains(rng); z, z0 = rng.integers(24, 248, (2, 16)); g0 = int(rng.integers(0, 8)); base = int(rng.integers(0, W))
    wd = 16 * 2 ** VI; k = np.arange(16)
    for i in range(min(2, W // (wd * N)) * N):
        r = i % N; b = (base - wd * i) % W
        for g in range(8):
            if g != g0:
                c = int(rng.integers(0, CUT)) + CUT * ((i // N + r) % 2)
                ta[r, g, c] = b; iv[r, g, :, c] = W - 2; d[r, g, :, c] = 32 * z + rng.integers(-EPS, EPS + 1, 16)
        q = (r + VI - 1) % N
        for g in range(8):
            m = rng.integers(0, 3, 16); m[9] = 1; m[15] = 1
            x[q, g][:, ((b - 2 ** VI * (k + 1) + m) % W)[m < 2]] = z[:, None]
        for t in range(VI - 1):
            x[(r + t) % N][:, :, (b - 2 ** (t + 1) * (k[1::2] + 1)) % W] = z[:, None]
    nf = min(C, W // 16); sg = np.where(z0 < 136, 1, -1)
    for q in range(N):
        cs = rng.permutation(C)[:nf]; st = 2 * int(rng.integers(0, W // 2)) + 1; b = int(rng.integers(0, W))
        col = (b + st * (np.arange(16 * nf) + 1)) % W
        x[q, g0][:, col] = z0[:, None]; ta[q, g0, cs] = (b + 16 * st * np.arange(nf)) % W; iv[q, g0][:, cs] = st
        e = rng.integers(-EPS, EPS + 1, (16, nf)); far = np.argsort(rng.random((16, 8)), axis=0); near = EPS * rng.choice(np.array([-1, 1]), (16, 8))
        e[:, :8] = np.where(far < 2, 512 * sg[:, None], np.where(far < 16 - HE, 2080 * sg[:, None], near))
        d[q, g0][:, cs] = 32 * z0[:, None] + e
        gain[q, g0][:, col[:128]] = 4 * (VI - 2) * (0.75 + 0.5 * rng.random((16, 128)))
    return pack(x, gain * 0.25, ta, iv, d)
def check_ranges(d):
    bad = []
    for name, lo, hi in (("xs", 16, 255), ("gn", 0.125, 4), ("tau", 0, W - 1), ("iv", 1, W - 1), ("pf", 512, 8160)):
        a = np.asarray(d[name]).astype(np.float64)
        if not np.all(np.isfinite(a)) or np.min(a) < lo or np.max(a) > hi: bad.append("range of " + name)
        elif name != "gn" and np.any(a != np.floor(a)): bad.append(name + " is not whole")
    return bad
def go(a, t):
    return np.concatenate([a[..., :CUT], np.roll(a[..., CUT:], t, axis=0)], axis=-1)
def reference(xs, gn, tau, iv, pf):
    X = xs.astype(np.float32).astype(np.int32).reshape(N, 8, 16, W) * np.int32(32); GA = gn.astype(np.float64).reshape(N, 8, 16, W)
    I = iv.astype(np.int32).reshape(N, 8, 16, C); D = pf.astype(np.int32).reshape(N, 8, 16, C); ta = tau.astype(np.int32)
    y = np.zeros((N, 8, 16, C)); eight = np.arange(8)[:, None]; rows = np.arange(16)[None, :, None]
    for t in range(VI):
        for r in range(N):
            q = (r + t) % N
            T = go((ta[r][:, None, :] + np.add.accumulate(I[r], axis=1)) & (W - 1), t).transpose(0, 2, 1).reshape(8, 16 * C); T1 = (T + 1) & (W - 1)
            Ds = go(D[r], t); Dx = np.repeat(Ds, 16, axis=2)
            e0 = np.take_along_axis(X[q], T[:, None, :], 2) - Dx; e1 = np.take_along_axis(X[q], T1[:, None, :], 2) - Dx
            on = np.sum((np.abs(e0) <= EPS).astype(np.int32), axis=1) >= HE
            late = ~on & (np.sum((np.abs(e1) <= EPS).astype(np.int32), axis=1) >= HE); heard = on | late
            P = np.where(late, T1, T); E = np.where(late[:, None, :], e1, e0)
            cnt = np.zeros((8, W), np.int32); np.add.at(cnt, (eight, P), heard.astype(np.int32))
            taken = heard & (np.take_along_axis(cnt, P, 1) == 1)
            z = np.where(taken[:, None, :], np.take_along_axis(GA[q], P[:, None, :], 2) * np.exp(-0.00390625 * np.abs(E)), 0.0)
            y[r] += go(np.add.reduce(z.reshape(8, 16, C, 16), axis=3), -t)
            if t == VI - 1: continue
            S = np.add.reduce(np.where(taken[:, None, :], E, 0).reshape(8, 16, C, 16), axis=3)
            D[r] = go(Ds + (S >> 4), -t)
            X[q] = np.where((cnt == 1)[:, None, :], 0, X[q])
            a = go(taken.reshape(8, C, 16).transpose(0, 2, 1), -t); l = go((taken & late).reshape(8, C, 16).transpose(0, 2, 1), -t)
            J = I[r] + l; leave = np.zeros((8, 16, C), bool); leave[:, :15] = ~a[:, :15] & a[:, 1:]
            J[:, 1:] = J[:, 1:] + np.where(leave[:, :15], J[:, :15], 0)
            o = np.argsort(leave.astype(np.int32), axis=1, kind="stable"); n = 16 - np.sum(leave.astype(np.int32), axis=1)[:, None, :]
            src = np.take_along_axis(o, np.where(rows < n, rows, rows - n), 1)
            I[r] = np.take_along_axis(J, src, 1)
    return {"y": y.reshape(N, 128, C).astype(np.float32)}

def check_inputs(d):
    bad = list(check_ranges(d))
    if not bad:
        for name, y in reference(**d).items():
            for q in range(N):
                v = np.abs(np.asarray(y[q], np.float64)); s = np.sqrt(np.mean(v * v))
                if v.max() > 10 * s or s < 2.0 ** -1: bad.append('%s of rank %d is uneven or too small' % (name, q))
    return bad

@@ -1,0 +1,631 @@
+import numpy as np
+from concourse.bass import DstId, RemoteDMATransfer
+from concourse.mybir import dt, AluOpType, AxisListType, ActivationFunctionType
+
+BF, F32, I32, U16, F16 = "bfloat16", "float32", "int32", "uint16", "float16"
+W, C, VI = 2048, 128, 4
+V = 131072.0
+BIG = 201326592.0
+
+
+def _sb(cols, dtype, rows=128):
+    return ("sbuf", [rows, cols], dtype)
+
+
+SCRATCH = {
+    "x0": _sb(2064, BF), "x1": _sb(W, BF), "x2": _sb(W, BF), "x3": _sb(W, BF),
+    "g0": _sb(2064, BF), "g1": _sb(2064, BF), "g2": _sb(2064, BF), "g3": _sb(2064, BF),
+    "xm": _sb(2064, BF), "xt": _sb(2064, BF), "ga0": _sb(W, BF), "ga1": _sb(W, BF), "ms0": _sb(W, BF), "ms1": _sb(W, BF),
+    "xg": _sb(W, BF), "ab": _sb(W, F32), "zz": _sb(W, F32), "zs": _sb(1024, F32), "oha": _sb(8192, BF), "ohb": _sb(4224, BF),
+    "qa": _sb(512, BF), "qb": _sb(512, BF), "fc": _sb(1152, F16),
+    "ivi": _sb(C, I32), "pfi": _sb(C, I32), "ivf": _sb(C, F32), "pff": _sb(C, F32),
+    "taui": _sb(512, I32, 8), "tauf": _sb(512, F32, 8),
+    "ti": _sb(C, I32), "t0i": _sb(C, I32), "t0f": _sb(C, F32), "off0": _sb(C, U16), "off1": _sb(C, U16),
+    "tt2": _sb(256, F32), "kk": _sb(256, F32), "ki": _sb(C, I32), "kf": _sb(C, F32), "hii": _sb(C, I32), "loi": _sb(C, I32),
+    "k2": _sb(C, I32), "k3": _sb(C, I32), "po0": _sb(C, U16), "po1": _sb(C, U16), "thr": _sb(C, F32),
+    "hp": _sb(264, F32), "ub": _sb(264, BF), "mt": _sb(C, BF), "nu": _sb(C, BF),
+    "so": _sb(3 * C, BF), "si": _sb(3 * C, BF),
+    "ak": _sb(C, BF), "lt": _sb(C, BF), "lv": _sb(C, BF), "jj": _sb(C, F16), "im": _sb(C, I32),
+    "ri": _sb(C, I32), "rx": _sb(C, I32), "rq": _sb(C, I32), "ru": _sb(C, F32), "vv": _sb(C, F32), "fa": _sb(C, I32),
+    "fb": _sb(C, I32), "dn": _sb(C, I32), "dw": _sb(C, F32), "nd": _sb(C, F32),
+    "sa0": _sb(C, BF), "sa1": _sb(C, BF), "ra0": _sb(C, BF), "ra1": _sb(C, BF), "yo": _sb(C, F32),
+    "ia": _sb(192, I32), "iam": _sb(192, I32), "idf": _sb(192, F32), "id1": _sb(C, BF), "id125": _sb(C, BF), "id2": _sb(C, BF),
+    "pvi": _sb(1, I32), "pw": _sb(4, I32), "pc": _sb(8, F32), "jr": _sb(160, I32), "jm": _sb(160, I32), "jb": _sb(160, I32),
+    "jk": _sb(160, I32), "jmf": _sb(160, F32), "jbf": _sb(160, F32), "gxb": _sb(160, BF),
+    "blk": _sb(144, F32), "tri": _sb(144, F32), "c1": _sb(144, F32), "c3": _sb(C, F32), "c4": _sb(C, F32),
+    "c5": _sb(C, F32), "c6": _sb(C, F32), "c7": _sb(C, F32), "tri16": _sb(144, F16), "ntri": _sb(144, F16),
+    "tx": _sb(C, F16), "tz": _sb(C, F16), "sh": _sb(C, BF), "dm": _sb(C, F32), "bo8": _sb(8, BF),
+    "j16": _sb(512, BF), "rep": _sb(W, BF), "rep8": _sb(C, F32, 8), "rep80": _sb(C, F32, 8),
+    "ones": _sb(640, BF), "on16": _sb(C, F16), "rl": _sb(512, BF), "selx": _sb(W, BF), "km": _sb(512, F32),
+    "rt": _sb(1152, F16), "qt": _sb(1152, F16), "ll": _sb(1152, BF), "ft": _sb(1296, F16),
+    "b1": _sb(C, F32, 8), "b2": _sb(C, F32, 8), "bs": _sb(4, F32, 8), "bp": _sb(2 * C, BF, 8), "ind": _sb(640, BF, 8),
+    "B0": ("psum", [128, 512], F32), "B1": ("psum", [128, 512], F32), "B2": ("psum", [128, 512], F32),
+    "B3": ("psum", [128, 512], F32), "S0": ("psum", [128, 512], F32), "S1": ("psum", [128, 512], F32),
+    "S2": ("psum", [128, 512], F32), "SY": ("psum", [128, 512], F32),
+}
+SEMAPHORES = (["pe", "dve", "act", "pool"] + ["ld%d" % i for i in range(16)] + ["ax1", "ax2", "ax3", "ag1", "ag2", "ag3",
+              "as1", "as2", "as3"] + ["lo%d" % i for i in range(9)])
+BANKS = ("B0", "B1", "B2", "B3", "S0", "S1", "S2", "SY")
+M = {"cy": 1.0, "pe": 0.5, "hop": 70.0, "gc": 1.56, "vo": 30.0, "ao": 65.0, "po": 15.0, "sil": 3500.0, "bulk": 11000.0,
+     "rounds": 2, "tries": 1200, "seed": 1}
+CFG = {"hear": "adaadaaa", "xt": "dada", "xg": "adad", "xgl": "adad", "small": "mt hp nu"}
+
+
+def segments():
+    out = []
+    for t in range(4):
+        s = t + 1
+        out.append((t, 0, 17 - 2 * s, 2 * s - 1, s - 1, 1))
+        out.append((t, 17 - 2 * s, 2 * s - 1, 17 - 2 * s, 8 - s, 1))
+    for w in range(5):
+        out.append((4 + w, 0, 16 - 2 * w, 0, 15 - w, 0))
+        if 0 < w < 4:
+            out.append((4 + w, 16 - 2 * w, 2 * w, 0, 7 + w, 0))
+    return out
+
+
+def build(g, core, T, topo, rank):
+    A, AF = AluOpType, ActivationFunctionType
+    n = len(T.cores)
+    ops = []
+    CY = M["cy"]
+
+    def op(eng, calls, r, w, dur, sem=None, inc=0, lat=0.0, ext=()):
+        ops.append({"eng": eng, "calls": calls, "r": list(r), "w": list(w), "dur": dur, "sem": sem, "inc": inc, "lat": lat,
+                    "ext": [e for e in ext if e is not None]})
+
+    def vd(n_, c):
+        return max(64.0, n_ * c) * CY + M["vo"]
+
+    def ts(out, in0, s1, s2, o0, o1, r, w, n_, c=1.0):
+        if o1 is None:
+            op("dve", [lambda: g.vector.tensor_scalar(out, in0, s1, None, o0)], r, w, vd(n_, c))
+        else:
+            op("dve", [lambda: g.vector.tensor_scalar(out, in0, s1, s2, o0, o1)], r, w, vd(n_, c))
+
+    def tt(out, a, b, o, r, w, n_, c=2.0, ext=()):
+        op("dve", [lambda: g.vector.tensor_tensor(out, a, b, o)], r, w, vd(n_, c), ext=ext)
+
+    def cp(out, a, r, w, n_, c=1.0):
+        op("dve", [lambda: g.vector.tensor_copy(out, a)], r, w, vd(n_, c))
+
+    def ms(out, val, w, n_):
+        op("dve", [lambda: g.vector.memset(out, val)], [], w, vd(n_, 0.5))
+
+    def act(out, a, f, r, w, n_, c=1.0, bias=0.0, scale=1.0, extra=0.0):
+        op("act", [lambda: g.scalar.activation(out, a, f, bias=bias, scale=scale)], r, w, n_ * c * CY + M["ao"] + extra)
+
+    def axpb(name, out, a, scale, bias, r, w, n_):
+        if name in CFG["small"]:
+            act(out, a, AF.Identity, r, w, n_, bias=bias, scale=scale)
+        else:
+            ts(out, a, scale, bias, A.mult, A.add, r, w, n_)
+
+    def one_mm(m):
+        return lambda: g.tensor.matmul(m[0], m[1], m[2], m[3], m[4])
+
+    def mm(lst, r, w, cyc, ext=()):
+        op("pe", [one_mm(m) for m in lst], r, w, cyc * M["pe"] + M["po"] * len(lst), ext=ext)
+
+    def iota(out, pat, base, cm, w, n_, flag=False):
+        if flag:
+            op("pool", [lambda: g.iota(out, pat, base, cm, allow_small_or_imprecise_dtypes=True)], [], w, 130 + 2 * n_ * CY)
+        else:
+            op("pool", [lambda: g.iota(out, pat, base, cm)], [], w, 130 + 2 * n_ * CY)
+
+    def sel(out, src, skey, pat, base, w, n_):
+        op("pool", [lambda: g.affine_select(out, src[:, 0:n_], pat, A.is_equal, 0.0, base, 1)], [skey], w, 170 + 2 * n_ * CY)
+
+    nld = [0]
+
+    def dma(q, out, a, r, w, lat):
+        s = "ld%d" % nld[0]
+        nld[0] += 1
+        eng = g.sync if q == "sp" else g.scalar
+        op(q, [lambda: eng.dma_start(out, a)], r, w, 100.0, sem=s, inc=16, lat=lat)
+
+    nlo = [0]
+
+    def emask(lst):
+        m = 0
+        for e in lst:
+            m |= 1 << e
+        return m
+
+    def engines(src, dst, kind):
+        e = topo.engines(src, dst)
+        return {"all": e, "bulk": e[:4], "sil": e[4:8]}[kind]
+
+    def send(dst_rank, out, a, sem, kind, r, w, lat):
+        d = T.cores[dst_rank % n]
+        e = engines(core, d, kind)
+        rid, pid = topo.addr(d, core)
+        s = "lo%d" % nlo[0]
+        nlo[0] += 1
+        op("pool", [lambda: g.remote_dma(out, a, T.sem[sem], T.sem[s], pid, rid, emask(e))], r, w, 1000.0, sem=s, inc=len(e), lat=lat)
+
+    def arrival(src_rank, sem, kind):
+        return (sem, len(engines(T.cores[src_rank % n], core, kind)))
+
+    X = [T.x0, T.x1, T.x2, T.x3]
+    G = [T.g0, T.g1, T.g2, T.g3]
+    B = [T.B0, T.B1, T.B2, T.B3]
+    ident = T.idf[:, 16:144]
+
+    dma("act", T.x0[:, 0:W], T.xs[:], [], ["x0"], 3300)
+    dma("sp", T.ivi[:], T.iv[:], [], ["ivi"], 2200)
+    dma("sp", T.taui[:, 0:C], T.tau[:], [], ["taui0"], 2000)
+    dma("sp", T.pfi[:], T.pf[:], [], ["pfi"], 2200)
+    dma("sp", T.g0[:, 0:W], T.gn[:], [], ["g0"], 3500)
+    for t in range(1, VI):
+        dma("sp", T.taui[:, t * C:t * C + 64], T.tau[:, 0:64], [], ["taui%da" % t], 2000)
+        dma("sp", T.taui[t:8, t * C + 64:t * C + C], T.tau[0:8 - t, 64:C], [], ["taui%db" % t], 2000)
+        dma("sp", T.taui[0:t, t * C + 64:t * C + C], T.tau[8 - t:8, 64:C], [], ["taui%dc" % t], 2000)
+
+    send(rank - 1, T.x1[:], T.x0[:, 0:W], "ax1", "all", ["x0"], ["x1", "bulk"], 0.8 * M["bulk"])
+    for j, (d, name) in enumerate(((2, "x"), (1, "g"), (3, "x"), (2, "g"), (3, "g"))):
+        send(rank - d, T["%s%d" % (name, d)][:, 0:W], T[name + "0"][:, 0:W], "a%s%d" % (name, d), "bulk", [name + "0"],
+             ["%s%d" % (name, d), "bulk"], (j + 1.8) * M["bulk"])
+    AX = [None] + [arrival(rank + t, "ax%d" % t, "all" if t == 1 else "bulk") for t in range(1, VI)]
+    AG = [None] + [arrival(rank + t, "ag%d" % t, "bulk") for t in range(1, VI)]
+    AS = [None] + [arrival(rank + 1, "as%d" % t, "sil") for t in range(1, VI)]
+    SO = [T.so[:, C * t:C * t + C] for t in range(3)]
+    SI = [None] + [T.si[:, C * t:C * t + C] for t in range(3)]
+
+    iota(T.ia[:], [[1, 192]], 112, -1, ["ia"], 192)
+    iota(T.pvi[:], [[1, 1]], 0, 1, ["pvi"], 1)
+    iota(T.jr[:], [[1, 160]], 96, 0, ["jr"], 160)
+    iota(T.j16[:], [[1, 32], [0, 16]], 0, -1, ["j16"], 512, True)
+    ms(T.ones[:], 1.0, ["ones"], 640)
+    ts(T.iam[:], T.ia[:], 127, None, A.bitwise_and, None, ["ia"], ["iam"], 192)
+    ts(T.idf[:], T.iam[:], 0.0, None, A.is_equal, None, ["iam"], ["idf"], 192)
+    for name, s in (("id125", 1.25), ("id1", 1.0), ("id2", 2.0)):
+        act(T[name][:], ident, AF.Identity, ["idf"], [name], C, scale=s)
+    ts(T.pw[:, 0:1], T.pvi[:], 112, None, A.bitwise_and, None, ["pvi"], ["pw0"], 1)
+    ts(T.pw[:, 1:2], T.pvi[:], 15, None, A.bitwise_and, None, ["pvi"], ["pw1"], 1)
+    pp, p16, pg, pl, pk = (T.pc[:, i:i + 1] for i in range(5))
+    cp(pp, T.pvi[:], ["pvi"], ["pp"], 1)
+    ts(p16, T.pvi[:], 16.0, None, A.mult, None, ["pvi"], ["p16"], 1)
+    cp(pg, T.pw[:, 0:1], ["pw0"], ["pg"], 1)
+    ts(pl, T.pw[:, 1:2], 14.5, -0.5, A.is_lt, A.add, ["pw1"], ["pl"], 1)
+    ts(pk, T.pw[:, 1:2], 2048.0, None, A.mult, None, ["pw1"], ["pk"], 1)
+    ts(T.jm[:], T.jr[:], 127, None, A.bitwise_and, None, ["jr"], ["jm"], 160)
+    ts(T.jb[:], T.jr[:], 112, None, A.bitwise_and, None, ["jr"], ["jb"], 160)
+    ts(T.jk[:], T.jr[:], 15, None, A.bitwise_and, None, ["jr"], ["jk"], 160)
+    cp(T.jmf[:], T.jm[:], ["jm"], ["jmf"], 160)
+    cp(T.jbf[:], T.jb[:], ["jb"], ["jbf"], 160)
+    ts(T.blk[:], T.jbf[:, 16:160], pg, None, A.is_equal, None, ["jbf", "pg"], ["blk"], 144)
+    ts(T.c1[:], T.jmf[:, 16:160], pp, None, A.is_ge, None, ["jmf", "pp"], ["c1"], 144)
+    tt(T.tri[:], T.c1[:], T.blk[:], A.mult, ["c1", "blk"], ["tri"], 144)
+    ts(T.rep8[:], T.jbf[0:8, 32:160], T.pc[0:8, 1:2], None, A.is_equal, None, ["jbf", "p16"], ["rep8"], C)
+    ts(T.rep80[:], T.jmf[0:8, 32:160], T.pc[0:8, 1:2], -1.0, A.is_equal, A.mult, ["jmf", "p16"], ["rep80"], C)
+    ts(T.bo8[:], T.jmf[:, 32:160:16], pg, 8192.0, A.is_equal, A.mult, ["jmf", "pg"], ["bo8"], 8)
+    for b in range(4):
+        s = slice(512 * b, 512 * b + 512)
+        ts(T.rep[:, s], T.j16[:], -32.0 * b, -0.625, A.is_equal, A.mult, ["j16"], ["rep%d" % b], 512, 0.5)
+        sel(T.selx[:, s], T.ones, "ones", [[-1, 4], [-16, 8], [0, 16]], -4 * b, ["selx%d" % b], 512)
+    ts(T.gxb[:], T.jmf[:], pg, None, A.is_equal, None, ["jmf", "pg"], ["gxb"], 160)
+    cp(T.tri16[:], T.tri[:], ["tri"], ["tri16"], 144)
+    ts(T.ntri[:], T.tri[:], -1.0, None, A.mult, None, ["tri"], ["ntri"], 144)
+    tt(T.c3[:], T.blk[:, 16:144], T.tri[:, 16:144], A.subtract, ["tri", "blk"], ["c3"], C)
+    ts(T.tx[:], T.c3[:], 2048.0, None, A.mult, None, ["c3"], ["tx"], C)
+    tt(T.c4[:], T.c3[:], T.blk[:, 16:144], A.add, ["c3", "blk"], ["c4"], C)
+    ts(T.tz[:], T.c4[:], -2048.0, None, A.mult, None, ["c4"], ["tz"], C)
+    ts(T.tz[:, 15:C:16], T.blk[:, 31:144:16], pk, None, A.mult, None, ["blk", "pk"], ["tz"], 8)
+    tt(T.c5[:], T.idf[:, 17:145], ident, A.subtract, ["idf"], ["c5"], C)
+    ts(T.c6[:], T.jk[:, 32:160], 14.5, None, A.is_lt, None, ["jk"], ["c6"], C)
+    tt(T.sh[:], T.c5[:], T.c6[:], A.mult, ["c5", "c6"], ["sh"], C)
+    ts(T.c4[:], T.jk[:, 32:160], 0.5, None, A.is_gt, None, ["jk"], ["c4"], C)
+    tt(T.c7[:], T.idf[:, 15:143], T.c4[:], A.mult, ["idf", "c4"], ["c7"], C)
+    tt(T.dm[:], ident, T.c7[:], A.subtract, ["idf", "c7"], ["dm"], C)
+    cp(T.on16[:], T.ones[:, 0:C], ["ones"], ["on16"], C, 0.5)
+    for h in range(2):
+        ms(T.ohb[:, 2112 * h + 2048:2112 * h + 2112], -1.0, ["ohbc%d" % h], 64)
+    ms(T.xt[:, W:2064], -V, ["xtc"], 16)
+    for t in range(VI):
+        ms(G[t][:, W:2064], 0.0, ["gc%d" % t], 16)
+    ms(T.km[:], 1.0, ["km"], 1024)
+    ms(T.km[:, 0:512:16], 0.0, ["km"], 64)
+    for u in range(2):
+        for p in range(2):
+            c0 = 256 * u + C * p
+            sel(T.rl[:, c0:c0 + C], T.ones, "ones", [[-2, 4], [-1000, 2], [-8, 16]], 1000 * p - u, ["rl%d%d" % (u, p)], C)
+    for name in ("rt", "qt"):
+        ts(T[name][:, 1088:1152], T.ones[:, 0:64], 0.0, None, A.mult, None, ["ones"], [name + "z"], 64)
+    tk = {}
+    for j, (tile, q0, nq, k0, d0, dstep) in enumerate(segments()):
+        c0 = C * tile + 8 * q0
+        sel(T.rt[:, c0:c0 + 8 * nq], T.on16, "on16", [[-16, 8], [-1, nq]], -k0, ["rt%d" % j], 8 * nq)
+        sel(T.qt[:, c0:c0 + 8 * nq], T.on16, "on16", [[-16, 8], [-dstep, nq]], -d0, ["qt%d" % j], 8 * nq)
+        tk.setdefault(tile, []).append(j)
+    PARTS = ((0, 4), (4, 8), (8, 9))
+    for j, (t0, t1) in enumerate(PARTS):
+        keys = ["rt%d" % x for t in range(t0, t1) for x in tk[t]] + ["rtz"]
+        nn = C * (t1 - t0)
+        mm([(B[j][:, 0:nn], (T.tx if j == 0 else T.tz)[:], T.rt[:, C * t0:C * t1], True, True)], keys + ["tx", "tz"], ["B%d" % j], nn)
+        act(T.ll[:, C * t0:C * t1], B[j][:, 0:nn], AF.Copy, ["B%d" % j], ["ll%d" % j], nn)
+    for j in range(3):
+        lst = []
+        for t in range(3 * j, 3 * j + 3):
+            o = B[j][:, 144 * (t % 3):144 * (t % 3) + 144]
+            lst.append((o, T.qt[:, C * t:C * t + C], T.tri16[:], True, t >= 4))
+            if t < 4:
+                lst.append((o, T.rt[:, C * t:C * t + C], T.ntri[:], False, True))
+        mm(lst, [a + "%d" % x for t in range(3 * j, 3 * j + 3) for x in tk[t] for a in ("rt", "qt")] + ["qtz", "tri16", "ntri"],
+           ["B%d" % j], 144 * len(lst))
+        cp(T.ft[:, 432 * j:432 * j + 432], B[j][:, 0:432], ["B%d" % j], ["ft%d" % j], 432)
+    iota(T.b1[:], [[1, C]], 0, 16, ["b1"], C, True)
+    for j, (base, cm) in enumerate(((-14336, 4096), (-2048, -2048), (16384, -4096), (2048, 2048))):
+        iota(T.bs[:, j:j + 1], [[1, 1]], base, cm, ["bs%d" % j], 1, True)
+    op("pool", [lambda: g.affine_select(T.ind[:], T.ones[0:8, :], [[-1, 5], [0, C]], A.is_equal, 0.0, 0, 1)], ["ones"], ["ind"],
+       170 + 1280 * CY)
+    for name, lim, j in (("bp", 119.5, 0), ("bw", 127.5, 2)):
+        ts(T.b2[:], T.b1[:], lim, T.bs[:, j:j + 1], A.is_gt, A.mult, ["b1", "bs%d" % j], ["b2"], C)
+        ts(T.bp[:, 64 * j:64 * j + C], T.b2[:], T.bs[:, j + 1:j + 2], None, A.add, None, ["b2", "bs%d" % (j + 1)], [name], C)
+    first_const_end = len(ops)
+
+    def profile(t):
+        sa, ra = "sa%d" % (t % 2), "ra%d" % (t % 2)
+        ts(T.fa[:], T.vv[:], -4112.0 + 1.0 / 32, 1.0 / 32, A.add, A.mult, ["vv"], ["fa"], C)
+        ts(T.fb[:], T.vv[:], -4081.0 + 1.0 / 32, 1.0 / 32, A.add, A.mult, ["vv"], ["fb"], C)
+        tt(T[sa][:], T.fa[:], T.fb[:], A.add, ["fa", "fb"], [sa], C)
+        ts(T.dn[:], T.vv[:], -15.0 / 32, None, A.add, None, ["vv"], ["dn"], C)
+        ts(T.dw[:], T.dn[:], -4096.0, 1.0 / 16, A.add, A.mult, ["dn"], ["dw"], C)
+        tt(T[ra][:], T.dw[:], T[sa][:], A.subtract, ["dw", sa], [ra], C)
+        if t < VI - 1:
+            act(T.nd[:], T.dw[:], AF.Identity, ["dw"], ["nd"], C, bias=-256.0, scale=-1.0)
+
+    def times(t):
+        cp(T.ti[:], T.S2[:, 0:C], ["S2"], ["ti"], C)
+        ts(T.t0i[:], T.ti[:], W - 1, None, A.bitwise_and, None, ["ti"], ["t0i"], C)
+        cp(T.off0[:], T.t0i[:], ["t0i"], ["off0"], C)
+        ts(T.off1[:], T.t0i[:], 1.0, None, A.add, None, ["t0i"], ["off1"], C)
+        cp(T.t0f[:], T.t0i[:], ["t0i"], ["t0f"], C)
+        mm([(T.S1[:, 0:C], T.t0f[:], ident, True, True)], ["t0f", "idf"], ["S1"], 512)
+        act(T.tt2[:, 0:C], T.S1[:, 0:C], AF.Identity, ["S1"], ["tt2a"], C, bias=32768.0)
+        act(T.tt2[:, C:2 * C], T.S1[:, 0:C], AF.Identity, ["S1"], ["tt2b"], C, bias=32768.0 + 4097.0)
+        if 0 < t < VI - 1:
+            mm([(T.S2[:, 0:C], T.dm[:], T.t0f[:], True, False),
+                (T.S2[:, 0:C], T.rep80[:], T.tauf[:, t * C:t * C + C], False, True)], ["t0f", "dm", "rep80", "taufr"], ["S2"], 1024)
+            cp(T.ti[:], T.S2[:, 0:C], ["S2"], ["ti"], C)
+            ts(T.im[:], T.ti[:], W - 1, None, A.bitwise_and, None, ["ti"], ["im"], C)
+
+    def table_x(t, b):
+        mm([(B[b][:], T.id1[:], X[t][:, 512 * b:512 * b + 512], True, False)], ["x%d" % t, "id1"], ["B%d" % b], 512, [AX[t]])
+
+    def table_mask(msk, mkey, b, with_x, ext=()):
+        mm([(B[b][:, C * j:C * j + C], T.selx[:, C * (4 * b + j):C * (4 * b + j) + C], msk, not with_x, (not with_x) or j == 3)
+            for j in range(4)], [mkey, "selx%d" % b], ["B%d" % b], 512, ext)
+
+    def gather(eng, out, win, off, r, w):
+        if eng == "a":
+            act(out, win.indirect(off), AF.Copy, r, w, 512, M["gc"])
+        else:
+            cp(out, win.indirect(off), r, w, 512, M["gc"])
+
+    def zwork(t, last):
+        sa, ra, po = "sa%d" % (t % 2), "ra%d" % (t % 2), "po%d" % (t % 2)
+        for b in range(4):
+            s = slice(512 * b, 512 * b + 512)
+            mm([(B[b][:], T[sa][:], T.rep[:, s], True, False), (B[b][:], T[ra][:], T.rep[:, s], False, False)],
+               [sa, ra, "rep%d" % b], ["B%d" % b], 1024)
+            mm([(B[b][:], T.id125[:], T.xg[:, s], False, True)], ["xg%d" % b, "id125"], ["B%d" % b], 512)
+        for b in range(4):
+            s = slice(512 * b, 512 * b + 512)
+            act(T.ab[:, s], B[b][:], AF.Abs, ["B%d" % b], ["ab%d" % b], 512, bias=-160.0)
+            act(T.ab[:, s], T.ab[:, s], AF.Exp, ["ab%d" % b], ["ab%d" % b], 512, scale=-0.1, extra=1300.0 if t + b == 0 else 0.0)
+            tt(T.zz[:, s], G[t][:, 0:2064].indirect(T[po][:, 32 * b:32 * b + 32]), T.ab[:, s], A.mult,
+               ["ab%d" % b, po, "gc%d" % t, "g%d" % t], ["zz%d" % b], 512, M["gc"], ext=[AG[t]])
+        if t == 0:
+            for q in range(8):
+                mm([(T.SY[:, 0:C], ident, T.zz[:, k:W:16], k == 0, False) for k in (2 * q, 2 * q + 1)],
+                   ["zz0", "zz1", "zz2", "zz3", "idf"], ["SY"], 1024)
+            return
+        for h in range(2):
+            w0 = 16 + 16 * t * h
+            if last and h == 1:
+                for b in (2, 3):
+                    zs = T.zs[:, 512 * (b - 2):512 * (b - 1)]
+                    op("dve", [scan(zs, T.zz[:, 512 * b:512 * b + 512])], ["km", "zz%d" % b], ["zs%d" % b], vd(512, 1.0))
+                    mm([(T.SY[:, 32 * b:32 * b + 32], T.idf[:, w0:w0 + C], T.zs[:, 512 * (b - 2) + 15:512 * (b - 1):16], False, b == 3)],
+                       ["zs%d" % b, "idf"], ["SY"], 256)
+                continue
+            for q in range(4):
+                mm([(T.SY[:, 64 * h:64 * h + 64], T.idf[:, w0:w0 + C], T.zz[:, 1024 * h + k:1024 * h + 1024:16], False, False)
+                    for k in range(4 * q, 4 * q + 4)], ["zz%d" % (2 * h), "zz%d" % (2 * h + 1), "idf"], ["SY"], 1024)
+
+    def scan(out, data):
+        return lambda: g.vector.tensor_tensor_scan(out, T.km[:], data, 0.0, A.mult, A.add)
+
+    cp(T.ivf[:], T.ivi[:], ["ivi"], ["ivf"], C)
+    cp(T.tauf[:, 0:C], T.taui[:, 0:C], ["taui0"], ["tauf0"], C)
+    mm([(T.S2[:, 0:C], T.tri[:, 16:144], T.ivf[:], True, False), (T.S2[:, 0:C], T.rep8[:], T.tauf[:, 0:C], False, True)],
+       ["tri", "ivf", "rep8", "tauf0"], ["S2"], 1024)
+    cp(T.pff[:], T.pfi[:], ["pfi"], ["pff"], C)
+    mm([(T.S0[:, 0:C], T.pff[:], ident, True, True)], ["pff", "idf"], ["S0"], 512)
+    act(T.vv[:], T.S0[:, 0:C], AF.Copy, ["S0"], ["vv0", "vv1", "vv"], C)
+    profile(0)
+    act(T.x0[:, W:W + 1], T.x0[:, 0:1], AF.Copy, ["x0"], ["x0c"], 1)
+    cp(T.tauf[:, C:4 * C], T.taui[:, C:4 * C], ["taui%d%s" % (t, s) for t in (1, 2, 3) for s in "abc"], ["taufr"], 3 * C)
+    times(0)
+    const_ops = ops[:first_const_end]
+
+    GA, MS, OFF = [T.ga0, T.ga1], [T.ms0, T.ms1], [T.off0, T.off1]
+    for t in range(VI):
+        last = t == VI - 1
+        sa, po = "sa%d" % (t % 2), "po%d" % (t % 2)
+        xw = T.x0 if t == 0 else T.xm
+        xkeys = ["x0", "x0c"] if t == 0 else ["xm0", "xm1", "xm2", "xm3", "xmc"]
+        for e in range(2):
+            for b in range(4):
+                s = slice(512 * b, 512 * b + 512)
+                gather(CFG["hear"][4 * e + b], GA[e][:, s], xw[:, 0:W + 1], OFF[e][:, 32 * b:32 * b + 32], xkeys + ["off%d" % e],
+                       ["ga%d%d" % (e, b)])
+                mm([(B[b][:], T[sa][:], T.rep[:, s], True, False)], [sa, "rep%d" % b], ["B%d" % b], 512)
+                mm([(B[b][:], T.id125[:], GA[e][:, s], False, True)], ["ga%d%d" % (e, b), "id125"], ["B%d" % b], 512)
+                ts(MS[e][:, s], B[b][:], BIG - 160.0, BIG, A.add, A.not_equal, ["B%d" % b], ["ms%d%d" % (e, b)], 512)
+            for q in range(2):
+                mm([(T.S0[:, C * e + k:C * e + C:16], MS[e][:, k:W:16], T.bo8[:], True, True) for k in range(8 * q, 8 * q + 8)],
+                   ["ms%d%d" % (e, b) for b in range(4)] + ["bo8"], ["S0"], 512)
+        tt(T.kk[:], T.S0[:, 0:256], T.tt2[:], A.max, ["S0", "tt2a", "tt2b"], ["kk"], 256, 1.0)
+        tt(T.ki[:], T.kk[:, 0:C], T.kk[:, C:2 * C], A.min, ["kk"], ["ki"], C)
+        ts(T.loi[:], T.ki[:], 31, None, A.bitwise_and, None, ["ki"], ["loi"], C)
+        ts(T.hii[:], T.ki[:], 5, 0xFFF3F, A.arith_shift_right, A.bitwise_and, ["ki"], ["hii"], C)
+        for h in range(2):
+            cp(T.qb[:, 256 * h:256 * h + 64], T.loi[:, 64 * h:64 * h + 64], ["loi"], ["qb%d0" % h], 64)
+        for h in range(2):
+            for s in range(4):
+                c0 = 256 * h + 64 * s
+                ts(T.qa[:, c0:c0 + 64], T.hii[:, 64 * h:64 * h + 64], -1024.0 - s, None, A.add, None, ["hii"], ["qa%d%d" % (h, s)], 64)
+                if s:
+                    act(T.qb[:, c0:c0 + 64], T.qb[:, 256 * h:256 * h + 64], AF.Identity, ["qb%d0" % h], ["qb%d%d" % (h, s)], 64, bias=-1.0 * s)
+            for a in range(16):
+                c0 = 4096 * h + 256 * a
+                ts(T.oha[:, c0:c0 + 256], T.qa[:, 256 * h:256 * h + 256], 4.0 * a, None, A.is_equal, None,
+                   ["qa%d%d" % (h, s) for s in range(4)], ["oha%d_%d" % (h, a)], 256, 0.5)
+            for b in range(8):
+                c0 = 2112 * h + 256 * b
+                act(T.ohb[:, c0:c0 + 256], T.qb[:, 256 * h:256 * h + 256], AF.Sign, ["qb%d%d" % (h, s) for s in range(4)],
+                    ["ohb%d_%d" % (h, b)], 256, bias=0.5 - 4.0 * b)
+        if t > 0:
+            zwork(t - 1, False)
+        cp(T.kf[:], T.ki[:], ["ki"], ["kf"], C)
+        mm([(T.S0[:, 0:C], T.kf[:], ident, True, True)], ["kf", "idf"], ["S0"], 512)
+        cp(T.k2[:], T.S0[:, 0:C], ["S0"], ["k2"], C)
+        if not last:
+            ts(T.thr[:], T.k2[:], 36864.0, 1.0e6, A.is_lt, A.mult, ["k2"], ["thr"], C)
+        ts(T.k3[:], T.k2[:], 0x367FF, None, A.bitwise_and, None, ["k2"], ["k3"], C)
+        ts(T[po][:], T.k3[:], 2048.0, None, A.min, None, ["k3"], [po], C)
+        for h in range(2):
+            H, hk = (T.S1, "S1") if h == 0 else (T.S2, "S2")
+            for p in range(2):
+                mm([(H[:, 66 * p:66 * p + 66], T.oha[:, 4096 * h + 16 * p + k:4096 * h + 4096:32],
+                     T.ohb[:, 2112 * h + 16 * p + k:2112 * h + 2112:32], k == 0, k == 15) for k in range(16)],
+                   ["oha%d_%d" % (h, a) for a in range(16)] + ["ohb%d_%d" % (h, b) for b in range(8)] + ["ohbc%d" % h], [hk], 16 * 66)
+            axpb("hp", T.hp[:, 132 * h:132 * h + 132], H[:, 0:132], 1.0, 2.0, [hk], ["hp%d" % h], 132)
+            tt(T.ub[:, 132 * h:132 * h + 130], H[:, 0:130], T.hp[:, 132 * h + 2:132 * h + 132], A.is_equal, [hk, "hp%d" % h],
+               ["ub%d" % h], 130, 1.0)
+        for h in range(2):
+            mm([(T.S0[64 * h + 32 * u:64 * h + 32 * u + 32, 32 * a:32 * a + 32],
+                 T.rl[:, 256 * u + C * p + 32 * a:256 * u + C * p + 32 * a + 32],
+                 T.ub[:, 132 * h + 66 * p + u:132 * h + 66 * p + 64:2], p == 0, p == 1)
+                for u in range(2) for a in range(4) for p in range(2)], ["ub%d" % h, "rl00", "rl01", "rl10", "rl11"], ["S0"], 512)
+        axpb("mt", T.mt[:], T.S0[:, 0:C], V, -V, ["S0"], ["mt"], C)
+        if not last:
+            if t == 0:
+                axpb("nu", SO[0], T.mt[:], -1.0, -V, ["mt"], ["so0"], C)
+            else:
+                axpb("nu", T.nu[:], T.mt[:], -1.0, -V, ["mt"], ["nu"], C)
+                tt(SO[t], T.nu[:], SI[t], A.add, ["nu", "si%d" % t], ["so%d" % t], C, ext=[AS[t]])
+            send(rank - 1, SI[t + 1], SO[t], "as%d" % (t + 1), "sil", ["so%d" % t], ["si%d" % (t + 1)], M["sil"])
+        for b in range(4):
+            if CFG["xt"][b] == "a":
+                table_x(t, b)
+        for b in range(4):
+            s = slice(512 * b, 512 * b + 512)
+            table_mask(T.mt[:], "mt", b, CFG["xt"][b] == "a")
+            if CFG["xt"][b] == "a":
+                act(T.xt[:, s], B[b][:], AF.Copy, ["B%d" % b], ["xt%d" % b], 512)
+            else:
+                tt(T.xt[:, s], X[t][:, s], B[b][:], A.add, ["x%d" % t, "B%d" % b], ["xt%d" % b], 512, 1.0, ext=[AX[t]])
+        for b in range(4):
+            gather(CFG["xgl" if last else "xg"][b], T.xg[:, 512 * b:512 * b + 512], T.xt[:, 0:W + 1], T[po][:, 32 * b:32 * b + 32],
+                   ["xt0", "xt1", "xt2", "xt3", "xtc", po], ["xg%d" % b])
+        if last:
+            zwork(t, True)
+            break
+        xgk = ["xg0", "xg1", "xg2", "xg3"]
+        for b in range(3):
+            table_x(t + 1, b)
+        for h in range(2):
+            mm([(T.S0[:, 64 * h:64 * h + 64], T.gxb[:, 32 - k:160 - k], T.xg[:, 1024 * h + k:1024 * h + 1024:16], k == 0, k == 15)
+                for k in range(16)], xgk[2 * h:2 * h + 2] + ["gxb"], ["S0"], 1024)
+        for q in range(4):
+            mm([(T.B3[:, 0:C], T.xg[:, k:W:16], T.id2[:], k == 0, k == 15) for k in range(4 * q, 4 * q + 4)], xgk + ["id2"], ["B3"], 512)
+        ts(T.ak[:], T.S0[:, 0:C], 0.0, None, A.is_gt, None, ["S0"], ["ak"], C)
+        tt(T.lt[:], T.S0[:, 0:C], T.thr[:], A.is_gt, ["S0", "thr"], ["lt"], C, 1.0)
+        ik = "ivi" if t == 0 else "im"
+        tt(T.jj[:], T.lt[:], T[ik][:], A.add, ["lt", ik], ["jj"], C)
+        mm([(T.S2[:, 0:C], T.sh[:], T.ak[:], True, True)], ["sh", "ak"], ["S2"], C)
+        ts(T.lv[:], T.S2[:, 0:C], pl, None, A.is_gt, None, ["S2", "pl"], ["lv"], C)
+        rtk = ["rt%d" % j for j in range(len(segments()))] + ["rtz"]
+        for j, bank in ((2, "S2"), (1, "S1"), (0, "S0")):
+            t0, t1 = PARTS[j]
+            nn = C * (t1 - t0)
+            i0 = 512 if j == 2 else 0
+            mm([(T[bank][:, 0:nn], T.bp[:, 0:C] if j == 0 else T.bp[:, C:2 * C], T.ind[:, i0:i0 + nn], True, False)], ["bp", "bw", "ind"], [bank], nn)
+            mm([(T[bank][:, C * (x - t0):C * (x - t0) + C], T.rt[:, C * x:C * x + C], T.jj[:], False, False) for x in range(t0, t1)],
+               rtk + ["jj"], [bank], nn)
+            mm([(T[bank][:, C * (x - t0):C * (x - t0) + C], T.ll[:, C * x:C * x + C], T.lv[:], False, x == t1 - 1) for x in range(t0, t1)],
+               ["ll%d" % j, "lv"], [bank], nn)
+            ts(T.fc[:, C * t0:C * t1], T[bank][:, 0:nn], 0.0, 2048.0, A.max, A.min, [bank], ["fc%d" % j], nn)
+        tn = (t + 1) * C
+        lst = [(T.S2[:, 0:C], T.rep8[:], T.tauf[:, tn:tn + C], True, False)]
+        for h in range(2):
+            lst.append((T.S2[:, 64 * h:64 * h + 64], T.tri16[:, 16 - 16 * h:144 - 16 * h], T.jj[:, 64 * h:64 * h + 64], False, False))
+        mm(lst, ["rep8", "taufr", "tri16", "jj"], ["S2"], 640)
+        for j in (2, 1, 0):
+            t0, t1 = PARTS[j]
+            mm([(T.S2[:, 64 * h:64 * h + 64], T.ft[:, 144 * x + 16 - 16 * h:144 * x + 144 - 16 * h],
+                 T.fc[:, C * x + 64 * h:C * x + 64 * h + 64], False, j == 0 and x == t1 - 1 and h == 1)
+                for x in range(t0, t1) for h in range(2)], ["fc%d" % j, "ft0", "ft1", "ft2"], ["S2"], C * (t1 - t0))
+        cp(T.ri[:], T.B3[:, 0:C], ["B3"], ["ri"], C)
+        ts(T.rq[:], T.ri[:], 18, None, A.arith_shift_right, None, ["ri"], ["rq"], C)
+        ts(T.rx[:], T.ri[:], 262143, None, A.bitwise_and, None, ["ri"], ["rx"], C)
+        tt(T.ru[:], T.rq[:], T.nd[:], A.mult, ["rq", "nd"], ["ru"], C)
+        tt(T.vv[0:64, :], T.ru[0:64, :], T.rx[0:64, :], A.add, ["ru", "rx"], ["vv"], C)
+        tt(T.vv[64:128, 16:C], T.ru[64:128, 0:112], T.rx[64:128, 0:112], A.add, ["ru", "rx"], ["vv"], 112)
+        tt(T.vv[64:128, 0:16], T.ru[64:128, 112:C], T.rx[64:128, 112:C], A.add, ["ru", "rx"], ["vv"], 16)
+        table_x(t + 1, 3)
+        for b in range(4):
+            table_mask(SI[t + 1], "si%d" % (t + 1), b, True, [AS[t + 1]])
+            act(T.xm[:, 512 * b:512 * b + 512], B[b][:], AF.Copy, ["B%d" % b], ["xm%d" % b], 512)
+            if b == 0:
+                act(T.xm[:, W:W + 1], T.xm[:, 0:1], AF.Copy, ["xm0"], ["xmc"], 1)
+        profile(t + 1)
+        times(t + 1)
+    cp(T.yo[:], T.SY[:, 0:C], ["SY"], ["yo"], C)
+    dma("sp", T.y[:], T.yo[:], ["yo"], [], 2000)
+    late = [o for o in const_ops if any(k in BANKS for k in o["r"] + o["w"])]
+    rest = [o for o in ops if not any(o is x for x in late)]
+    at = min(i for i, o in enumerate(rest) if "kf" in o["w"])
+    return rest[:at] + late + rest[at:]
+
+
+def schedule(ops):
+    nops = len(ops)
+    lastw, readers = {}, {}
+    pred = [set() for _ in ops]
+    for i, o in enumerate(ops):
+        rd = [k for k in o["r"] if k not in BANKS]
+        wr = o["w"] + [k for k in o["r"] if k in BANKS]
+        for k in rd:
+            if k in lastw:
+                pred[i].add(lastw[k])
+        for k in wr:
+            if k in lastw:
+                pred[i].add(lastw[k])
+            pred[i].update(readers.get(k, ()))
+        for k in rd:
+            readers.setdefault(k, []).append(i)
+        for k in wr:
+            lastw[k] = i
+            readers[k] = []
+        pred[i].discard(i)
+    succ = [[] for _ in ops]
+    for i in range(nops):
+        for j in pred[i]:
+            succ[j].append(i)
+
+    def gap(j, i):
+        if "bulk" in ops[j]["w"] and "bulk" in ops[i]["w"]:
+            return 0.0
+        return ops[j]["lat"] + (0.0 if ops[j]["eng"] == ops[i]["eng"] == "pe" else M["hop"])
+
+    prio = [0.0] * nops
+    for i in range(nops - 1, -1, -1):
+        prio[i] = ops[i]["dur"] + max([gap(i, k) + prio[k] for k in succ[i]] + [ops[i]["lat"]])
+
+    def place(seq, before, back):
+        at, busy = [0.0] * nops, {}
+        for i in seq:
+            s = ops[i]["lat"] if back and not before[i] else 0.0
+            for j in before[i]:
+                s = max(s, at[j] + ops[j]["dur"] + (gap(i, j) if back else gap(j, i)))
+            lst = busy.setdefault(ops[i]["eng"], [])
+            d = ops[i]["dur"]
+            pos = 0
+            for a, b in lst:
+                if b > s:
+                    if s + d <= a:
+                        break
+                    s = b
+                pos += 1
+            lst.insert(pos, (s, s + d))
+            at[i] = s
+        return at
+
+    def length(at):
+        return max(at[i] + ops[i]["dur"] + (0.0 if succ[i] else ops[i]["lat"]) for i in range(nops))
+
+    start = place(sorted(range(nops), key=lambda i: (-prio[i], i)), pred, False)
+    best = start
+    for _ in range(M["rounds"]):
+        rev = place(sorted(range(nops), key=lambda i: (-(start[i] + ops[i]["dur"]), -i)), succ, True)
+        start = place(sorted(range(nops), key=lambda i: (-(rev[i] + ops[i]["dur"]), i)), pred, False)
+        if length(start) < length(best):
+            best = start
+    rng = np.random.default_rng(M["seed"])
+    blen = length(best)
+    for it in range(M["tries"]):
+        key = list(best)
+        lo = rng.random() * blen
+        noise = rng.random(nops) * (300.0, 800.0, 2000.0)[it % 3]
+        for i in range(nops):
+            k = key[i] - (float(noise[i]) if lo <= key[i] <= lo + 12000.0 else 0.0)
+            for j in pred[i]:
+                if key[j] >= k:
+                    k = key[j] + 0.001
+            key[i] = k
+        start = place(sorted(range(nops), key=lambda i: (key[i], i)), pred, False)
+        if it % 4 == 3:
+            rev = place(sorted(range(nops), key=lambda i: (-(start[i] + ops[i]["dur"]), -i)), succ, True)
+            start = place(sorted(range(nops), key=lambda i: (-(rev[i] + ops[i]["dur"]), i)), pred, False)
+        if length(start) <= blen:
+            best, blen = start, length(start)
+    order = sorted(range(nops), key=lambda i: (best[i], i))
+    return order, pred, best
+
+
+PLAN = {}
+
+
+def rank_program(g, core, T, topo):
+    rank = T.rank_of(core)
+    if rank is None:
+        return
+    ops = build(g, core, T, topo, rank)
+    if not PLAN:
+        PLAN["all ranks"] = schedule(ops)
+    order, pred, start = PLAN["all ranks"]
+    queue = {"pe": g.tensor, "dve": g.vector, "act": g.scalar, "pool": g, "sp": g.sync}
+    know = {q: {} for q in queue}
+    count = {"pe": 0, "dve": 0, "act": 0, "pool": 0}
+    done, snap, total = {}, {}, {}
+    for i in order:
+        o = ops[i]
+        q, kn = o["eng"], know[o["eng"]]
+        need = [(e[0], e[1], None) for e in o["ext"]]
+        for j in pred[i]:
+            pj = ops[j]
+            if pj["eng"] == q and q == "pe":
+                continue
+            if pj["sem"] is not None and pj["sem"].startswith("lo"):
+                continue
+            need.append((done[j][0], done[j][1], j))
+        need.sort(key=lambda x: -(start[x[2]] if x[2] is not None else -1.0))
+        for sem, val, j in need:
+            if kn.get(sem, 0) < val:
+                queue[q].wait_ge(T.sem[sem], val)
+                kn[sem] = val
+                if j is not None:
+                    for s2, v2 in snap[j].items():
+                        if kn.get(s2, 0) < v2:
+                            kn[s2] = v2
+        snap[i] = dict(kn)
+        if o["sem"] is None:
+            for call in o["calls"]:
+                call().then_inc(T.sem[q], 1)
+            count[q] += len(o["calls"])
+            done[i] = (q, count[q])
+        else:
+            ins = o["calls"][0]()
+            if o["sem"].startswith("ld"):
+                ins.then_inc(T.sem[o["sem"]], 16)
+            done[i] = (o["sem"], o["inc"])
+        total[done[i][0]] = done[i][1]
+        for e in o["ext"]:
+            total[e[0]] = e[1]
+    for sem, val in total.items():
+        if max(know[q].get(sem, 0) for q in know) < val:
+            g.wait_ge(T.sem[sem], val)

@@ -1,3 +1,4 @@
+import math
 import numpy as np
 from concourse.bass import DstId, RemoteDMATransfer
 from concourse.mybir import dt, AluOpType, AxisListType, ActivationFunctionType
@@ -5,7 +6,11 @@ from concourse.mybir import dt, AluOpType, AxisListType, ActivationFunctionType
 BF, F32, I32, U16, F16 = "bfloat16", "float32", "int32", "uint16", "float16"
 W, C, VI = 2048, 128, 4
 V = 131072.0
-BIG = 201326592.0
+CS = 85.0 / 64
+BIG = 1.5 * 2.0 ** 32
+BIG1 = 1.5 * 2.0 ** 23
+LOW = math.log(1.0 / 8191)
+SHIFT = 16.0
 
 
 def _sb(cols, dtype, rows=128):
@@ -14,41 +19,41 @@ def _sb(cols, dtype, rows=128):
 
 SCRATCH = {
     "x0": _sb(2064, BF), "x1": _sb(W, BF), "x2": _sb(W, BF), "x3": _sb(W, BF),
-    "g0": _sb(2064, BF), "g1": _sb(2064, BF), "g2": _sb(2064, BF), "g3": _sb(2064, BF),
-    "xm": _sb(2064, BF), "xt": _sb(2064, BF), "ga0": _sb(W, BF), "ga1": _sb(W, BF), "ms0": _sb(W, BF), "ms1": _sb(W, BF),
-    "xg": _sb(W, BF), "ab": _sb(W, F32), "zz": _sb(W, F32), "zs": _sb(1024, F32), "oha": _sb(8192, BF), "ohb": _sb(4224, BF),
-    "qa": _sb(512, BF), "qb": _sb(512, BF), "fc": _sb(1152, F16),
-    "ivi": _sb(C, I32), "pfi": _sb(C, I32), "ivf": _sb(C, F32), "pff": _sb(C, F32),
-    "taui": _sb(512, I32, 8), "tauf": _sb(512, F32, 8),
-    "ti": _sb(C, I32), "t0i": _sb(C, I32), "t0f": _sb(C, F32), "off0": _sb(C, U16), "off1": _sb(C, U16),
-    "tt2": _sb(256, F32), "kk": _sb(256, F32), "ki": _sb(C, I32), "kf": _sb(C, F32), "hii": _sb(C, I32), "loi": _sb(C, I32),
-    "k2": _sb(C, I32), "k3": _sb(C, I32), "po0": _sb(C, U16), "po1": _sb(C, U16), "thr": _sb(C, F32),
-    "hp": _sb(264, F32), "ub": _sb(264, BF), "mt": _sb(C, BF), "nu": _sb(C, BF),
-    "so": _sb(3 * C, BF), "si": _sb(3 * C, BF),
-    "ak": _sb(C, BF), "lt": _sb(C, BF), "lv": _sb(C, BF), "jj": _sb(C, F16), "im": _sb(C, I32),
-    "ri": _sb(C, I32), "rx": _sb(C, I32), "rq": _sb(C, I32), "ru": _sb(C, F32), "vv": _sb(C, F32), "fa": _sb(C, I32),
-    "fb": _sb(C, I32), "dn": _sb(C, I32), "dw": _sb(C, F32), "nd": _sb(C, F32),
-    "sa0": _sb(C, BF), "sa1": _sb(C, BF), "ra0": _sb(C, BF), "ra1": _sb(C, BF), "yo": _sb(C, F32),
-    "ia": _sb(192, I32), "iam": _sb(192, I32), "idf": _sb(192, F32), "id1": _sb(C, BF), "id125": _sb(C, BF), "id2": _sb(C, BF),
-    "pvi": _sb(1, I32), "pw": _sb(4, I32), "pc": _sb(8, F32), "jr": _sb(160, I32), "jm": _sb(160, I32), "jb": _sb(160, I32),
-    "jk": _sb(160, I32), "jmf": _sb(160, F32), "jbf": _sb(160, F32), "gxb": _sb(160, BF),
-    "blk": _sb(144, F32), "tri": _sb(144, F32), "c1": _sb(144, F32), "c3": _sb(C, F32), "c4": _sb(C, F32),
-    "c5": _sb(C, F32), "c6": _sb(C, F32), "c7": _sb(C, F32), "tri16": _sb(144, F16), "ntri": _sb(144, F16),
-    "tx": _sb(C, F16), "tz": _sb(C, F16), "sh": _sb(C, BF), "dm": _sb(C, F32), "bo8": _sb(8, BF),
-    "j16": _sb(512, BF), "rep": _sb(W, BF), "rep8": _sb(C, F32, 8), "rep80": _sb(C, F32, 8),
-    "ones": _sb(640, BF), "on16": _sb(C, F16), "rl": _sb(512, BF), "selx": _sb(W, BF), "km": _sb(512, F32),
-    "rt": _sb(1152, F16), "qt": _sb(1152, F16), "ll": _sb(1152, BF), "ft": _sb(1296, F16),
-    "b1": _sb(C, F32, 8), "b2": _sb(C, F32, 8), "bs": _sb(4, F32, 8), "bp": _sb(2 * C, BF, 8), "ind": _sb(640, BF, 8),
+    "g0": _sb(2064, BF), "g1": _sb(2064, BF), "g2": _sb(2064, BF), "g3": _sb(W, BF),
+    "xm": _sb(2064, BF), "xt": _sb(2064, BF), "gt": _sb(2064, BF),
+    "ga0": _sb(W, BF), "ga1": _sb(W, BF), "ms0": _sb(W, BF), "ms1": _sb(W, BF),
+    "xg": _sb(W, BF), "ab": _sb(W, F32), "zz": _sb(W, F32), "za": _sb(W, F32), "zs": _sb(1024, F32),
+    "oha": _sb(4096, BF), "ohb": _sb(4096, BF), "qa": _sb(512, BF), "qb": _sb(1024, BF), "fc": _sb(1152, F16),
+    "ivi": _sb(C, I32), "pfi": _sb(C, I32), "ivh": _sb(C, F16), "pff": _sb(C, F32),
+    "taui": _sb(512, I32, 8), "tauh": _sb(512, F16, 8),
+    "ti": _sb(C, I32), "t0i": _sb(C, I32), "t0h": _sb(C, F16), "off0": _sb(C, U16), "off1": _sb(C, U16),
+    "tc": _sb(C, F32), "on": _sb(C, BF), "idv": _sb(C, BF), "ki": _sb(C, I32), "hii": _sb(C, I32), "loi": _sb(C, I32),
+    "po0": _sb(C, U16), "po1": _sb(C, U16), "thr": _sb(C, F32),
+    "rr": _sb(80, F16), "ff": _sb(80, F16), "mt": _sb(4 * C, BF), "si": _sb(3 * C, BF), "vc": _sb(C, BF),
+    "nak": _sb(C, BF), "lt": _sb(C, BF), "lv": _sb(C, BF), "jj": _sb(C, F16), "im": _sb(C, I32), "tj": _sb(C, I32),
+    "ru": _sb(C, F32), "dn": _sb(C, I32), "q0": _sb(2 * C, BF), "q1": _sb(2 * C, BF), "yo": _sb(C, F32),
+    "onf": _sb(256, F32), "idw": _sb(256, F32), "id1": _sb(C, BF), "idc": _sb(C, BF), "id2": _sb(C, BF), "id64": _sb(C, BF),
+    "idn": _sb(C, BF), "id8p": _sb(C, BF), "id8n": _sb(C, BF),
+    "pvi": _sb(1, I32), "pw": _sb(4, I32), "pc": _sb(12, F32), "jr": _sb(160, I32), "jm": _sb(160, I32), "jb": _sb(160, I32),
+    "gxb": _sb(160, BF),
+    "blk": _sb(144, BF), "tri": _sb(144, BF), "ntri": _sb(144, BF), "c1": _sb(144, BF), "c3": _sb(C, BF), "c4": _sb(C, BF),
+    "c5": _sb(C, BF), "c7": _sb(C, F32), "blk18": _sb(C, BF), "blk16": _sb(C, BF),
+    "tx": _sb(C, BF), "tz": _sb(C, BF), "tq": _sb(2 * C, BF), "sh": _sb(C, BF), "dm": _sb(C, BF), "bo8": _sb(8, BF),
+    "j16": _sb(512, BF), "rep": _sb(1024, BF), "rep8": _sb(C, BF, 8), "rep80": _sb(C, BF, 8),
+    "ones": _sb(512, BF), "fl": _sb(C, BF, 8), "selx": _sb(W, BF), "km": _sb(512, BF),
+    "rt": _sb(1152, BF), "qt": _sb(1152, BF), "ll": _sb(1152, BF), "ft": _sb(1296, BF),
     "B0": ("psum", [128, 512], F32), "B1": ("psum", [128, 512], F32), "B2": ("psum", [128, 512], F32),
     "B3": ("psum", [128, 512], F32), "S0": ("psum", [128, 512], F32), "S1": ("psum", [128, 512], F32),
     "S2": ("psum", [128, 512], F32), "SY": ("psum", [128, 512], F32),
 }
-SEMAPHORES = (["pe", "dve", "act", "pool"] + ["ld%d" % i for i in range(16)] + ["ax1", "ax2", "ax3", "ag1", "ag2", "ag3",
-              "as1", "as2", "as3"] + ["lo%d" % i for i in range(9)])
+SEMAPHORES = (["pe", "dve", "act", "pool", "za1", "za2"] + ["ld%d" % i for i in range(16)] + ["ax1", "ax2", "ax3", "ag1", "ag2", "ag3",
+              "as1", "as2", "as3"] + ["lo%d" % i for i in range(12)])
 BANKS = ("B0", "B1", "B2", "B3", "S0", "S1", "S2", "SY")
-M = {"cy": 1.0, "pe": 0.5, "hop": 70.0, "gc": 1.56, "vo": 30.0, "ao": 65.0, "po": 15.0, "sil": 3500.0, "bulk": 11000.0,
-     "rounds": 2, "tries": 1200, "seed": 1}
-CFG = {"hear": "adaadaaa", "xt": "dada", "xg": "adad", "xgl": "adad", "small": "mt hp nu"}
+M = {"cy": 0.85, "pe": 0.43, "hop": 70.0, "gc": 1.56, "vo": 30.0, "ao": 65.0, "po": 5.0, "sil": 3500.0, "x1": 15000.0,
+     "bulk": 11000.0, "add": 6000.0, "rounds": 2, "tries": 60000, "seed": 1, "temp": 50.0, "mean": 0.5}
+CFG = {"hear": "adaaaaaa", "xt": "dada", "xg": "adad", "xm": "aaaa", "xgl": "dada", "gt": "adad", "qb": 8,
+       "bh": "01230123", "bt": "b0c1", "bm": "2301", "bz": "yyyy", "bzl": "2323", "bg": "0b1c"}
+BANK = dict(zip("0123abcy", BANKS))
 
 
 def segments():
@@ -64,15 +69,32 @@ def segments():
     return out
 
 
+def near(topo, a, b):
+    return b in topo.cores_of(a)
+
+
+def routes(topo, cores):
+    n, out = len(cores), []
+    for s in range(n):
+        holders = [s]
+        for d in range(1, VI):
+            r = (s - d) % n
+            same = [h for h in holders if near(topo, cores[h], cores[r])]
+            quiet = [h for h in holders if near(topo, cores[h], cores[(h - 1) % n])]
+            out.append((s, d, (same or quiet or [s])[0]))
+            holders.append(r)
+    return out
+
+
 def build(g, core, T, topo, rank):
     A, AF = AluOpType, ActivationFunctionType
     n = len(T.cores)
     ops = []
     CY = M["cy"]
 
-    def op(eng, calls, r, w, dur, sem=None, inc=0, lat=0.0, ext=()):
+    def op(eng, calls, r, w, dur, sem=None, inc=0, lat=0.0, ext=(), t0=0.0):
         ops.append({"eng": eng, "calls": calls, "r": list(r), "w": list(w), "dur": dur, "sem": sem, "inc": inc, "lat": lat,
-                    "ext": [e for e in ext if e is not None]})
+                    "ext": [e for e in ext if e is not None], "t0": t0})
 
     def vd(n_, c):
         return max(64.0, n_ * c) * CY + M["vo"]
@@ -95,17 +117,11 @@ def build(g, core, T, topo, rank):
     def act(out, a, f, r, w, n_, c=1.0, bias=0.0, scale=1.0, extra=0.0):
         op("act", [lambda: g.scalar.activation(out, a, f, bias=bias, scale=scale)], r, w, n_ * c * CY + M["ao"] + extra)
 
-    def axpb(name, out, a, scale, bias, r, w, n_):
-        if name in CFG["small"]:
-            act(out, a, AF.Identity, r, w, n_, bias=bias, scale=scale)
-        else:
-            ts(out, a, scale, bias, A.mult, A.add, r, w, n_)
-
     def one_mm(m):
         return lambda: g.tensor.matmul(m[0], m[1], m[2], m[3], m[4])
 
-    def mm(lst, r, w, cyc, ext=()):
-        op("pe", [one_mm(m) for m in lst], r, w, cyc * M["pe"] + M["po"] * len(lst), ext=ext)
+    def mm(lst, r, w, cyc, ext=(), t0=0.0):
+        op("pe", [one_mm(m) for m in lst], r, w, cyc * M["pe"] + M["po"] * len(lst), ext=ext, t0=t0)
 
     def iota(out, pat, base, cm, w, n_, flag=False):
         if flag:
@@ -113,8 +129,8 @@ def build(g, core, T, topo, rank):
         else:
             op("pool", [lambda: g.iota(out, pat, base, cm)], [], w, 130 + 2 * n_ * CY)
 
-    def sel(out, src, skey, pat, base, w, n_):
-        op("pool", [lambda: g.affine_select(out, src[:, 0:n_], pat, A.is_equal, 0.0, base, 1)], [skey], w, 170 + 2 * n_ * CY)
+    def sel(out, src, skey, pat, base, w, n_, cmp=A.is_equal, cm=1, c0=0):
+        op("pool", [lambda: g.affine_select(out, src[:, c0:c0 + n_], pat, cmp, 0.0, base, cm)], [skey], w, 170 + 2 * n_ * CY)
 
     nld = [0]
 
@@ -124,178 +140,192 @@ def build(g, core, T, topo, rank):
         eng = g.sync if q == "sp" else g.scalar
         op(q, [lambda: eng.dma_start(out, a)], r, w, 100.0, sem=s, inc=16, lat=lat)
 
+    def engines(src, dst):
+        if not near(topo, src, dst):
+            return topo.engines(src, dst)
+        far = [c for c in T.cores if not near(topo, src, c)][0]
+        return [e for e in topo.engines(src, dst) if e not in topo.engines(src, far)]
+
     nlo = [0]
 
-    def emask(lst):
-        m = 0
-        for e in lst:
-            m |= 1 << e
-        return m
-
-    def engines(src, dst, kind):
-        e = topo.engines(src, dst)
-        return {"all": e, "bulk": e[:4], "sil": e[4:8]}[kind]
-
-    def send(dst_rank, out, a, sem, kind, r, w, lat):
-        d = T.cores[dst_rank % n]
-        e = engines(core, d, kind)
-        rid, pid = topo.addr(d, core)
+    def send(items, r, w, lat, ext=()):
+        trs, inc = [], 0
+        for dst_rank, out, srcs, sem in items:
+            d = T.cores[dst_rank % n]
+            e = engines(core, d)
+            rid, pid = topo.addr(d, core)
+            trs.append(RemoteDMATransfer(dst_ids=[DstId(rid=rid, pnc=pid)], dma_engine_mask=sum(1 << x for x in e),
+                                         remote_sem=T.sem[sem], srcs=srcs, dsts=[out], alu_op=1 if len(srcs) > 1 else 0))
+            inc += len(e)
         s = "lo%d" % nlo[0]
         nlo[0] += 1
-        op("pool", [lambda: g.remote_dma(out, a, T.sem[sem], T.sem[s], pid, rid, emask(e))], r, w, 1000.0, sem=s, inc=len(e), lat=lat)
-
-    def arrival(src_rank, sem, kind):
-        return (sem, len(engines(T.cores[src_rank % n], core, kind)))
+        op("pool", [lambda: g.remote_dma_fused(trs, local_sem=T.sem[s])], r, w, 1000.0, sem=s, inc=inc, lat=lat, ext=ext)
 
     X = [T.x0, T.x1, T.x2, T.x3]
     G = [T.g0, T.g1, T.g2, T.g3]
     B = [T.B0, T.B1, T.B2, T.B3]
-    ident = T.idf[:, 16:144]
+    ident = T.idw[:, 0:C]
+    ways = routes(topo, T.cores)
+    sender = {d: h for s, d, h in ways if (s - d) % n == rank}
+    AX = [None] + [("ax%d" % t, len(engines(T.cores[sender[t]], core))) for t in range(1, VI)]
+    AG = [None] + [("ag%d" % t, len(engines(T.cores[sender[t]], core))) for t in range(1, VI)]
+    AS = [None] + [("as%d" % t, len(engines(T.cores[(rank + 1) % n], core))) for t in range(1, VI)]
+    quiet = near(topo, core, T.cores[(rank - 1) % n])
+
+    def bulk(window):
+        for name in "xg":
+            for held in range(VI - 1):
+                mine = [(s, d) for s, d, h in ways if h == rank and (s - rank) % n == held]
+                when = (0 if name == "x" or quiet else 1) if held == 0 else (1 if name == "x" else 2)
+                if mine and when == window:
+                    src = T["%s%d" % (name, held)][:, 0:W]
+                    send([(s - d, T["%s%d" % (name, d)][:, 0:W], [src], "a%s%d" % (name, d)) for s, d in mine],
+                         ["%s%d" % (name, held), "sent"], [], M["bulk"], [(AX if name == "x" else AG)[held]])
 
     dma("act", T.x0[:, 0:W], T.xs[:], [], ["x0"], 3300)
     dma("sp", T.ivi[:], T.iv[:], [], ["ivi"], 2200)
     dma("sp", T.taui[:, 0:C], T.tau[:], [], ["taui0"], 2000)
     dma("sp", T.pfi[:], T.pf[:], [], ["pfi"], 2200)
-    dma("sp", T.g0[:, 0:W], T.gn[:], [], ["g0"], 3500)
+    dma("sp", T.g0[:, 0:W], T.gn[:], [], ["g0"], 4500)
     for t in range(1, VI):
         dma("sp", T.taui[:, t * C:t * C + 64], T.tau[:, 0:64], [], ["taui%da" % t], 2000)
         dma("sp", T.taui[t:8, t * C + 64:t * C + C], T.tau[0:8 - t, 64:C], [], ["taui%db" % t], 2000)
         dma("sp", T.taui[0:t, t * C + 64:t * C + C], T.tau[8 - t:8, 64:C], [], ["taui%dc" % t], 2000)
-
-    send(rank - 1, T.x1[:], T.x0[:, 0:W], "ax1", "all", ["x0"], ["x1", "bulk"], 0.8 * M["bulk"])
-    for j, (d, name) in enumerate(((2, "x"), (1, "g"), (3, "x"), (2, "g"), (3, "g"))):
-        send(rank - d, T["%s%d" % (name, d)][:, 0:W], T[name + "0"][:, 0:W], "a%s%d" % (name, d), "bulk", [name + "0"],
-             ["%s%d" % (name, d), "bulk"], (j + 1.8) * M["bulk"])
-    AX = [None] + [arrival(rank + t, "ax%d" % t, "all" if t == 1 else "bulk") for t in range(1, VI)]
-    AG = [None] + [arrival(rank + t, "ag%d" % t, "bulk") for t in range(1, VI)]
-    AS = [None] + [arrival(rank + 1, "as%d" % t, "sil") for t in range(1, VI)]
-    SO = [T.so[:, C * t:C * t + C] for t in range(3)]
+    bulk(0)
+    MT = [T.mt[:, C * t:C * t + C] for t in range(VI)]
     SI = [None] + [T.si[:, C * t:C * t + C] for t in range(3)]
 
-    iota(T.ia[:], [[1, 192]], 112, -1, ["ia"], 192)
     iota(T.pvi[:], [[1, 1]], 0, 1, ["pvi"], 1)
     iota(T.jr[:], [[1, 160]], 96, 0, ["jr"], 160)
-    iota(T.j16[:], [[1, 32], [0, 16]], 0, -1, ["j16"], 512, True)
-    ms(T.ones[:], 1.0, ["ones"], 640)
-    ts(T.iam[:], T.ia[:], 127, None, A.bitwise_and, None, ["ia"], ["iam"], 192)
-    ts(T.idf[:], T.iam[:], 0.0, None, A.is_equal, None, ["iam"], ["idf"], 192)
-    for name, s in (("id125", 1.25), ("id1", 1.0), ("id2", 2.0)):
-        act(T[name][:], ident, AF.Identity, ["idf"], [name], C, scale=s)
+    iota(T.j16[:], [[1, 32], [0, 16]], 0, 0, ["j16"], 512, True)
+    ms(T.ones[:], 1.0, ["ones"], 512)
+    ms(T.onf[:], 1.0, ["onf"], 512)
+    sel(T.idw[:], T.onf, "onf", [[0, 2], [-1, C]], 0, ["idw"], 256)
+    act(T.id1[:], ident, AF.Sigmoid, ["idw"], ["id1"], C, bias=-200.0, scale=400.0, extra=1300.0)
+    for name, s in (("idc", 32 * CS), ("id64", 64.0), ("idn", -1.0), ("id8p", 8192.0), ("id8n", -8192.0), ("id2", 2.0), ("idv", V)):
+        act(T[name][:], ident, AF.Identity, ["idw"], [name], C, scale=s)
     ts(T.pw[:, 0:1], T.pvi[:], 112, None, A.bitwise_and, None, ["pvi"], ["pw0"], 1)
     ts(T.pw[:, 1:2], T.pvi[:], 15, None, A.bitwise_and, None, ["pvi"], ["pw1"], 1)
-    pp, p16, pg, pl, pk = (T.pc[:, i:i + 1] for i in range(5))
+    ts(T.pw[:, 2:3], T.pvi[:], 63, None, A.bitwise_and, None, ["pvi"], ["pw2"], 1)
+    pp, p16, pg, pl, pk, pn, pr, pa, pb = (T.pc[:, i:i + 1] for i in range(9))
     cp(pp, T.pvi[:], ["pvi"], ["pp"], 1)
     ts(p16, T.pvi[:], 16.0, None, A.mult, None, ["pvi"], ["p16"], 1)
     cp(pg, T.pw[:, 0:1], ["pw0"], ["pg"], 1)
     ts(pl, T.pw[:, 1:2], 14.5, -0.5, A.is_lt, A.add, ["pw1"], ["pl"], 1)
     ts(pk, T.pw[:, 1:2], 2048.0, None, A.mult, None, ["pw1"], ["pk"], 1)
+    ts(pn, T.pw[:, 1:2], -2048.0, None, A.mult, None, ["pw1"], ["pn"], 1)
+    ts(pr, T.pw[:, 1:2], -2048.0, 32768.0, A.mult, A.add, ["pw1"], ["pr"], 1)
+    cp(pa, T.pw[:, 2:3], ["pw2"], ["pa"], 1)
+    ts(pb, T.pw[:, 2:3], -32.0, None, A.add, None, ["pw2"], ["pb"], 1)
     ts(T.jm[:], T.jr[:], 127, None, A.bitwise_and, None, ["jr"], ["jm"], 160)
     ts(T.jb[:], T.jr[:], 112, None, A.bitwise_and, None, ["jr"], ["jb"], 160)
-    ts(T.jk[:], T.jr[:], 15, None, A.bitwise_and, None, ["jr"], ["jk"], 160)
-    cp(T.jmf[:], T.jm[:], ["jm"], ["jmf"], 160)
-    cp(T.jbf[:], T.jb[:], ["jb"], ["jbf"], 160)
-    ts(T.blk[:], T.jbf[:, 16:160], pg, None, A.is_equal, None, ["jbf", "pg"], ["blk"], 144)
-    ts(T.c1[:], T.jmf[:, 16:160], pp, None, A.is_ge, None, ["jmf", "pp"], ["c1"], 144)
+    ts(T.blk[:], T.jb[:, 16:160], pg, None, A.is_equal, None, ["jb", "pg"], ["blk"], 144)
+    ts(T.c1[:], T.jm[:, 16:160], pp, None, A.is_ge, None, ["jm", "pp"], ["c1"], 144)
     tt(T.tri[:], T.c1[:], T.blk[:], A.mult, ["c1", "blk"], ["tri"], 144)
-    ts(T.rep8[:], T.jbf[0:8, 32:160], T.pc[0:8, 1:2], None, A.is_equal, None, ["jbf", "p16"], ["rep8"], C)
-    ts(T.rep80[:], T.jmf[0:8, 32:160], T.pc[0:8, 1:2], -1.0, A.is_equal, A.mult, ["jmf", "p16"], ["rep80"], C)
-    ts(T.bo8[:], T.jmf[:, 32:160:16], pg, 8192.0, A.is_equal, A.mult, ["jmf", "pg"], ["bo8"], 8)
+    ts(T.rep8[:], T.jb[0:8, 32:160], T.pc[0:8, 1:2], None, A.is_equal, None, ["jb", "p16"], ["rep8"], C)
+    ts(T.rep80[:], T.jm[0:8, 32:160], T.pc[0:8, 1:2], -1.0, A.is_equal, A.mult, ["jm", "p16"], ["rep80"], C)
+    ts(T.bo8[:], T.jm[:, 32:160:16], pg, 8192.0, A.is_equal, A.mult, ["jm", "pg"], ["bo8"], 8)
+    for b, (col, key) in enumerate(((pa, "pa"), (pb, "pb"))):
+        ts(T.rep[:, 512 * b:512 * b + 512], T.j16[:], col, -CS, A.is_equal, A.mult, ["j16", key], ["rep%d" % b], 512, 0.5)
     for b in range(4):
-        s = slice(512 * b, 512 * b + 512)
-        ts(T.rep[:, s], T.j16[:], -32.0 * b, -0.625, A.is_equal, A.mult, ["j16"], ["rep%d" % b], 512, 0.5)
-        sel(T.selx[:, s], T.ones, "ones", [[-1, 4], [-16, 8], [0, 16]], -4 * b, ["selx%d" % b], 512)
-    ts(T.gxb[:], T.jmf[:], pg, None, A.is_equal, None, ["jmf", "pg"], ["gxb"], 160)
-    cp(T.tri16[:], T.tri[:], ["tri"], ["tri16"], 144)
-    ts(T.ntri[:], T.tri[:], -1.0, None, A.mult, None, ["tri"], ["ntri"], 144)
-    tt(T.c3[:], T.blk[:, 16:144], T.tri[:, 16:144], A.subtract, ["tri", "blk"], ["c3"], C)
-    ts(T.tx[:], T.c3[:], 2048.0, None, A.mult, None, ["c3"], ["tx"], C)
-    tt(T.c4[:], T.c3[:], T.blk[:, 16:144], A.add, ["c3", "blk"], ["c4"], C)
-    ts(T.tz[:], T.c4[:], -2048.0, None, A.mult, None, ["c4"], ["tz"], C)
-    ts(T.tz[:, 15:C:16], T.blk[:, 31:144:16], pk, None, A.mult, None, ["blk", "pk"], ["tz"], 8)
-    tt(T.c5[:], T.idf[:, 17:145], ident, A.subtract, ["idf"], ["c5"], C)
-    ts(T.c6[:], T.jk[:, 32:160], 14.5, None, A.is_lt, None, ["jk"], ["c6"], C)
-    tt(T.sh[:], T.c5[:], T.c6[:], A.mult, ["c5", "c6"], ["sh"], C)
-    ts(T.c4[:], T.jk[:, 32:160], 0.5, None, A.is_gt, None, ["jk"], ["c4"], C)
-    tt(T.c7[:], T.idf[:, 15:143], T.c4[:], A.mult, ["idf", "c4"], ["c7"], C)
-    tt(T.dm[:], ident, T.c7[:], A.subtract, ["idf", "c7"], ["dm"], C)
-    cp(T.on16[:], T.ones[:, 0:C], ["ones"], ["on16"], C, 0.5)
-    for h in range(2):
-        ms(T.ohb[:, 2112 * h + 2048:2112 * h + 2112], -1.0, ["ohbc%d" % h], 64)
+        sel(T.selx[:, 512 * b:512 * b + 512], T.ones, "ones", [[-1, 4], [-16, 8], [0, 16]], -4 * b, ["selx%d" % b], 512)
+    ts(T.gxb[:], T.jm[:], pg, 2.0 ** -13, A.is_equal, A.mult, ["jm", "pg"], ["gxb"], 160)
+    blk = T.blk[:, 16:144]
+    act(T.ntri[:], T.tri[:], AF.Identity, ["tri"], ["ntri"], 144, scale=-1.0)
+    act(T.blk18[:], blk, AF.Identity, ["blk"], ["blk18"], C, scale=2 * V)
+    act(T.blk16[:], blk, AF.Identity, ["blk"], ["blk16"], C, scale=1.0 / 16)
+    tt(T.c3[:], blk, T.tri[:, 16:144], A.subtract, ["tri", "blk"], ["c3"], C)
+    act(T.tx[:], T.c3[:], AF.Identity, ["c3"], ["tx"], C, scale=2048.0)
+    tt(T.c4[:], T.c3[:], blk, A.add, ["c3", "blk"], ["c4"], C)
+    act(T.tz[:], T.c4[:], AF.Identity, ["c4"], ["tz"], C, scale=-2048.0)
+    ms(T.tq[:], 0.0, ["tq"], 2 * C)
+    last_rows = T.blk[:, 31:144:16]
+    ts(T.tx[:, 15:C:16], last_rows, pn, None, A.mult, None, ["blk", "pn"], ["tx"], 8)
+    ts(T.tz[:, 15:C:16], last_rows, pk, None, A.mult, None, ["blk", "pk"], ["tz"], 8)
+    ts(T.tq[:, 15:C:16], last_rows, pk, None, A.mult, None, ["blk", "pk"], ["tq"], 8)
+    ts(T.tq[:, C + 15:2 * C:16], last_rows, pr, None, A.mult, None, ["blk", "pr"], ["tq"], 8)
+    tt(T.c5[:], ident, T.idw[:, 1:C + 1], A.subtract, ["idw"], ["c5"], C)
+    sel(T.sh[:], T.c5, "c5", [[0, 8], [-1, 16]], 15, ["sh"], C, A.is_gt, 0)
+    sel(T.c7[:], T.idw, "idw", [[0, 8], [1, 16]], 0, ["c7"], C, A.is_gt, 0, C - 1)
+    tt(T.dm[:], ident, T.c7[:], A.subtract, ["idw", "c7"], ["dm"], C)
+    ms(T.rr[:], 0.0, ["rr0", "rr1"], 80)
+    ms(T.ff[:], 0.0, ["ff0", "ff1"], 80)
+    ms(T.vc[:], V, ["vc"], C)
+    ms(T.fl[:], -15.0 / 256, ["fl"], C)
     ms(T.xt[:, W:2064], -V, ["xtc"], 16)
-    for t in range(VI):
+    ms(T.gt[:, W:2064], 0.0, ["gtc"], 16)
+    for t in range(VI - 1):
         ms(G[t][:, W:2064], 0.0, ["gc%d" % t], 16)
-    ms(T.km[:], 1.0, ["km"], 1024)
-    ms(T.km[:, 0:512:16], 0.0, ["km"], 64)
-    for u in range(2):
-        for p in range(2):
-            c0 = 256 * u + C * p
-            sel(T.rl[:, c0:c0 + C], T.ones, "ones", [[-2, 4], [-1000, 2], [-8, 16]], 1000 * p - u, ["rl%d%d" % (u, p)], C)
+    sel(T.km[:], T.ones, "ones", [[0, 32], [1, 16]], 0, ["km"], 512, A.is_gt, 0)
     for name in ("rt", "qt"):
-        ts(T[name][:, 1088:1152], T.ones[:, 0:64], 0.0, None, A.mult, None, ["ones"], [name + "z"], 64)
+        ms(T[name][:, 1088:1152], 0.0, [name + "z"], 64)
     tk = {}
     for j, (tile, q0, nq, k0, d0, dstep) in enumerate(segments()):
         c0 = C * tile + 8 * q0
-        sel(T.rt[:, c0:c0 + 8 * nq], T.on16, "on16", [[-16, 8], [-1, nq]], -k0, ["rt%d" % j], 8 * nq)
-        sel(T.qt[:, c0:c0 + 8 * nq], T.on16, "on16", [[-16, 8], [-dstep, nq]], -d0, ["qt%d" % j], 8 * nq)
+        sel(T.rt[:, c0:c0 + 8 * nq], T.ones, "ones", [[-16, 8], [-1, nq]], -k0, ["rt%d" % j], 8 * nq)
+        sel(T.qt[:, c0:c0 + 8 * nq], T.ones, "ones", [[-16, 8], [-dstep, nq]], -d0, ["qt%d" % j], 8 * nq)
         tk.setdefault(tile, []).append(j)
     PARTS = ((0, 4), (4, 8), (8, 9))
+    late_from = len(ops)
     for j, (t0, t1) in enumerate(PARTS):
-        keys = ["rt%d" % x for t in range(t0, t1) for x in tk[t]] + ["rtz"]
+        keys = [a + "%d" % x for t in range(t0, t1) for x in tk[t] for a in ("rt", "qt")] + ["rtz", "qtz"]
         nn = C * (t1 - t0)
-        mm([(B[j][:, 0:nn], (T.tx if j == 0 else T.tz)[:], T.rt[:, C * t0:C * t1], True, True)], keys + ["tx", "tz"], ["B%d" % j], nn)
+        u = 0 if j == 0 else C
+        mm([(B[j][:, 0:nn], (T.tx if j == 0 else T.tz)[:], T.rt[:, C * t0:C * t1], True, False),
+            (B[j][:, 0:nn], T.tq[:, u:u + C], T.qt[:, C * t0:C * t1], False, True)], keys + ["tx", "tz", "tq"], ["B%d" % j], 2 * nn)
         act(T.ll[:, C * t0:C * t1], B[j][:, 0:nn], AF.Copy, ["B%d" % j], ["ll%d" % j], nn)
     for j in range(3):
         lst = []
         for t in range(3 * j, 3 * j + 3):
             o = B[j][:, 144 * (t % 3):144 * (t % 3) + 144]
-            lst.append((o, T.qt[:, C * t:C * t + C], T.tri16[:], True, t >= 4))
+            lst.append((o, T.qt[:, C * t:C * t + C], T.tri[:], True, t >= 4))
             if t < 4:
                 lst.append((o, T.rt[:, C * t:C * t + C], T.ntri[:], False, True))
-        mm(lst, [a + "%d" % x for t in range(3 * j, 3 * j + 3) for x in tk[t] for a in ("rt", "qt")] + ["qtz", "tri16", "ntri"],
+        mm(lst, [a + "%d" % x for t in range(3 * j, 3 * j + 3) for x in tk[t] for a in ("rt", "qt")] + ["qtz", "tri", "ntri"],
            ["B%d" % j], 144 * len(lst))
-        cp(T.ft[:, 432 * j:432 * j + 432], B[j][:, 0:432], ["B%d" % j], ["ft%d" % j], 432)
-    iota(T.b1[:], [[1, C]], 0, 16, ["b1"], C, True)
-    for j, (base, cm) in enumerate(((-14336, 4096), (-2048, -2048), (16384, -4096), (2048, 2048))):
-        iota(T.bs[:, j:j + 1], [[1, 1]], base, cm, ["bs%d" % j], 1, True)
-    op("pool", [lambda: g.affine_select(T.ind[:], T.ones[0:8, :], [[-1, 5], [0, C]], A.is_equal, 0.0, 0, 1)], ["ones"], ["ind"],
-       170 + 1280 * CY)
-    for name, lim, j in (("bp", 119.5, 0), ("bw", 127.5, 2)):
-        ts(T.b2[:], T.b1[:], lim, T.bs[:, j:j + 1], A.is_gt, A.mult, ["b1", "bs%d" % j], ["b2"], C)
-        ts(T.bp[:, 64 * j:64 * j + C], T.b2[:], T.bs[:, j + 1:j + 2], None, A.add, None, ["b2", "bs%d" % (j + 1)], [name], C)
-    first_const_end = len(ops)
+        act(T.ft[:, 432 * j:432 * j + 432], B[j][:, 0:432], AF.Copy, ["B%d" % j], ["ft%d" % j], 432)
+    late = ops[late_from:]
+    del ops[late_from:]
 
-    def profile(t):
-        sa, ra = "sa%d" % (t % 2), "ra%d" % (t % 2)
-        ts(T.fa[:], T.vv[:], -4112.0 + 1.0 / 32, 1.0 / 32, A.add, A.mult, ["vv"], ["fa"], C)
-        ts(T.fb[:], T.vv[:], -4081.0 + 1.0 / 32, 1.0 / 32, A.add, A.mult, ["vv"], ["fb"], C)
-        tt(T[sa][:], T.fa[:], T.fb[:], A.add, ["fa", "fb"], [sa], C)
-        ts(T.dn[:], T.vv[:], -15.0 / 32, None, A.add, None, ["vv"], ["dn"], C)
-        ts(T.dw[:], T.dn[:], -4096.0, 1.0 / 16, A.add, A.mult, ["dn"], ["dw"], C)
-        tt(T[ra][:], T.dw[:], T[sa][:], A.subtract, ["dw", sa], [ra], C)
-        if t < VI - 1:
-            act(T.nd[:], T.dw[:], AF.Identity, ["dw"], ["nd"], C, bias=-256.0, scale=-1.0)
+    Q = [T.q0, T.q1]
+
+    def parts(t):
+        q, k = Q[t % 2], "q%d" % (t % 2)
+        cp(q[0:64, 0:C], T.dn[0:64, :], ["dn0"], [k + "a"], C)
+        cp(q[64:C, C:2 * C], T.dn[64:C, :], ["dn1", "dn2"], [k + "b"], C)
+        tt(q[64:C, 0:C], T.dn[0:64, :], q[0:64, 0:C], A.subtract, ["dn0", k + "a"], [k + "c"], C)
+        tt(q[0:64, C:2 * C], T.dn[64:C, :], q[64:C, C:2 * C], A.subtract, ["dn1", "dn2", k + "b"], [k + "d"], C)
+
+    def minus_d(t, b, bk):
+        q, k, h = Q[t % 2], "q%d" % (t % 2), b // 2
+        mm([(T[bk][:], q[:, C * h:C * h + C], T.rep[:, 512 * (b % 2):512 * (b % 2) + 512], True, False)],
+           [k + "ab"[h], k + "cd"[h], "rep%d" % (b % 2)], [bk], 512)
 
     def times(t):
         cp(T.ti[:], T.S2[:, 0:C], ["S2"], ["ti"], C)
         ts(T.t0i[:], T.ti[:], W - 1, None, A.bitwise_and, None, ["ti"], ["t0i"], C)
         cp(T.off0[:], T.t0i[:], ["t0i"], ["off0"], C)
         ts(T.off1[:], T.t0i[:], 1.0, None, A.add, None, ["t0i"], ["off1"], C)
-        cp(T.t0f[:], T.t0i[:], ["t0i"], ["t0f"], C)
-        mm([(T.S1[:, 0:C], T.t0f[:], ident, True, True)], ["t0f", "idf"], ["S1"], 512)
-        act(T.tt2[:, 0:C], T.S1[:, 0:C], AF.Identity, ["S1"], ["tt2a"], C, bias=32768.0)
-        act(T.tt2[:, C:2 * C], T.S1[:, 0:C], AF.Identity, ["S1"], ["tt2b"], C, bias=32768.0 + 4097.0)
+        cp(T.t0h[:], T.t0i[:], ["t0i"], ["t0h"], C)
         if 0 < t < VI - 1:
-            mm([(T.S2[:, 0:C], T.dm[:], T.t0f[:], True, False),
-                (T.S2[:, 0:C], T.rep80[:], T.tauf[:, t * C:t * C + C], False, True)], ["t0f", "dm", "rep80", "taufr"], ["S2"], 1024)
-            cp(T.ti[:], T.S2[:, 0:C], ["S2"], ["ti"], C)
-            ts(T.im[:], T.ti[:], W - 1, None, A.bitwise_and, None, ["ti"], ["im"], C)
+            mm([(T.S2[:, 0:C], T.dm[:], T.t0h[:], True, False),
+                (T.S2[:, 0:C], T.rep80[:], T.tauh[:, t * C:t * C + C], False, True)], ["t0h", "dm", "rep80", "tauhr"], ["S2"], 2 * C)
+            cp(T.tj[:], T.S2[:, 0:C], ["S2"], ["tj"], C)
+            ts(T.im[:], T.tj[:], W - 1, None, A.bitwise_and, None, ["tj"], ["im"], C)
 
-    def table_x(t, b):
-        mm([(B[b][:], T.id1[:], X[t][:, 512 * b:512 * b + 512], True, False)], ["x%d" % t, "id1"], ["B%d" % b], 512, [AX[t]])
-
-    def table_mask(msk, mkey, b, with_x, ext=()):
-        mm([(B[b][:, C * j:C * j + C], T.selx[:, C * (4 * b + j):C * (4 * b + j) + C], msk, not with_x, (not with_x) or j == 3)
-            for j in range(4)], [mkey, "selx%d" % b], ["B%d" % b], 512, ext)
+    def table(eng, out, okey, src, skey, sext, msk, mkey, mext, b, bank, clip=False, t0=0.0):
+        s, bk = slice(512 * b, 512 * b + 512), BANK[bank]
+        with_x = eng == "a" or clip
+        if with_x:
+            mm([(T[bk][:], T.id1[:], src[:, s], True, False)], [skey, "id1"], [bk], 512, [sext], t0)
+        mm([(T[bk][:, C * j:C * j + C], T.selx[:, C * (4 * b + j):C * (4 * b + j) + C], msk, not with_x, (not with_x) or j == 3)
+            for j in range(4)], [mkey, "selx%d" % b], [bk], 512, [mext])
+        if eng == "a":
+            act(out[:, s], T[bk][:], AF.Relu if clip else AF.Copy, [bk], [okey + "%d" % b], 512)
+        elif clip:
+            ts(out[:, s], T[bk][:], 0.0, None, A.max, None, [bk], [okey + "%d" % b], 512)
+        else:
+            tt(out[:, s], src[:, s], T[bk][:], A.add, [skey, bk], [okey + "%d" % b], 512, 1.0, ext=[sext])
 
     def gather(eng, out, win, off, r, w):
         if eng == "a":
@@ -303,57 +333,50 @@ def build(g, core, T, topo, rank):
         else:
             cp(out, win.indirect(off), r, w, 512, M["gc"])
 
-    def zwork(t, last):
-        sa, ra, po = "sa%d" % (t % 2), "ra%d" % (t % 2), "po%d" % (t % 2)
+    def weights(t):
+        for b in range(4):
+            s, bk = slice(512 * b, 512 * b + 512), BANK[CFG["bz" if t < VI - 1 else "bzl"][b]]
+            minus_d(t, b, bk)
+            mm([(T[bk][:], T.idc[:], T.xg[:, s], False, True)], ["xg%d" % b, "idc"], [bk], 512)
+            act(T.ab[:, s], T[bk][:], AF.Abs, [bk], ["ab%d" % b], 512)
+            act(T.ab[:, s], T.ab[:, s], AF.Sigmoid, ["ab%d" % b], ["ab%d" % b], 512, bias=-SHIFT, scale=-1.0 / (256 * CS))
+
+    def terms(t, win, keys):
+        po = "po%d" % (t % 2)
+        z, zk = (T.za, "za") if t == 0 else (T.zz, "zz")
         for b in range(4):
             s = slice(512 * b, 512 * b + 512)
-            mm([(B[b][:], T[sa][:], T.rep[:, s], True, False), (B[b][:], T[ra][:], T.rep[:, s], False, False)],
-               [sa, ra, "rep%d" % b], ["B%d" % b], 1024)
-            mm([(B[b][:], T.id125[:], T.xg[:, s], False, True)], ["xg%d" % b, "id125"], ["B%d" % b], 512)
-        for b in range(4):
-            s = slice(512 * b, 512 * b + 512)
-            act(T.ab[:, s], B[b][:], AF.Abs, ["B%d" % b], ["ab%d" % b], 512, bias=-160.0)
-            act(T.ab[:, s], T.ab[:, s], AF.Exp, ["ab%d" % b], ["ab%d" % b], 512, scale=-0.1, extra=1300.0 if t + b == 0 else 0.0)
-            tt(T.zz[:, s], G[t][:, 0:2064].indirect(T[po][:, 32 * b:32 * b + 32]), T.ab[:, s], A.mult,
-               ["ab%d" % b, po, "gc%d" % t, "g%d" % t], ["zz%d" % b], 512, M["gc"], ext=[AG[t]])
-        if t == 0:
-            for q in range(8):
-                mm([(T.SY[:, 0:C], ident, T.zz[:, k:W:16], k == 0, False) for k in (2 * q, 2 * q + 1)],
-                   ["zz0", "zz1", "zz2", "zz3", "idf"], ["SY"], 1024)
-            return
-        for h in range(2):
-            w0 = 16 + 16 * t * h
-            if last and h == 1:
-                for b in (2, 3):
-                    zs = T.zs[:, 512 * (b - 2):512 * (b - 1)]
-                    op("dve", [scan(zs, T.zz[:, 512 * b:512 * b + 512])], ["km", "zz%d" % b], ["zs%d" % b], vd(512, 1.0))
-                    mm([(T.SY[:, 32 * b:32 * b + 32], T.idf[:, w0:w0 + C], T.zs[:, 512 * (b - 2) + 15:512 * (b - 1):16], False, b == 3)],
-                       ["zs%d" % b, "idf"], ["SY"], 256)
-                continue
-            for q in range(4):
-                mm([(T.SY[:, 64 * h:64 * h + 64], T.idf[:, w0:w0 + C], T.zz[:, 1024 * h + k:1024 * h + 1024:16], False, False)
-                    for k in range(4 * q, 4 * q + 4)], ["zz%d" % (2 * h), "zz%d" % (2 * h + 1), "idf"], ["SY"], 1024)
+            tt(z[:, s], win[:, 0:2064].indirect(T[po][:, 32 * b:32 * b + 32]), T.ab[:, s], A.mult,
+               ["ab%d" % b, po] + keys, [zk + "%d" % b], 512, M["gc"], ext=[AG[t]])
+        if 0 < t < VI - 1:
+            u = 16 * t
+            pairs = ((T.za[:, 0:1024], T.zz[:, 0:1024]), (T.za[0:C - u, 1024:W], T.zz[u:C, 1024:W]), (T.za[C - u:C, 1024:W], T.zz[0:u, 1024:W]))
+            op("pool", [add_dma(o, a) for o, a in pairs], ["zz%d" % b for b in range(4)], ["za%d" % b for b in range(4)],
+               3000.0, sem="za%d" % t, inc=48, lat=M["add"])
+
+    def add_dma(out, a):
+        return lambda: g.dma_start(out, a, accum_op=A.add)
 
     def scan(out, data):
         return lambda: g.vector.tensor_tensor_scan(out, T.km[:], data, 0.0, A.mult, A.add)
 
-    cp(T.ivf[:], T.ivi[:], ["ivi"], ["ivf"], C)
-    cp(T.tauf[:, 0:C], T.taui[:, 0:C], ["taui0"], ["tauf0"], C)
-    mm([(T.S2[:, 0:C], T.tri[:, 16:144], T.ivf[:], True, False), (T.S2[:, 0:C], T.rep8[:], T.tauf[:, 0:C], False, True)],
-       ["tri", "ivf", "rep8", "tauf0"], ["S2"], 1024)
+    cp(T.ivh[:], T.ivi[:], ["ivi"], ["ivh"], C)
+    cp(T.tauh[:, 0:C], T.taui[:, 0:C], ["taui0"], ["tauh0"], C)
+    mm([(T.S2[:, 0:C], T.tri[:, 16:144], T.ivh[:], True, False), (T.S2[:, 0:C], T.rep8[:], T.tauh[:, 0:C], False, True)],
+       ["tri", "ivh", "rep8", "tauh0"], ["S2"], 2 * C)
     cp(T.pff[:], T.pfi[:], ["pfi"], ["pff"], C)
-    mm([(T.S0[:, 0:C], T.pff[:], ident, True, True)], ["pff", "idf"], ["S0"], 512)
-    act(T.vv[:], T.S0[:, 0:C], AF.Copy, ["S0"], ["vv0", "vv1", "vv"], C)
-    profile(0)
+    mm([(T.S0[:, 0:C], T.pff[:], ident, True, True)], ["pff", "idw"], ["S0"], 512)
+    cp(T.dn[:], T.S0[:, 0:C], ["S0"], ["dn0", "dn1", "dn2"], C)
+    parts(0)
     act(T.x0[:, W:W + 1], T.x0[:, 0:1], AF.Copy, ["x0"], ["x0c"], 1)
-    cp(T.tauf[:, C:4 * C], T.taui[:, C:4 * C], ["taui%d%s" % (t, s) for t in (1, 2, 3) for s in "abc"], ["taufr"], 3 * C)
+    cp(T.tauh[:, C:4 * C], T.taui[:, C:4 * C], ["taui%d%s" % (t, s) for t in (1, 2, 3) for s in "abc"], ["tauhr"], 3 * C)
     times(0)
-    const_ops = ops[:first_const_end]
 
     GA, MS, OFF = [T.ga0, T.ga1], [T.ms0, T.ms1], [T.off0, T.off1]
+    R = CFG["qb"]
     for t in range(VI):
         last = t == VI - 1
-        sa, po = "sa%d" % (t % 2), "po%d" % (t % 2)
+        po = "po%d" % (t % 2)
         xw = T.x0 if t == 0 else T.xm
         xkeys = ["x0", "x0c"] if t == 0 else ["xm0", "xm1", "xm2", "xm3", "xmc"]
         for e in range(2):
@@ -361,135 +384,149 @@ def build(g, core, T, topo, rank):
                 s = slice(512 * b, 512 * b + 512)
                 gather(CFG["hear"][4 * e + b], GA[e][:, s], xw[:, 0:W + 1], OFF[e][:, 32 * b:32 * b + 32], xkeys + ["off%d" % e],
                        ["ga%d%d" % (e, b)])
-                mm([(B[b][:], T[sa][:], T.rep[:, s], True, False)], [sa, "rep%d" % b], ["B%d" % b], 512)
-                mm([(B[b][:], T.id125[:], GA[e][:, s], False, True)], ["ga%d%d" % (e, b), "id125"], ["B%d" % b], 512)
-                ts(MS[e][:, s], B[b][:], BIG - 160.0, BIG, A.add, A.not_equal, ["B%d" % b], ["ms%d%d" % (e, b)], 512)
+                bk = BANK[CFG["bh"][4 * e + b]]
+                minus_d(t, b, bk)
+                mm([(T[bk][:], T.idc[:], GA[e][:, s], False, True)], ["ga%d%d" % (e, b), "idc"], [bk], 512)
+                ts(MS[e][:, s], T[bk][:], BIG, BIG, A.add, A.not_equal, [bk], ["ms%d%d" % (e, b)], 512)
             for q in range(2):
-                mm([(T.S0[:, C * e + k:C * e + C:16], MS[e][:, k:W:16], T.bo8[:], True, True) for k in range(8 * q, 8 * q + 8)],
-                   ["ms%d%d" % (e, b) for b in range(4)] + ["bo8"], ["S0"], 512)
-        tt(T.kk[:], T.S0[:, 0:256], T.tt2[:], A.max, ["S0", "tt2a", "tt2b"], ["kk"], 256, 1.0)
-        tt(T.ki[:], T.kk[:, 0:C], T.kk[:, C:2 * C], A.min, ["kk"], ["ki"], C)
-        ts(T.loi[:], T.ki[:], 31, None, A.bitwise_and, None, ["ki"], ["loi"], C)
-        ts(T.hii[:], T.ki[:], 5, 0xFFF3F, A.arith_shift_right, A.bitwise_and, ["ki"], ["hii"], C)
+                mm([(T.S0[:, C * e + k:C * e + C:16], MS[e][:, k:W:16], T.bo8[:], e == 0, e == 0 or k == 15)
+                    for k in range(8 * q, 8 * q + 8)], ["ms%d%d" % (e, b) for b in range(4)] + ["bo8"], ["S0"], 512)
+            if e == 0:
+                ts(T.on[:], T.S0[:, 0:C], 36864.0, -1.0, A.is_lt, A.mult, ["S0"], ["on"], C)
+                mm([(T.S1[:, 0:C], T.t0h[:], T.id1[:], True, False), (T.S1[:, 0:C], T.id1[:], T.on[:], False, True)],
+                   ["t0h", "id1", "on"], ["S1"], 2 * C)
+                act(T.tc[:], T.S1[:, 0:C], AF.Identity, ["S1"], ["tc"], C, bias=32769.0)
+                mm([(T.S0[:, C:2 * C], T.idv[:], T.on[:], True, False)], ["idv", "on"], ["S0"], C)
+        tt(T.ki[:], T.S0[:, C:2 * C], T.tc[:], A.max, ["S0", "tc"], ["ki"], C, 1.0)
+        ts(T.loi[:], T.ki[:], 63, None, A.bitwise_and, None, ["ki"], ["loi"], C)
+        ts(T.hii[:], T.ki[:], 6, 0xD9F, A.arith_shift_right, A.bitwise_and, ["ki"], ["hii"], C)
+        if t == 0:
+            ops.extend(late)
         for h in range(2):
-            cp(T.qb[:, 256 * h:256 * h + 64], T.loi[:, 64 * h:64 * h + 64], ["loi"], ["qb%d0" % h], 64)
-        for h in range(2):
-            for s in range(4):
-                c0 = 256 * h + 64 * s
-                ts(T.qa[:, c0:c0 + 64], T.hii[:, 64 * h:64 * h + 64], -1024.0 - s, None, A.add, None, ["hii"], ["qa%d%d" % (h, s)], 64)
-                if s:
-                    act(T.qb[:, c0:c0 + 64], T.qb[:, 256 * h:256 * h + 64], AF.Identity, ["qb%d0" % h], ["qb%d%d" % (h, s)], 64, bias=-1.0 * s)
-            for a in range(16):
-                c0 = 4096 * h + 256 * a
+            for name, src, step, reps in (("qb", "loi", 2.0, R), ("qa", "hii", 1.0, 4)):
+                c0, key = 64 * reps * h, "%s%d" % (name, h)
+                cp(T[name][:, c0:c0 + 64], T[src][:, 64 * h:64 * h + 64], [src], [key + "0", key], 64)
+                r = 1
+                while r < reps:
+                    ts(T[name][:, c0 + 64 * r:c0 + 128 * r], T[name][:, c0:c0 + 64 * r], -step * r, None, A.add, None,
+                       [key], [key], 64 * r, 0.5)
+                    r *= 2
+            for a in range(8):
+                c0 = 2048 * h + 256 * a
                 ts(T.oha[:, c0:c0 + 256], T.qa[:, 256 * h:256 * h + 256], 4.0 * a, None, A.is_equal, None,
-                   ["qa%d%d" % (h, s) for s in range(4)], ["oha%d_%d" % (h, a)], 256, 0.5)
-            for b in range(8):
-                c0 = 2112 * h + 256 * b
-                act(T.ohb[:, c0:c0 + 256], T.qb[:, 256 * h:256 * h + 256], AF.Sign, ["qb%d%d" % (h, s) for s in range(4)],
-                    ["ohb%d_%d" % (h, b)], 256, bias=0.5 - 4.0 * b)
-        if t > 0:
-            zwork(t - 1, False)
-        cp(T.kf[:], T.ki[:], ["ki"], ["kf"], C)
-        mm([(T.S0[:, 0:C], T.kf[:], ident, True, True)], ["kf", "idf"], ["S0"], 512)
-        cp(T.k2[:], T.S0[:, 0:C], ["S0"], ["k2"], C)
-        if not last:
-            ts(T.thr[:], T.k2[:], 36864.0, 1.0e6, A.is_lt, A.mult, ["k2"], ["thr"], C)
-        ts(T.k3[:], T.k2[:], 0x367FF, None, A.bitwise_and, None, ["k2"], ["k3"], C)
-        ts(T[po][:], T.k3[:], 2048.0, None, A.min, None, ["k3"], [po], C)
+                   ["qa%d" % h], ["oha%d_%d" % (h, a)], 256, 0.5)
+            for b in range(32 // R):
+                c0 = 2048 * h + 64 * R * b
+                act(T.ohb[:, c0:c0 + 64 * R], T.qb[:, 64 * R * h:64 * R * (h + 1)], AF.Sigmoid, ["qb%d" % h, "id1"],
+                    ["ohb%d_%d" % (h, b)], 64 * R, bias=LOW - 200.0 * R * b, scale=100.0)
+        lst = []
+        for h in range(2):
+            lst.append((T.S0[64 * h:64 * h + 64, 0:C], T.qa[:, 256 * h:256 * h + 64], T.id64[:], True, False))
+            lst.append((T.S0[64 * h:64 * h + 64, 0:C], T.qb[:, 64 * R * h:64 * R * h + 64], T.id1[:], False, True))
+        mm(lst, ["qa00", "qa10", "qb00", "qb10", "id64", "id1"], ["S0"], 4 * C)
+        ts(T[po][:], T.S0[:, 0:C], 2048.0, None, A.min, None, ["S0"], [po], C)
+        if last:
+            for b in range(4):
+                gather(CFG["xgl"][b], T.xg[:, 512 * b:512 * b + 512], T.xm[:, 0:W + 1], T[po][:, 32 * b:32 * b + 32],
+                       xkeys + [po], ["xg%d" % b])
+            weights(t)
+            for q in range(8):
+                mm([(T.SY[:, 0:C], ident, T.za[:, k:W:16], k == 0, False) for k in (2 * q, 2 * q + 1)],
+                   ["za0", "za1", "za2", "za3", "idw"], ["SY"], 1024)
+        else:
+            tt(T.thr[:], T.S0[:, 0:C], T.t0h[:], A.is_equal, ["S0", "t0h"], ["thr"], C, 1.0)
         for h in range(2):
             H, hk = (T.S1, "S1") if h == 0 else (T.S2, "S2")
-            for p in range(2):
-                mm([(H[:, 66 * p:66 * p + 66], T.oha[:, 4096 * h + 16 * p + k:4096 * h + 4096:32],
-                     T.ohb[:, 2112 * h + 16 * p + k:2112 * h + 2112:32], k == 0, k == 15) for k in range(16)],
-                   ["oha%d_%d" % (h, a) for a in range(16)] + ["ohb%d_%d" % (h, b) for b in range(8)] + ["ohbc%d" % h], [hk], 16 * 66)
-            axpb("hp", T.hp[:, 132 * h:132 * h + 132], H[:, 0:132], 1.0, 2.0, [hk], ["hp%d" % h], 132)
-            tt(T.ub[:, 132 * h:132 * h + 130], H[:, 0:130], T.hp[:, 132 * h + 2:132 * h + 132], A.is_equal, [hk, "hp%d" % h],
-               ["ub%d" % h], 130, 1.0)
-        for h in range(2):
-            mm([(T.S0[64 * h + 32 * u:64 * h + 32 * u + 32, 32 * a:32 * a + 32],
-                 T.rl[:, 256 * u + C * p + 32 * a:256 * u + C * p + 32 * a + 32],
-                 T.ub[:, 132 * h + 66 * p + u:132 * h + 66 * p + 64:2], p == 0, p == 1)
-                for u in range(2) for a in range(4) for p in range(2)], ["ub%d" % h, "rl00", "rl01", "rl10", "rl11"], ["S0"], 512)
-        axpb("mt", T.mt[:], T.S0[:, 0:C], V, -V, ["S0"], ["mt"], C)
-        if not last:
-            if t == 0:
-                axpb("nu", SO[0], T.mt[:], -1.0, -V, ["mt"], ["so0"], C)
-            else:
-                axpb("nu", T.nu[:], T.mt[:], -1.0, -V, ["mt"], ["nu"], C)
-                tt(SO[t], T.nu[:], SI[t], A.add, ["nu", "si%d" % t], ["so%d" % t], C, ext=[AS[t]])
-            send(rank - 1, SI[t + 1], SO[t], "as%d" % (t + 1), "sil", ["so%d" % t], ["si%d" % (t + 1)], M["sil"])
-        for b in range(4):
-            if CFG["xt"][b] == "a":
-                table_x(t, b)
-        for b in range(4):
-            s = slice(512 * b, 512 * b + 512)
-            table_mask(T.mt[:], "mt", b, CFG["xt"][b] == "a")
-            if CFG["xt"][b] == "a":
-                act(T.xt[:, s], B[b][:], AF.Copy, ["B%d" % b], ["xt%d" % b], 512)
-            else:
-                tt(T.xt[:, s], X[t][:, s], B[b][:], A.add, ["x%d" % t, "B%d" % b], ["xt%d" % b], 512, 1.0, ext=[AX[t]])
-        for b in range(4):
-            gather(CFG["xgl" if last else "xg"][b], T.xg[:, 512 * b:512 * b + 512], T.xt[:, 0:W + 1], T[po][:, 32 * b:32 * b + 32],
-                   ["xt0", "xt1", "xt2", "xt3", "xtc", po], ["xg%d" % b])
+            for u in range(4):
+                c0 = 2048 * h + 16 * u
+                mm([(H[32 * u:32 * u + 32, 0:32], T.oha[:, c0 + k:2048 * h + 2048:64], T.ohb[:, c0 + k:2048 * h + 2048:64],
+                     k == 0, k == 15) for k in range(16)],
+                   ["oha%d_%d" % (h, a) for a in range(8)] + ["ohb%d_%d" % (h, b) for b in range(32 // R)], [hk], 16 * 32)
+            c0 = 40 * h
+            ts(T.rr[:, c0:c0 + 32], H[:, 0:32], BIG1, -BIG1, A.add, A.add, [hk], ["rr%d" % h], 32)
+            tt(T.ff[:, c0:c0 + 32], H[:, 0:32], T.rr[:, c0:c0 + 32], A.subtract, [hk, "rr%d" % h], ["ff%d" % h], 32, 1.0)
+            lst = []
+            for a in range(2):
+                even, odd = (T.S0[64 * h:64 * h + 64, C + 64 * a + p:C + 64 * a + 64:2] for p in range(2))
+                lst += [(even, T.id8p[:, a:C:2], T.ff[:, c0:c0 + 32], True, True),
+                        (odd, T.id1[:, a:C:2], T.rr[:, c0:c0 + 32], True, False),
+                        (odd, T.idn[:, a:C:2], T.rr[:, c0 + 1:c0 + 33], False, False),
+                        (odd, T.id8n[:, a:C:2], T.ff[:, c0 + 1:c0 + 33], False, True)]
+            mm(lst, ["rr%d" % h, "ff%d" % h, "id1", "idn", "id8p", "id8n"], ["S0"], 512)
+        mk = "mt%d" % t
+        ts(MT[t], T.S0[:, C:2 * C], 1.0, -V, A.not_equal, A.mult, ["S0"], [mk], C)
         if last:
-            zwork(t, True)
+            for b in range(4):
+                table(CFG["gt"][b], T.gt, "gt", G[t], "g%d" % t, AG[t], MT[t], mk, None, b, CFG["bg"][b], True)
+            terms(t, T.gt, ["gt0", "gt1", "gt2", "gt3", "gtc"])
+            w0 = 16 * t
+            for q in range(4):
+                mm([(T.SY[:, 0:64], ident, T.zz[:, k:1024:16], False, False) for k in range(4 * q, 4 * q + 4)],
+                   ["zz0", "zz1", "idw"], ["SY"], 1024)
+            for b in (2, 3):
+                zs = T.zs[:, 512 * (b - 2):512 * (b - 1)]
+                op("dve", [scan(zs, T.zz[:, 512 * b:512 * b + 512])], ["km", "zz%d" % b], ["zs%d" % b], vd(512, 1.0))
+                mm([(T.SY[:, 32 * b:32 * b + 32], T.idw[:, w0:w0 + C], T.zs[:, 512 * (b - 2) + 15:512 * (b - 1):16], False, b == 3)],
+                   ["zs%d" % b, "idw"], ["SY"], 256)
             break
+        send([(rank - 1, SI[t + 1], [MT[t], T.vc[:]] + ([SI[t]] if t else []), "as%d" % (t + 1))],
+             [mk, "vc", "si%d" % t], ["si%d" % (t + 1), "sent"], M["sil"], [AS[t]])
+        bulk(t + 1)
+        for b in range(4):
+            table(CFG["xt"][b], T.xt, "xt", X[t], "x%d" % t, AX[t], MT[t], mk, None, b, CFG["bt"][b])
+        for b in range(4):
+            gather(CFG["xg"][b], T.xg[:, 512 * b:512 * b + 512], T.xt[:, 0:W + 1], T[po][:, 32 * b:32 * b + 32],
+                   ["xt0", "xt1", "xt2", "xt3", "xtc", po], ["xg%d" % b])
         xgk = ["xg0", "xg1", "xg2", "xg3"]
-        for b in range(3):
-            table_x(t + 1, b)
         for h in range(2):
             mm([(T.S0[:, 64 * h:64 * h + 64], T.gxb[:, 32 - k:160 - k], T.xg[:, 1024 * h + k:1024 * h + 1024:16], k == 0, k == 15)
                 for k in range(16)], xgk[2 * h:2 * h + 2] + ["gxb"], ["S0"], 1024)
         for q in range(4):
-            mm([(T.B3[:, 0:C], T.xg[:, k:W:16], T.id2[:], k == 0, k == 15) for k in range(4 * q, 4 * q + 4)], xgk + ["id2"], ["B3"], 512)
-        ts(T.ak[:], T.S0[:, 0:C], 0.0, None, A.is_gt, None, ["S0"], ["ak"], C)
+            mm([(T.SY[:, 0:C], T.xg[:, k:W:16], T.id2[:], k == 0, False) for k in range(4 * q, 4 * q + 4)], xgk + ["id2"], ["SY"], 512)
+        ts(T.nak[:], T.S0[:, 0:C], 0.0, None, A.is_le, None, ["S0"], ["nak"], C)
         tt(T.lt[:], T.S0[:, 0:C], T.thr[:], A.is_gt, ["S0", "thr"], ["lt"], C, 1.0)
         ik = "ivi" if t == 0 else "im"
         tt(T.jj[:], T.lt[:], T[ik][:], A.add, ["lt", ik], ["jj"], C)
-        mm([(T.S2[:, 0:C], T.sh[:], T.ak[:], True, True)], ["sh", "ak"], ["S2"], C)
+        mm([(T.S2[:, 0:C], T.sh[:], T.nak[:], True, True)], ["sh", "nak"], ["S2"], C)
         ts(T.lv[:], T.S2[:, 0:C], pl, None, A.is_gt, None, ["S2", "pl"], ["lv"], C)
         rtk = ["rt%d" % j for j in range(len(segments()))] + ["rtz"]
         for j, bank in ((2, "S2"), (1, "S1"), (0, "S0")):
             t0, t1 = PARTS[j]
             nn = C * (t1 - t0)
-            i0 = 512 if j == 2 else 0
-            mm([(T[bank][:, 0:nn], T.bp[:, 0:C] if j == 0 else T.bp[:, C:2 * C], T.ind[:, i0:i0 + nn], True, False)], ["bp", "bw", "ind"], [bank], nn)
-            mm([(T[bank][:, C * (x - t0):C * (x - t0) + C], T.rt[:, C * x:C * x + C], T.jj[:], False, False) for x in range(t0, t1)],
-               rtk + ["jj"], [bank], nn)
-            mm([(T[bank][:, C * (x - t0):C * (x - t0) + C], T.ll[:, C * x:C * x + C], T.lv[:], False, x == t1 - 1) for x in range(t0, t1)],
-               ["ll%d" % j, "lv"], [bank], nn)
+            lst = []
+            for x in range(t0, t1):
+                o = T[bank][:, C * (x - t0):C * (x - t0) + C]
+                lst += [(o, T.rt[:, C * x:C * x + C], T.jj[:], True, False), (o, T.ll[:, C * x:C * x + C], T.lv[:], False, True)]
+            mm(lst, rtk + ["jj", "ll%d" % j, "lv"], [bank], 2 * nn)
             ts(T.fc[:, C * t0:C * t1], T[bank][:, 0:nn], 0.0, 2048.0, A.max, A.min, [bank], ["fc%d" % j], nn)
         tn = (t + 1) * C
-        lst = [(T.S2[:, 0:C], T.rep8[:], T.tauf[:, tn:tn + C], True, False)]
+        lst = [(T.S2[:, 0:C], T.rep8[:], T.tauh[:, tn:tn + C], True, False)]
         for h in range(2):
-            lst.append((T.S2[:, 64 * h:64 * h + 64], T.tri16[:, 16 - 16 * h:144 - 16 * h], T.jj[:, 64 * h:64 * h + 64], False, False))
-        mm(lst, ["rep8", "taufr", "tri16", "jj"], ["S2"], 640)
+            lst.append((T.S2[:, 64 * h:64 * h + 64], T.tri[:, 16 - 16 * h:144 - 16 * h], T.jj[:, 64 * h:64 * h + 64], False, False))
+        mm(lst, ["rep8", "tauhr", "tri", "jj"], ["S2"], 2 * C)
         for j in (2, 1, 0):
             t0, t1 = PARTS[j]
             mm([(T.S2[:, 64 * h:64 * h + 64], T.ft[:, 144 * x + 16 - 16 * h:144 * x + 144 - 16 * h],
                  T.fc[:, C * x + 64 * h:C * x + 64 * h + 64], False, j == 0 and x == t1 - 1 and h == 1)
                 for x in range(t0, t1) for h in range(2)], ["fc%d" % j, "ft0", "ft1", "ft2"], ["S2"], C * (t1 - t0))
-        cp(T.ri[:], T.B3[:, 0:C], ["B3"], ["ri"], C)
-        ts(T.rq[:], T.ri[:], 18, None, A.arith_shift_right, None, ["ri"], ["rq"], C)
-        ts(T.rx[:], T.ri[:], 262143, None, A.bitwise_and, None, ["ri"], ["rx"], C)
-        tt(T.ru[:], T.rq[:], T.nd[:], A.mult, ["rq", "nd"], ["ru"], C)
-        tt(T.vv[0:64, :], T.ru[0:64, :], T.rx[0:64, :], A.add, ["ru", "rx"], ["vv"], C)
-        tt(T.vv[64:128, 16:C], T.ru[64:128, 0:112], T.rx[64:128, 0:112], A.add, ["ru", "rx"], ["vv"], 112)
-        tt(T.vv[64:128, 0:16], T.ru[64:128, 112:C], T.rx[64:128, 112:C], A.add, ["ru", "rx"], ["vv"], 16)
-        table_x(t + 1, 3)
+        mm([(T.SY[:, 0:C], T.nak[:], T.blk18[:], False, False), (T.SY[:, 0:C], T.ones[0:8, 0:C], T.fl[:], False, True),
+            (T.SY[:, C:2 * C], T.nak[:], T.blk16[:], True, True)], ["nak", "blk18", "blk16", "ones", "fl"], ["SY"], 3 * C)
+        tt(T.ru[:], T.SY[:, C:2 * C], T.dn[:], A.mult, ["SY", "dn0", "dn1", "dn2"], ["ru"], C, 1.0)
+        tt(T.dn[0:64, :], T.SY[0:64, 0:C], T.ru[0:64, :], A.add, ["SY", "ru"], ["dn0"], C, 1.0)
+        tt(T.dn[64:C, 16:C], T.SY[64:C, 0:112], T.ru[64:C, 0:112], A.add, ["SY", "ru"], ["dn1"], 112, 1.0)
+        tt(T.dn[64:C, 0:16], T.SY[64:C, 112:C], T.ru[64:C, 112:C], A.add, ["SY", "ru"], ["dn2"], 16, 1.0)
+        weights(t)
         for b in range(4):
-            table_mask(SI[t + 1], "si%d" % (t + 1), b, True, [AS[t + 1]])
-            act(T.xm[:, 512 * b:512 * b + 512], B[b][:], AF.Copy, ["B%d" % b], ["xm%d" % b], 512)
+            table(CFG["xm"][b], T.xm, "xm", X[t + 1], "x%d" % (t + 1), AX[t + 1], SI[t + 1], "si%d" % (t + 1), AS[t + 1], b, CFG["bm"][b],
+                  t0=M["x1"] if t == 0 else 0.0)
             if b == 0:
                 act(T.xm[:, W:W + 1], T.xm[:, 0:1], AF.Copy, ["xm0"], ["xmc"], 1)
-        profile(t + 1)
+        parts(t + 1)
         times(t + 1)
-    cp(T.yo[:], T.SY[:, 0:C], ["SY"], ["yo"], C)
+        terms(t, G[t], ["gc%d" % t, "g%d" % t])
+    act(T.yo[:], T.SY[:, 0:C], AF.Identity, ["SY"], ["yo"], C, scale=math.exp(SHIFT))
     dma("sp", T.y[:], T.yo[:], ["yo"], [], 2000)
-    late = [o for o in const_ops if any(k in BANKS for k in o["r"] + o["w"])]
-    rest = [o for o in ops if not any(o is x for x in late)]
-    at = min(i for i, o in enumerate(rest) if "kf" in o["w"])
-    return rest[:at] + late + rest[at:]
+    return ops
 
 
 def schedule(ops):
@@ -497,11 +534,12 @@ def schedule(ops):
     lastw, readers = {}, {}
     pred = [set() for _ in ops]
     for i, o in enumerate(ops):
-        rd = [k for k in o["r"] if k not in BANKS]
-        wr = o["w"] + [k for k in o["r"] if k in BANKS]
+        rd, wr = o["r"], o["w"]
         for k in rd:
             if k in lastw:
                 pred[i].add(lastw[k])
+            if k in BANKS:
+                pred[i].update(j for j in readers.get(k, ()) if ops[j]["eng"] != o["eng"])
         for k in wr:
             if k in lastw:
                 pred[i].add(lastw[k])
@@ -518,63 +556,110 @@ def schedule(ops):
             succ[j].append(i)
 
     def gap(j, i):
-        if "bulk" in ops[j]["w"] and "bulk" in ops[i]["w"]:
+        if "sent" in ops[j]["w"] and "sent" in ops[i]["r"]:
             return 0.0
         return ops[j]["lat"] + (0.0 if ops[j]["eng"] == ops[i]["eng"] == "pe" else M["hop"])
 
+    fore = [[(j, ops[j]["dur"] + gap(j, i)) for j in pred[i]] for i in range(nops)]
+    back = [[(k, ops[k]["dur"] + gap(i, k)) for k in succ[i]] for i in range(nops)]
     prio = [0.0] * nops
     for i in range(nops - 1, -1, -1):
         prio[i] = ops[i]["dur"] + max([gap(i, k) + prio[k] for k in succ[i]] + [ops[i]["lat"]])
+    first = [o["t0"] for o in ops]
+    final = [0.0 if succ[i] else ops[i]["lat"] for i in range(nops)]
 
-    def place(seq, before, back):
+    def place(seq, before, low):
         at, busy = [0.0] * nops, {}
         for i in seq:
-            s = ops[i]["lat"] if back and not before[i] else 0.0
-            for j in before[i]:
-                s = max(s, at[j] + ops[j]["dur"] + (gap(i, j) if back else gap(j, i)))
+            s = low[i]
+            for j, d in before[i]:
+                if at[j] + d > s:
+                    s = at[j] + d
             lst = busy.setdefault(ops[i]["eng"], [])
             d = ops[i]["dur"]
-            pos = 0
-            for a, b in lst:
-                if b > s:
-                    if s + d <= a:
-                        break
-                    s = b
+            pos = len(lst)
+            while pos > 0 and lst[pos - 1][1] > s:
+                pos -= 1
+            while pos < len(lst) and s + d > lst[pos][0]:
+                s = max(s, lst[pos][1])
                 pos += 1
             lst.insert(pos, (s, s + d))
             at[i] = s
         return at
 
     def length(at):
-        return max(at[i] + ops[i]["dur"] + (0.0 if succ[i] else ops[i]["lat"]) for i in range(nops))
+        return max(at[i] + ops[i]["dur"] + final[i] for i in range(nops))
 
-    start = place(sorted(range(nops), key=lambda i: (-prio[i], i)), pred, False)
+    def both_ways(start):
+        rev = place(sorted(range(nops), key=lambda i: (-(start[i] + ops[i]["dur"]), -i)), back, final)
+        return place(sorted(range(nops), key=lambda i: (-(rev[i] + ops[i]["dur"]), i)), fore, first)
+
+    start = place(sorted(range(nops), key=lambda i: (-prio[i], i)), fore, first)
     best = start
     for _ in range(M["rounds"]):
-        rev = place(sorted(range(nops), key=lambda i: (-(start[i] + ops[i]["dur"]), -i)), succ, True)
-        start = place(sorted(range(nops), key=lambda i: (-(rev[i] + ops[i]["dur"]), i)), pred, False)
+        start = both_ways(start)
         if length(start) < length(best):
             best = start
-    rng = np.random.default_rng(M["seed"])
-    blen = length(best)
-    for it in range(M["tries"]):
-        key = list(best)
-        lo = rng.random() * blen
-        noise = rng.random(nops) * (300.0, 800.0, 2000.0)[it % 3]
-        for i in range(nops):
-            k = key[i] - (float(noise[i]) if lo <= key[i] <= lo + 12000.0 else 0.0)
-            for j in pred[i]:
-                if key[j] >= k:
-                    k = key[j] + 0.001
-            key[i] = k
-        start = place(sorted(range(nops), key=lambda i: (key[i], i)), pred, False)
-        if it % 4 == 3:
-            rev = place(sorted(range(nops), key=lambda i: (-(start[i] + ops[i]["dur"]), -i)), succ, True)
-            start = place(sorted(range(nops), key=lambda i: (-(rev[i] + ops[i]["dur"]), i)), pred, False)
-        if length(start) <= blen:
-            best, blen = start, length(start)
-    order = sorted(range(nops), key=lambda i: (best[i], i))
-    return order, pred, best
+    return improve(ops, pred, succ, fore, first, final, sorted(range(nops), key=lambda i: (best[i], i)))
+
+
+def improve(ops, pred, succ, fore, first, final, seq):
+    nops = len(ops)
+    names = sorted(set(o["eng"] for o in ops))
+    eng = [names.index(o["eng"]) for o in ops]
+    dur = [o["dur"] for o in ops]
+
+    def play(seq):
+        at, free, prev, last = [0.0] * nops, [0.0] * len(names), [-1] * nops, [-1] * len(names)
+        for i in seq:
+            e = eng[i]
+            s = free[e] if free[e] > first[i] else first[i]
+            for j, d in fore[i]:
+                if at[j] + d > s:
+                    s = at[j] + d
+            at[i], free[e], prev[i], last[e] = s, s + dur[i], last[e], i
+        end = max(range(nops), key=lambda i: at[i] + dur[i] + final[i])
+        return at, prev, end, at[end] + dur[end] + final[end] + M["mean"] * sum(at) / nops
+
+    at, prev, end, cost = play(seq)
+    top, held = (cost, seq, at), None
+    for it, r in enumerate(np.random.default_rng(M["seed"]).random((M["tries"], 6)).tolist()):
+        if held is None:
+            held, i = [], end
+            while True:
+                c = [j for j, d in fore[i] if at[j] + d >= at[i] - 0.5]
+                p = prev[i]
+                if p >= 0 and at[p] + dur[p] >= at[i] - 0.5 and p not in pred[i]:
+                    held.append(i)
+                    c.append(p)
+                if not c:
+                    break
+                i = c[int(r[0] * 997 + len(held)) % len(c)]
+            pos = {x: k for k, x in enumerate(seq)}
+        b = held[int(r[1] * len(held))] if r[2] < 0.6 and held else int(r[1] * nops)
+        a = prev[b]
+        for _ in range(int(r[3] ** 3 * 8)):
+            if a >= 0 and prev[a] >= 0:
+                a = prev[a]
+        if a < 0:
+            continue
+        part = seq[pos[a]:pos[b] + 1]
+        ahead = r[4] < 0.5
+        move = {b if ahead else a}
+        for x in (part[::-1] if ahead else part):
+            if x in move:
+                move.update(pred[x] if ahead else succ[x])
+        if a in move and b in move:
+            continue
+        part = [x for x in part if (x in move) == ahead] + [x for x in part if (x in move) != ahead]
+        new = seq[:pos[a]] + part + seq[pos[b] + 1:]
+        at2, prev2, end2, cost2 = play(new)
+        if cost2 <= cost - M["temp"] * (1.0 - it / M["tries"]) * math.log(r[5] + 1e-12):
+            seq = [new[k] for k in sorted(range(nops), key=lambda k: (at2[new[k]], k))]
+            at, prev, end, cost, held = at2, prev2, end2, cost2, None
+            if cost < top[0]:
+                top = (cost, seq, at)
+    return top[1], pred, top[2]
 
 
 PLAN = {}
@@ -585,9 +670,9 @@ def rank_program(g, core, T, topo):
     if rank is None:
         return
     ops = build(g, core, T, topo, rank)
-    if not PLAN:
-        PLAN["all ranks"] = schedule(ops)
-    order, pred, start = PLAN["all ranks"]
+    if len(ops) not in PLAN:
+        PLAN[len(ops)] = schedule(ops)
+    order, pred, start = PLAN[len(ops)]
     queue = {"pe": g.tensor, "dve": g.vector, "act": g.scalar, "pool": g, "sp": g.sync}
     know = {q: {} for q in queue}
     count = {"pe": 0, "dve": 0, "act": 0, "pool": 0}
@@ -601,6 +686,8 @@ def rank_program(g, core, T, topo):
             if pj["eng"] == q and q == "pe":
                 continue
             if pj["sem"] is not None and pj["sem"].startswith("lo"):
+                continue
+            if pj["eng"] == q == "pool" and "sent" in o["w"]:
                 continue
             need.append((done[j][0], done[j][1], j))
         need.sort(key=lambda x: -(start[x[2]] if x[2] is not None else -1.0))
@@ -619,9 +706,10 @@ def rank_program(g, core, T, topo):
             count[q] += len(o["calls"])
             done[i] = (q, count[q])
         else:
-            ins = o["calls"][0]()
-            if o["sem"].startswith("ld"):
-                ins.then_inc(T.sem[o["sem"]], 16)
+            for call in o["calls"]:
+                ins = call()
+                if not o["sem"].startswith("lo"):
+                    ins.then_inc(T.sem[o["sem"]], 16)
             done[i] = (o["sem"], o["inc"])
         total[done[i][0]] = done[i][1]
         for e in o["ext"]:

@@ -11,6 +11,9 @@ BIG = 1.5 * 2.0 ** 32
 BIG1 = 1.5 * 2.0 ** 23
 LOW = math.log(1.0 / 8191)
 SHIFT = 16.0
+BIG2 = 1.5 * 2.0 ** 34
+MID = 1023.5
+STEP = 4096.0
 
 
 def _sb(cols, dtype, rows=128):
@@ -22,15 +25,16 @@ SCRATCH = {
     "g0": _sb(2064, BF), "g1": _sb(2064, BF), "g2": _sb(2064, BF), "g3": _sb(W, BF),
     "xm": _sb(2064, BF), "xt": _sb(2064, BF), "gt": _sb(2064, BF),
     "ga0": _sb(W, BF), "ga1": _sb(W, BF), "ms0": _sb(W, BF), "ms1": _sb(W, BF),
-    "xg": _sb(W, BF), "ab": _sb(W, F32), "zz": _sb(W, F32), "za": _sb(W, F32), "zs": _sb(1024, F32),
-    "oha": _sb(4096, BF), "ohb": _sb(4096, BF), "qa": _sb(512, BF), "qb": _sb(1024, BF), "fc": _sb(1152, F16),
+    "xg": _sb(W, BF), "xl": _sb(W, BF), "ab": _sb(W, F32), "al": _sb(W, F32),
+    "zz": _sb(W, F32), "za": _sb(W, F32), "zb": _sb(W, F32), "zc": _sb(W, F32), "zs": _sb(W, F32),
+    "oha": _sb(4096, BF), "ohb": _sb(4096, BF), "qa": _sb(512, BF), "qb": _sb(576, BF), "less": _sb(512, BF, 8), "fc": _sb(1152, F16),
     "ivi": _sb(C, I32), "pfi": _sb(C, I32), "ivh": _sb(C, F16), "pff": _sb(C, F32),
     "taui": _sb(512, I32, 8), "tauh": _sb(512, F16, 8),
-    "ti": _sb(C, I32), "t0i": _sb(C, I32), "t0h": _sb(C, F16), "off0": _sb(C, U16), "off1": _sb(C, U16),
+    "tr": _sb(C, BF), "t0f": _sb(C, F16), "off0": _sb(C, U16), "off1": _sb(C, U16),
     "tc": _sb(C, F32), "on": _sb(C, BF), "idv": _sb(C, BF), "ki": _sb(C, I32), "hii": _sb(C, I32), "loi": _sb(C, I32),
     "po0": _sb(C, U16), "po1": _sb(C, U16), "thr": _sb(C, F32),
-    "rr": _sb(80, F16), "ff": _sb(80, F16), "mt": _sb(4 * C, BF), "si": _sb(3 * C, BF), "vc": _sb(C, BF),
-    "nak": _sb(C, BF), "lt": _sb(C, BF), "lv": _sb(C, BF), "jj": _sb(C, F16), "im": _sb(C, I32), "tj": _sb(C, I32),
+    "rr": _sb(160, F16), "ff": _sb(160, F16), "mt": _sb(4 * C, BF), "si": _sb(4 * C, BF),
+    "nak": _sb(C, BF), "lt": _sb(C, BF), "lv": _sb(C, BF), "jj": _sb(C, F16),
     "ru": _sb(C, F32), "dn": _sb(C, I32), "q0": _sb(2 * C, BF), "q1": _sb(2 * C, BF), "yo": _sb(C, F32),
     "onf": _sb(256, F32), "idw": _sb(256, F32), "id1": _sb(C, BF), "idc": _sb(C, BF), "id2": _sb(C, BF), "id64": _sb(C, BF),
     "idn": _sb(C, BF), "id8p": _sb(C, BF), "id8n": _sb(C, BF),
@@ -39,20 +43,21 @@ SCRATCH = {
     "blk": _sb(144, BF), "tri": _sb(144, BF), "ntri": _sb(144, BF), "c1": _sb(144, BF), "c3": _sb(C, BF), "c4": _sb(C, BF),
     "c5": _sb(C, BF), "c7": _sb(C, F32), "blk18": _sb(C, BF), "blk16": _sb(C, BF),
     "tx": _sb(C, BF), "tz": _sb(C, BF), "tq": _sb(2 * C, BF), "sh": _sb(C, BF), "dm": _sb(C, BF), "bo8": _sb(8, BF),
-    "j16": _sb(512, BF), "rep": _sb(1024, BF), "rep8": _sb(C, BF, 8), "rep80": _sb(C, BF, 8),
+    "j16": _sb(512, BF), "sx": _sb(512, BF), "rep": _sb(1024, BF), "rep8": _sb(C, BF, 8), "rep80": _sb(C, BF, 8),
     "ones": _sb(512, BF), "fl": _sb(C, BF, 8), "selx": _sb(W, BF), "km": _sb(512, BF),
     "rt": _sb(1152, BF), "qt": _sb(1152, BF), "ll": _sb(1152, BF), "ft": _sb(1296, BF),
     "B0": ("psum", [128, 512], F32), "B1": ("psum", [128, 512], F32), "B2": ("psum", [128, 512], F32),
     "B3": ("psum", [128, 512], F32), "S0": ("psum", [128, 512], F32), "S1": ("psum", [128, 512], F32),
     "S2": ("psum", [128, 512], F32), "SY": ("psum", [128, 512], F32),
 }
-SEMAPHORES = (["pe", "dve", "act", "pool", "za1", "za2"] + ["ld%d" % i for i in range(16)] + ["ax1", "ax2", "ax3", "ag1", "ag2", "ag3",
+SEMAPHORES = (["pe", "dve", "act", "pool", "za10", "za11", "za20", "za21"] + ["ld%d" % i for i in range(16)] + ["ax1", "ax2", "ax3", "ag1", "ag2", "ag3",
               "as1", "as2", "as3"] + ["lo%d" % i for i in range(12)])
 BANKS = ("B0", "B1", "B2", "B3", "S0", "S1", "S2", "SY")
-M = {"cy": 0.85, "pe": 0.43, "hop": 70.0, "gc": 1.56, "vo": 30.0, "ao": 65.0, "po": 5.0, "sil": 3500.0, "x1": 15000.0,
-     "bulk": 11000.0, "add": 6000.0, "rounds": 2, "tries": 60000, "seed": 1, "temp": 50.0, "mean": 0.5}
-CFG = {"hear": "adaaaaaa", "xt": "dada", "xg": "adad", "xm": "aaaa", "xgl": "dada", "gt": "adad", "qb": 8,
-       "bh": "01230123", "bt": "b0c1", "bm": "2301", "bz": "yyyy", "bzl": "2323", "bg": "0b1c"}
+M = {"cy": 0.9, "pe": 0.45, "hop": 110.0, "gc": 1.56, "vo": 35.0, "ao": 70.0, "po": 4.0, "sil": 3500.0, "x1": 17000.0,
+     "bulk": {"x": 15000.0, "g": 13500.0, 1: 11000.0, 2: 11000.0}, "add": 5500.0,
+     "rounds": 2, "tries": 200000, "seed": 1, "temp": 60.0, "mean": 0.3, "slow": (1.15, 1.7), "weight": 0.5}
+CFG = {"hear": "adaaaaaa", "xt": "dada", "xg": "adad", "xgl": "dada", "scan": 2, "qb": 8, "step": "",
+       "bh": "01230123", "bt": "b0c1", "bm": "2301", "bq": "2", "bz": "yyy3", "bg": "0b1c"}
 BANK = dict(zip("0123abcy", BANKS))
 
 
@@ -117,6 +122,12 @@ def build(g, core, T, topo, rank):
     def act(out, a, f, r, w, n_, c=1.0, bias=0.0, scale=1.0, extra=0.0):
         op("act", [lambda: g.scalar.activation(out, a, f, bias=bias, scale=scale)], r, w, n_ * c * CY + M["ao"] + extra)
 
+    def below(name, out, a, lim, steep, r):
+        if name in CFG["step"]:
+            act(out, a, AF.Sigmoid, r, [name], C, bias=steep * lim, scale=-steep)
+        else:
+            ts(out, a, lim, None, A.is_lt, None, r, [name], C)
+
     def one_mm(m):
         return lambda: g.tensor.matmul(m[0], m[1], m[2], m[3], m[4])
 
@@ -148,22 +159,26 @@ def build(g, core, T, topo, rank):
 
     nlo = [0]
 
-    def send(items, r, w, lat, ext=()):
-        trs, inc = [], 0
-        for dst_rank, out, srcs, sem in items:
-            d = T.cores[dst_rank % n]
-            e = engines(core, d)
-            rid, pid = topo.addr(d, core)
-            trs.append(RemoteDMATransfer(dst_ids=[DstId(rid=rid, pnc=pid)], dma_engine_mask=sum(1 << x for x in e),
-                                         remote_sem=T.sem[sem], srcs=srcs, dsts=[out], alu_op=1 if len(srcs) > 1 else 0))
-            inc += len(e)
-        s = "lo%d" % nlo[0]
+    def fused(trs, s):
+        return lambda: g.remote_dma_fused(trs, local_sem=T.sem[s])
+
+    def send(groups, r, w, dur, lat, ext=()):
+        s, calls, inc = "lo%d" % nlo[0], [], 0
         nlo[0] += 1
-        op("pool", [lambda: g.remote_dma_fused(trs, local_sem=T.sem[s])], r, w, 1000.0, sem=s, inc=inc, lat=lat, ext=ext)
+        for items in groups:
+            trs = []
+            for dst_rank, out, src, sem in items:
+                d = T.cores[dst_rank % n]
+                e = engines(core, d)
+                rid, pid = topo.addr(d, core)
+                trs.append(RemoteDMATransfer(dst_ids=[DstId(rid=rid, pnc=pid)], dma_engine_mask=sum(1 << x for x in e),
+                                             remote_sem=T.sem[sem], src=src, dst=out))
+                inc += len(e)
+            calls.append(fused(trs, s))
+        op("pool", calls, r, w, dur, sem=s, inc=inc, lat=lat, ext=ext)
 
     X = [T.x0, T.x1, T.x2, T.x3]
     G = [T.g0, T.g1, T.g2, T.g3]
-    B = [T.B0, T.B1, T.B2, T.B3]
     ident = T.idw[:, 0:C]
     ways = routes(topo, T.cores)
     sender = {d: h for s, d, h in ways if (s - d) % n == rank}
@@ -172,15 +187,17 @@ def build(g, core, T, topo, rank):
     AS = [None] + [("as%d" % t, len(engines(T.cores[(rank + 1) % n], core))) for t in range(1, VI)]
     quiet = near(topo, core, T.cores[(rank - 1) % n])
 
-    def bulk(window):
-        for name in "xg":
+    def bulk(window, names):
+        groups, ext = [], []
+        for name in names:
             for held in range(VI - 1):
                 mine = [(s, d) for s, d, h in ways if h == rank and (s - rank) % n == held]
                 when = (0 if name == "x" or quiet else 1) if held == 0 else (1 if name == "x" else 2)
                 if mine and when == window:
                     src = T["%s%d" % (name, held)][:, 0:W]
-                    send([(s - d, T["%s%d" % (name, d)][:, 0:W], [src], "a%s%d" % (name, d)) for s, d in mine],
-                         ["%s%d" % (name, held), "sent"], [], M["bulk"], [(AX if name == "x" else AG)[held]])
+                    groups.append([(s - d, T["%s%d" % (name, d)][:, 0:W], src, "a%s%d" % (name, d)) for s, d in mine])
+                    ext.append((AX if name == "x" else AG)[held])
+        send(groups, [name + "0" for name in names] + ["sent"], [], 1000.0 * len(names), M["bulk"][window if window else names], ext)
 
     dma("act", T.x0[:, 0:W], T.xs[:], [], ["x0"], 3300)
     dma("sp", T.ivi[:], T.iv[:], [], ["ivi"], 2200)
@@ -191,18 +208,21 @@ def build(g, core, T, topo, rank):
         dma("sp", T.taui[:, t * C:t * C + 64], T.tau[:, 0:64], [], ["taui%da" % t], 2000)
         dma("sp", T.taui[t:8, t * C + 64:t * C + C], T.tau[0:8 - t, 64:C], [], ["taui%db" % t], 2000)
         dma("sp", T.taui[0:t, t * C + 64:t * C + C], T.tau[8 - t:8, 64:C], [], ["taui%dc" % t], 2000)
-    bulk(0)
+    bulk(0, "x")
+    bulk(0, "g")
     MT = [T.mt[:, C * t:C * t + C] for t in range(VI)]
-    SI = [None] + [T.si[:, C * t:C * t + C] for t in range(3)]
+    SI = [T.si[:, C * t:C * t + C] for t in range(VI)]
 
     iota(T.pvi[:], [[1, 1]], 0, 1, ["pvi"], 1)
     iota(T.jr[:], [[1, 160]], 96, 0, ["jr"], 160)
     iota(T.j16[:], [[1, 32], [0, 16]], 0, 0, ["j16"], 512, True)
+    iota(T.less[:], [[-2, 8], [0, 64]], 0, 0, ["less"], 512, True)
+    iota(T.sx[:], [[1, 4], [16, 8], [0, 16]], 0, -1, ["sx"], 512, True)
     ms(T.ones[:], 1.0, ["ones"], 512)
     ms(T.onf[:], 1.0, ["onf"], 512)
     sel(T.idw[:], T.onf, "onf", [[0, 2], [-1, C]], 0, ["idw"], 256)
     act(T.id1[:], ident, AF.Sigmoid, ["idw"], ["id1"], C, bias=-200.0, scale=400.0, extra=1300.0)
-    for name, s in (("idc", 32 * CS), ("id64", 64.0), ("idn", -1.0), ("id8p", 8192.0), ("id8n", -8192.0), ("id2", 2.0), ("idv", V)):
+    for name, s in (("idc", 32 * CS), ("id64", 64.0), ("idn", -1.0), ("id8p", 8192.0), ("id8n", -8192.0), ("id2", 2.0), ("idv", -V)):
         act(T[name][:], ident, AF.Identity, ["idw"], [name], C, scale=s)
     ts(T.pw[:, 0:1], T.pvi[:], 112, None, A.bitwise_and, None, ["pvi"], ["pw0"], 1)
     ts(T.pw[:, 1:2], T.pvi[:], 15, None, A.bitwise_and, None, ["pvi"], ["pw1"], 1)
@@ -211,10 +231,12 @@ def build(g, core, T, topo, rank):
     cp(pp, T.pvi[:], ["pvi"], ["pp"], 1)
     ts(p16, T.pvi[:], 16.0, None, A.mult, None, ["pvi"], ["p16"], 1)
     cp(pg, T.pw[:, 0:1], ["pw0"], ["pg"], 1)
-    ts(pl, T.pw[:, 1:2], 14.5, -0.5, A.is_lt, A.add, ["pw1"], ["pl"], 1)
-    ts(pk, T.pw[:, 1:2], 2048.0, None, A.mult, None, ["pw1"], ["pk"], 1)
-    ts(pn, T.pw[:, 1:2], -2048.0, None, A.mult, None, ["pw1"], ["pn"], 1)
-    ts(pr, T.pw[:, 1:2], -2048.0, 32768.0, A.mult, A.add, ["pw1"], ["pr"], 1)
+    sg = -1.0 if "lv" in CFG["step"] else 1.0
+    ts(T.pc[:, 9:10], T.pw[:, 1:2], 14.5, 400.0 * sg, A.is_lt, A.mult, ["pw1"], ["pl0"], 1)
+    ts(pl, T.pc[:, 9:10], -200.0 * sg, None, A.add, None, ["pl0"], ["pl"], 1)
+    ts(pk, T.pw[:, 1:2], STEP, None, A.mult, None, ["pw1"], ["pk"], 1)
+    ts(pn, T.pw[:, 1:2], -STEP, None, A.mult, None, ["pw1"], ["pn"], 1)
+    ts(pr, T.pw[:, 1:2], -STEP, 16 * STEP, A.mult, A.add, ["pw1"], ["pr"], 1)
     cp(pa, T.pw[:, 2:3], ["pw2"], ["pa"], 1)
     ts(pb, T.pw[:, 2:3], -32.0, None, A.add, None, ["pw2"], ["pb"], 1)
     ts(T.jm[:], T.jr[:], 127, None, A.bitwise_and, None, ["jr"], ["jm"], 160)
@@ -228,16 +250,16 @@ def build(g, core, T, topo, rank):
     for b, (col, key) in enumerate(((pa, "pa"), (pb, "pb"))):
         ts(T.rep[:, 512 * b:512 * b + 512], T.j16[:], col, -CS, A.is_equal, A.mult, ["j16", key], ["rep%d" % b], 512, 0.5)
     for b in range(4):
-        sel(T.selx[:, 512 * b:512 * b + 512], T.ones, "ones", [[-1, 4], [-16, 8], [0, 16]], -4 * b, ["selx%d" % b], 512)
+        ts(T.selx[:, 512 * b:512 * b + 512], T.sx[:], -4.0 * b, V, A.is_equal, A.mult, ["sx"], ["selx%d" % b], 512, 0.5)
     ts(T.gxb[:], T.jm[:], pg, 2.0 ** -13, A.is_equal, A.mult, ["jm", "pg"], ["gxb"], 160)
     blk = T.blk[:, 16:144]
     act(T.ntri[:], T.tri[:], AF.Identity, ["tri"], ["ntri"], 144, scale=-1.0)
     act(T.blk18[:], blk, AF.Identity, ["blk"], ["blk18"], C, scale=2 * V)
     act(T.blk16[:], blk, AF.Identity, ["blk"], ["blk16"], C, scale=1.0 / 16)
     tt(T.c3[:], blk, T.tri[:, 16:144], A.subtract, ["tri", "blk"], ["c3"], C)
-    act(T.tx[:], T.c3[:], AF.Identity, ["c3"], ["tx"], C, scale=2048.0)
+    act(T.tx[:], T.c3[:], AF.Identity, ["c3"], ["tx"], C, scale=STEP)
     tt(T.c4[:], T.c3[:], blk, A.add, ["c3", "blk"], ["c4"], C)
-    act(T.tz[:], T.c4[:], AF.Identity, ["c4"], ["tz"], C, scale=-2048.0)
+    act(T.tz[:], T.c4[:], AF.Identity, ["c4"], ["tz"], C, scale=-STEP)
     ms(T.tq[:], 0.0, ["tq"], 2 * C)
     last_rows = T.blk[:, 31:144:16]
     ts(T.tx[:, 15:C:16], last_rows, pn, None, A.mult, None, ["blk", "pn"], ["tx"], 8)
@@ -248,10 +270,10 @@ def build(g, core, T, topo, rank):
     sel(T.sh[:], T.c5, "c5", [[0, 8], [-1, 16]], 15, ["sh"], C, A.is_gt, 0)
     sel(T.c7[:], T.idw, "idw", [[0, 8], [1, 16]], 0, ["c7"], C, A.is_gt, 0, C - 1)
     tt(T.dm[:], ident, T.c7[:], A.subtract, ["idw", "c7"], ["dm"], C)
-    ms(T.rr[:], 0.0, ["rr0", "rr1"], 80)
-    ms(T.ff[:], 0.0, ["ff0", "ff1"], 80)
-    ms(T.vc[:], V, ["vc"], C)
+    ms(T.rr[:], 0.0, ["rr0", "rr1"], 160)
+    ms(T.ff[:], 0.0, ["ff0", "ff1"], 160)
     ms(T.fl[:], -15.0 / 256, ["fl"], C)
+    ms(SI[0], 1.0, ["si0"], C)
     ms(T.xt[:, W:2064], -V, ["xtc"], 16)
     ms(T.gt[:, W:2064], 0.0, ["gtc"], 16)
     for t in range(VI - 1):
@@ -270,20 +292,20 @@ def build(g, core, T, topo, rank):
     for j, (t0, t1) in enumerate(PARTS):
         keys = [a + "%d" % x for t in range(t0, t1) for x in tk[t] for a in ("rt", "qt")] + ["rtz", "qtz"]
         nn = C * (t1 - t0)
-        u = 0 if j == 0 else C
-        mm([(B[j][:, 0:nn], (T.tx if j == 0 else T.tz)[:], T.rt[:, C * t0:C * t1], True, False),
-            (B[j][:, 0:nn], T.tq[:, u:u + C], T.qt[:, C * t0:C * t1], False, True)], keys + ["tx", "tz", "tq"], ["B%d" % j], 2 * nn)
-        act(T.ll[:, C * t0:C * t1], B[j][:, 0:nn], AF.Copy, ["B%d" % j], ["ll%d" % j], nn)
+        u, bk = 0 if j == 0 else C, ("B2", "B3")[j % 2]
+        mm([(T[bk][:, 0:nn], (T.tx if j == 0 else T.tz)[:], T.rt[:, C * t0:C * t1], True, False),
+            (T[bk][:, 0:nn], T.tq[:, u:u + C], T.qt[:, C * t0:C * t1], False, True)], keys + ["tx", "tz", "tq"], [bk], 2 * nn)
+        act(T.ll[:, C * t0:C * t1], T[bk][:, 0:nn], AF.Copy, [bk], ["ll%d" % j], nn)
     for j in range(3):
-        lst = []
+        lst, bk = [], ("B3", "B2")[j % 2]
         for t in range(3 * j, 3 * j + 3):
-            o = B[j][:, 144 * (t % 3):144 * (t % 3) + 144]
+            o = T[bk][:, 144 * (t % 3):144 * (t % 3) + 144]
             lst.append((o, T.qt[:, C * t:C * t + C], T.tri[:], True, t >= 4))
             if t < 4:
                 lst.append((o, T.rt[:, C * t:C * t + C], T.ntri[:], False, True))
         mm(lst, [a + "%d" % x for t in range(3 * j, 3 * j + 3) for x in tk[t] for a in ("rt", "qt")] + ["qtz", "tri", "ntri"],
-           ["B%d" % j], 144 * len(lst))
-        act(T.ft[:, 432 * j:432 * j + 432], B[j][:, 0:432], AF.Copy, ["B%d" % j], ["ft%d" % j], 432)
+           [bk], 144 * len(lst))
+        act(T.ft[:, 432 * j:432 * j + 432], T[bk][:, 0:432], AF.Copy, [bk], ["ft%d" % j], 432)
     late = ops[late_from:]
     del ops[late_from:]
 
@@ -302,30 +324,22 @@ def build(g, core, T, topo, rank):
            [k + "ab"[h], k + "cd"[h], "rep%d" % (b % 2)], [bk], 512)
 
     def times(t):
-        cp(T.ti[:], T.S2[:, 0:C], ["S2"], ["ti"], C)
-        ts(T.t0i[:], T.ti[:], W - 1, None, A.bitwise_and, None, ["ti"], ["t0i"], C)
-        cp(T.off0[:], T.t0i[:], ["t0i"], ["off0"], C)
-        ts(T.off1[:], T.t0i[:], 1.0, None, A.add, None, ["t0i"], ["off1"], C)
-        cp(T.t0h[:], T.t0i[:], ["t0i"], ["t0h"], C)
-        if 0 < t < VI - 1:
-            mm([(T.S2[:, 0:C], T.dm[:], T.t0h[:], True, False),
-                (T.S2[:, 0:C], T.rep80[:], T.tauh[:, t * C:t * C + C], False, True)], ["t0h", "dm", "rep80", "tauhr"], ["S2"], 2 * C)
-            cp(T.tj[:], T.S2[:, 0:C], ["S2"], ["tj"], C)
-            ts(T.im[:], T.tj[:], W - 1, None, A.bitwise_and, None, ["tj"], ["im"], C)
+        ts(T.tr[:], T.S2[:, 0:C], BIG2, -BIG2, A.add, A.add, ["S2"], ["tr"], C)
+        tt(T.t0f[:], T.S2[:, 0:C], T.tr[:], A.subtract, ["S2", "tr"], ["t0f"], C, 1.0)
+        ts(T.off0[:], T.t0f[:], MID, None, A.add, None, ["t0f"], ["off0"], C)
+        ts(T.off1[:], T.t0f[:], MID + 1, None, A.add, None, ["t0f"], ["off1"], C)
 
-    def table(eng, out, okey, src, skey, sext, msk, mkey, mext, b, bank, clip=False, t0=0.0):
+    def table(eng, out, okey, src, skey, sext, msk, mkey, mext, b, bank, how=A.subtract, t0=0.0, plus=0.0):
         s, bk = slice(512 * b, 512 * b + 512), BANK[bank]
-        with_x = eng == "a" or clip
+        with_x = eng == "a"
         if with_x:
-            mm([(T[bk][:], T.id1[:], src[:, s], True, False)], [skey, "id1"], [bk], 512, [sext], t0)
+            mm([(T[bk][:], T.idn[:], src[:, s], True, False)], [skey, "idn"], [bk], 512, [sext], t0)
         mm([(T[bk][:, C * j:C * j + C], T.selx[:, C * (4 * b + j):C * (4 * b + j) + C], msk, not with_x, (not with_x) or j == 3)
             for j in range(4)], [mkey, "selx%d" % b], [bk], 512, [mext])
         if eng == "a":
-            act(out[:, s], T[bk][:], AF.Relu if clip else AF.Copy, [bk], [okey + "%d" % b], 512)
-        elif clip:
-            ts(out[:, s], T[bk][:], 0.0, None, A.max, None, [bk], [okey + "%d" % b], 512)
+            act(out[:, s], T[bk][:], AF.Identity, [bk], [okey + "%d" % b], 512, bias=plus, scale=-1.0)
         else:
-            tt(out[:, s], src[:, s], T[bk][:], A.add, [skey, bk], [okey + "%d" % b], 512, 1.0, ext=[sext])
+            tt(out[:, s], src[:, s], T[bk][:], how, [skey, bk], [okey + "%d" % b], 512, 1.0, ext=[sext])
 
     def gather(eng, out, win, off, r, w):
         if eng == "a":
@@ -334,25 +348,27 @@ def build(g, core, T, topo, rank):
             cp(out, win.indirect(off), r, w, 512, M["gc"])
 
     def weights(t):
+        xg, ab = ("xg", "ab") if t < VI - 1 else ("xl", "al")
         for b in range(4):
-            s, bk = slice(512 * b, 512 * b + 512), BANK[CFG["bz" if t < VI - 1 else "bzl"][b]]
+            s, bk = slice(512 * b, 512 * b + 512), BANK[CFG["bz"][t]]
             minus_d(t, b, bk)
-            mm([(T[bk][:], T.idc[:], T.xg[:, s], False, True)], ["xg%d" % b, "idc"], [bk], 512)
-            act(T.ab[:, s], T[bk][:], AF.Abs, [bk], ["ab%d" % b], 512)
-            act(T.ab[:, s], T.ab[:, s], AF.Sigmoid, ["ab%d" % b], ["ab%d" % b], 512, bias=-SHIFT, scale=-1.0 / (256 * CS))
+            mm([(T[bk][:], T.idc[:], T[xg][:, s], False, True)], [xg + "%d" % b, "idc"], [bk], 512)
+            act(T[ab][:, s], T[bk][:], AF.Abs, [bk], [ab + "%d" % b], 512)
+            act(T[ab][:, s], T[ab][:, s], AF.Sigmoid, [ab + "%d" % b], [ab + "%d" % b], 512,
+                bias=-SHIFT - (math.log(V) if t == VI - 1 else 0.0), scale=-1.0 / (256 * CS))
 
     def terms(t, win, keys):
-        po = "po%d" % (t % 2)
-        z, zk = (T.za, "za") if t == 0 else (T.zz, "zz")
+        po, ab, zk = "po%d" % (t % 2), "ab" if t < VI - 1 else "al", ("za", "zb", "zc", "zz")[t]
         for b in range(4):
             s = slice(512 * b, 512 * b + 512)
-            tt(z[:, s], win[:, 0:2064].indirect(T[po][:, 32 * b:32 * b + 32]), T.ab[:, s], A.mult,
-               ["ab%d" % b, po] + keys, [zk + "%d" % b], 512, M["gc"], ext=[AG[t]])
+            tt(T[zk][:, s], win[:, 0:2064].indirect(T[po][:, 32 * b:32 * b + 32]), T[ab][:, s], A.mult,
+               [ab + "%d" % b, po] + keys, [zk + "%d" % b], 512, M["gc"], ext=[AG[t]])
         if 0 < t < VI - 1:
             u = 16 * t
-            pairs = ((T.za[:, 0:1024], T.zz[:, 0:1024]), (T.za[0:C - u, 1024:W], T.zz[u:C, 1024:W]), (T.za[C - u:C, 1024:W], T.zz[0:u, 1024:W]))
-            op("pool", [add_dma(o, a) for o, a in pairs], ["zz%d" % b for b in range(4)], ["za%d" % b for b in range(4)],
-               3000.0, sem="za%d" % t, inc=48, lat=M["add"])
+            pairs = ((T.za[:, 0:1024], T[zk][:, 0:1024]), (T.za[0:C - u, 1024:W], T[zk][u:C, 1024:W]), (T.za[C - u:C, 1024:W], T[zk][0:u, 1024:W]))
+            for h, part in enumerate((pairs[:1], pairs[1:])):
+                op("pool", [add_dma(o, a) for o, a in part], [zk + "%d" % (2 * h), zk + "%d" % (2 * h + 1)], ["za%d" % (2 * h), "za%d" % (2 * h + 1)],
+                   1000.0 * len(part), sem="za%d%d" % (t, h), inc=16 * len(part), lat=M["add"])
 
     def add_dma(out, a):
         return lambda: g.dma_start(out, a, accum_op=A.add)
@@ -361,7 +377,7 @@ def build(g, core, T, topo, rank):
         return lambda: g.vector.tensor_tensor_scan(out, T.km[:], data, 0.0, A.mult, A.add)
 
     cp(T.ivh[:], T.ivi[:], ["ivi"], ["ivh"], C)
-    cp(T.tauh[:, 0:C], T.taui[:, 0:C], ["taui0"], ["tauh0"], C)
+    ts(T.tauh[:, 0:C], T.taui[:, 0:C], -MID, None, A.add, None, ["taui0"], ["tauh0"], C)
     mm([(T.S2[:, 0:C], T.tri[:, 16:144], T.ivh[:], True, False), (T.S2[:, 0:C], T.rep8[:], T.tauh[:, 0:C], False, True)],
        ["tri", "ivh", "rep8", "tauh0"], ["S2"], 2 * C)
     cp(T.pff[:], T.pfi[:], ["pfi"], ["pff"], C)
@@ -369,7 +385,7 @@ def build(g, core, T, topo, rank):
     cp(T.dn[:], T.S0[:, 0:C], ["S0"], ["dn0", "dn1", "dn2"], C)
     parts(0)
     act(T.x0[:, W:W + 1], T.x0[:, 0:1], AF.Copy, ["x0"], ["x0c"], 1)
-    cp(T.tauh[:, C:4 * C], T.taui[:, C:4 * C], ["taui%d%s" % (t, s) for t in (1, 2, 3) for s in "abc"], ["tauhr"], 3 * C)
+    ts(T.tauh[:, C:4 * C], T.taui[:, C:4 * C], -MID, None, A.add, None, ["taui%d%s" % (t, s) for t in (1, 2, 3) for s in "abc"], ["tauhr"], 3 * C)
     times(0)
 
     GA, MS, OFF = [T.ga0, T.ga1], [T.ms0, T.ms1], [T.off0, T.off1]
@@ -381,10 +397,9 @@ def build(g, core, T, topo, rank):
         xkeys = ["x0", "x0c"] if t == 0 else ["xm0", "xm1", "xm2", "xm3", "xmc"]
         for e in range(2):
             for b in range(4):
-                s = slice(512 * b, 512 * b + 512)
+                s, bk = slice(512 * b, 512 * b + 512), BANK[CFG["bh"][4 * e + b]]
                 gather(CFG["hear"][4 * e + b], GA[e][:, s], xw[:, 0:W + 1], OFF[e][:, 32 * b:32 * b + 32], xkeys + ["off%d" % e],
                        ["ga%d%d" % (e, b)])
-                bk = BANK[CFG["bh"][4 * e + b]]
                 minus_d(t, b, bk)
                 mm([(T[bk][:], T.idc[:], GA[e][:, s], False, True)], ["ga%d%d" % (e, b), "idc"], [bk], 512)
                 ts(MS[e][:, s], T[bk][:], BIG, BIG, A.add, A.not_equal, [bk], ["ms%d%d" % (e, b)], 512)
@@ -392,86 +407,92 @@ def build(g, core, T, topo, rank):
                 mm([(T.S0[:, C * e + k:C * e + C:16], MS[e][:, k:W:16], T.bo8[:], e == 0, e == 0 or k == 15)
                     for k in range(8 * q, 8 * q + 8)], ["ms%d%d" % (e, b) for b in range(4)] + ["bo8"], ["S0"], 512)
             if e == 0:
-                ts(T.on[:], T.S0[:, 0:C], 36864.0, -1.0, A.is_lt, A.mult, ["S0"], ["on"], C)
-                mm([(T.S1[:, 0:C], T.t0h[:], T.id1[:], True, False), (T.S1[:, 0:C], T.id1[:], T.on[:], False, True)],
-                   ["t0h", "id1", "on"], ["S1"], 2 * C)
-                act(T.tc[:], T.S1[:, 0:C], AF.Identity, ["S1"], ["tc"], C, bias=32769.0)
+                below("on", T.on[:], T.S0[:, 0:C], 36864.0, 0.05, ["S0"])
+                mm([(T.S1[:, 0:C], T.t0f[:], T.id1[:], True, False)], ["t0f", "id1"], ["S1"], C)
+                mm([(T.S1[:, 0:C], T.idn[:], T.on[:], False, True)], ["idn", "on"], ["S1"], C)
+                act(T.tc[:], T.S1[:, 0:C], AF.Identity, ["S1"], ["tc"], C, bias=32769.0 + MID)
                 mm([(T.S0[:, C:2 * C], T.idv[:], T.on[:], True, False)], ["idv", "on"], ["S0"], C)
+                if not last:
+                    mm([(T.S2[:, 0:C], T.on[:], T.id1[:], True, True)], ["id1", "on"], ["S2"], C)
+                    act(T.thr[:], T.S2[:, 0:C], AF.Copy, ["S2"], ["thr"], C)
         tt(T.ki[:], T.S0[:, C:2 * C], T.tc[:], A.max, ["S0", "tc"], ["ki"], C, 1.0)
         ts(T.loi[:], T.ki[:], 63, None, A.bitwise_and, None, ["ki"], ["loi"], C)
         ts(T.hii[:], T.ki[:], 6, 0xD9F, A.arith_shift_right, A.bitwise_and, ["ki"], ["hii"], C)
-        if t == 0:
-            ops.extend(late)
+        cp(T.qb[:, 0:C], T.loi[:], ["loi"], ["qb", "qc"], C)
         for h in range(2):
-            for name, src, step, reps in (("qb", "loi", 2.0, R), ("qa", "hii", 1.0, 4)):
-                c0, key = 64 * reps * h, "%s%d" % (name, h)
-                cp(T[name][:, c0:c0 + 64], T[src][:, 64 * h:64 * h + 64], [src], [key + "0", key], 64)
-                r = 1
-                while r < reps:
-                    ts(T[name][:, c0 + 64 * r:c0 + 128 * r], T[name][:, c0:c0 + 64 * r], -step * r, None, A.add, None,
-                       [key], [key], 64 * r, 0.5)
-                    r *= 2
+            bk = BANK[CFG["bq"]] if h == 0 else "qc"
+            if h == 0:
+                mm([(T[bk][:], T.ones[0:1, 0:C], T.less[0:1, :], True, False)], ["ones", "less"], [bk], 512)
+                mm([(T[bk][:, 64 * s:64 * s + 64], T.id1[:], T.qb[:, 0:64], False, s == 7) for s in range(8)], ["id1", "qb"], [bk], 512)
+            for r in (1, 2, 4)[:3 * h]:
+                ts(T.qb[:, 64 + 64 * r:64 + 128 * r], T.qb[:, 64:64 + 64 * r], -2.0 * r, None, A.add, None, ["qb", bk], [bk], 64 * r, 0.5)
+            c0, key = 256 * h, "qa%d" % h
+            cp(T.qa[:, c0:c0 + 64], T.hii[:, 64 * h:64 * h + 64], ["hii"], [key + "0", key], 64)
+            for r in (1, 2):
+                ts(T.qa[:, c0 + 64 * r:c0 + 128 * r], T.qa[:, c0:c0 + 64 * r], -1.0 * r, None, A.add, None, [key], [key], 64 * r, 0.5)
             for a in range(8):
                 c0 = 2048 * h + 256 * a
                 ts(T.oha[:, c0:c0 + 256], T.qa[:, 256 * h:256 * h + 256], 4.0 * a, None, A.is_equal, None,
                    ["qa%d" % h], ["oha%d_%d" % (h, a)], 256, 0.5)
             for b in range(32 // R):
                 c0 = 2048 * h + 64 * R * b
-                act(T.ohb[:, c0:c0 + 64 * R], T.qb[:, 64 * R * h:64 * R * (h + 1)], AF.Sigmoid, ["qb%d" % h, "id1"],
+                act(T.ohb[:, c0:c0 + 64 * R], T.qb[:, 64:576] if h else T[bk][:], AF.Sigmoid, [bk, "id1"],
                     ["ohb%d_%d" % (h, b)], 64 * R, bias=LOW - 200.0 * R * b, scale=100.0)
         lst = []
         for h in range(2):
             lst.append((T.S0[64 * h:64 * h + 64, 0:C], T.qa[:, 256 * h:256 * h + 64], T.id64[:], True, False))
-            lst.append((T.S0[64 * h:64 * h + 64, 0:C], T.qb[:, 64 * R * h:64 * R * h + 64], T.id1[:], False, True))
-        mm(lst, ["qa00", "qa10", "qb00", "qb10", "id64", "id1"], ["S0"], 4 * C)
+            lst.append((T.S0[64 * h:64 * h + 64, 0:C], T.qb[:, 64 * h:64 * h + 64], T.id1[:], False, True))
+        mm(lst, ["qa00", "qa10", "qb", "id64", "id1"], ["S0"], 4 * C)
         ts(T[po][:], T.S0[:, 0:C], 2048.0, None, A.min, None, ["S0"], [po], C)
         if last:
             for b in range(4):
-                gather(CFG["xgl"][b], T.xg[:, 512 * b:512 * b + 512], T.xm[:, 0:W + 1], T[po][:, 32 * b:32 * b + 32],
-                       xkeys + [po], ["xg%d" % b])
+                gather(CFG["xgl"][b], T.xl[:, 512 * b:512 * b + 512], T.xm[:, 0:W + 1], T[po][:, 32 * b:32 * b + 32],
+                       xkeys + [po], ["xl%d" % b])
             weights(t)
             for q in range(8):
                 mm([(T.SY[:, 0:C], ident, T.za[:, k:W:16], k == 0, False) for k in (2 * q, 2 * q + 1)],
                    ["za0", "za1", "za2", "za3", "idw"], ["SY"], 1024)
-        else:
-            tt(T.thr[:], T.S0[:, 0:C], T.t0h[:], A.is_equal, ["S0", "t0h"], ["thr"], C, 1.0)
+        if t == 0:
+            ops.extend(late)
         for h in range(2):
             H, hk = (T.S1, "S1") if h == 0 else (T.S2, "S2")
-            for u in range(4):
-                c0 = 2048 * h + 16 * u
-                mm([(H[32 * u:32 * u + 32, 0:32], T.oha[:, c0 + k:2048 * h + 2048:64], T.ohb[:, c0 + k:2048 * h + 2048:64],
-                     k == 0, k == 15) for k in range(16)],
-                   ["oha%d_%d" % (h, a) for a in range(8)] + ["ohb%d_%d" % (h, b) for b in range(32 // R)], [hk], 16 * 32)
-            c0 = 40 * h
-            ts(T.rr[:, c0:c0 + 32], H[:, 0:32], BIG1, -BIG1, A.add, A.add, [hk], ["rr%d" % h], 32)
-            tt(T.ff[:, c0:c0 + 32], H[:, 0:32], T.rr[:, c0:c0 + 32], A.subtract, [hk, "rr%d" % h], ["ff%d" % h], 32, 1.0)
+            for p in range(2):
+                c0 = 2048 * h + 16 * p
+                for q in range(2):
+                    mm([(H[64 * p:64 * p + 64, 0:64], T.oha[:, c0 + k:2048 * h + 2048:32], T.ohb[:, c0 + k:2048 * h + 2048:32],
+                         k == 0, k == 15) for k in range(8 * q, 8 * q + 8)],
+                       ["oha%d_%d" % (h, a) for a in range(8)] + ["ohb%d_%d" % (h, b) for b in range(32 // R)], [hk], 8 * 64)
+            c0 = 80 * h
+            ts(T.rr[:, c0:c0 + 64], H[:, 0:64], BIG1, -BIG1, A.add, A.add, [hk], ["rr%d" % h], 64)
+            tt(T.ff[:, c0:c0 + 64], H[:, 0:64], T.rr[:, c0:c0 + 64], A.subtract, [hk, "rr%d" % h], ["ff%d" % h], 64, 1.0)
             lst = []
-            for a in range(2):
-                even, odd = (T.S0[64 * h:64 * h + 64, C + 64 * a + p:C + 64 * a + 64:2] for p in range(2))
-                lst += [(even, T.id8p[:, a:C:2], T.ff[:, c0:c0 + 32], True, True),
-                        (odd, T.id1[:, a:C:2], T.rr[:, c0:c0 + 32], True, False),
-                        (odd, T.idn[:, a:C:2], T.rr[:, c0 + 1:c0 + 33], False, False),
-                        (odd, T.id8n[:, a:C:2], T.ff[:, c0 + 1:c0 + 33], False, True)]
+            for u in range(2):
+                here, on = slice(c0 + u, c0 + 64, 2), slice(c0 + u + 2, c0 + 66, 2)
+                for a in range(2):
+                    pick = slice(2 * a + u, C, 4)
+                    even, odd = (T.S0[64 * h + 32 * u:64 * h + 32 * u + 32, C + 64 * a + p:C + 64 * a + 64:2] for p in range(2))
+                    lst += [(even, T.id8p[:, pick], T.ff[:, here], True, True), (odd, T.id1[:, pick], T.rr[:, here], True, False),
+                            (odd, T.idn[:, pick], T.rr[:, on], False, False),
+                            (odd, T.id8n[:, pick], T.ff[:, on], False, True)]
             mm(lst, ["rr%d" % h, "ff%d" % h, "id1", "idn", "id8p", "id8n"], ["S0"], 512)
         mk = "mt%d" % t
-        ts(MT[t], T.S0[:, C:2 * C], 1.0, -V, A.not_equal, A.mult, ["S0"], [mk], C)
+        tt(MT[t], T.S0[:, C:2 * C], SI[t], A.is_equal if last else A.not_equal, ["S0", "si%d" % t], [mk], C, 1.0, ext=[AS[t]])
         if last:
             for b in range(4):
-                table(CFG["gt"][b], T.gt, "gt", G[t], "g%d" % t, AG[t], MT[t], mk, None, b, CFG["bg"][b], True)
+                table("d", T.gt, "gt", G[t], "g%d" % t, AG[t], MT[t], mk, None, b, CFG["bg"][b], A.mult)
             terms(t, T.gt, ["gt0", "gt1", "gt2", "gt3", "gtc"])
-            w0 = 16 * t
-            for q in range(4):
+            for q in range(4 if CFG["scan"] == 2 else 0):
                 mm([(T.SY[:, 0:64], ident, T.zz[:, k:1024:16], False, False) for k in range(4 * q, 4 * q + 4)],
                    ["zz0", "zz1", "idw"], ["SY"], 1024)
-            for b in (2, 3):
-                zs = T.zs[:, 512 * (b - 2):512 * (b - 1)]
+            for b in range(4 - CFG["scan"], 4):
+                zs, w0 = T.zs[:, 512 * b:512 * b + 512], 16 * t * (b // 2)
                 op("dve", [scan(zs, T.zz[:, 512 * b:512 * b + 512])], ["km", "zz%d" % b], ["zs%d" % b], vd(512, 1.0))
-                mm([(T.SY[:, 32 * b:32 * b + 32], T.idw[:, w0:w0 + C], T.zs[:, 512 * (b - 2) + 15:512 * (b - 1):16], False, b == 3)],
+                mm([(T.SY[:, 32 * b:32 * b + 32], T.idw[:, w0:w0 + C], T.zs[:, 512 * b + 15:512 * b + 512:16], False, b == 3)],
                    ["zs%d" % b, "idw"], ["SY"], 256)
             break
-        send([(rank - 1, SI[t + 1], [MT[t], T.vc[:]] + ([SI[t]] if t else []), "as%d" % (t + 1))],
-             [mk, "vc", "si%d" % t], ["si%d" % (t + 1), "sent"], M["sil"], [AS[t]])
-        bulk(t + 1)
+        send([[(rank - 1, SI[t + 1], MT[t], "as%d" % (t + 1))]], [mk], ["si%d" % (t + 1), "sent"], 1000.0, M["sil"])
+        if t < VI - 2:
+            bulk(t + 1, "xg")
         for b in range(4):
             table(CFG["xt"][b], T.xt, "xt", X[t], "x%d" % t, AX[t], MT[t], mk, None, b, CFG["bt"][b])
         for b in range(4):
@@ -483,12 +504,16 @@ def build(g, core, T, topo, rank):
                 for k in range(16)], xgk[2 * h:2 * h + 2] + ["gxb"], ["S0"], 1024)
         for q in range(4):
             mm([(T.SY[:, 0:C], T.xg[:, k:W:16], T.id2[:], k == 0, False) for k in range(4 * q, 4 * q + 4)], xgk + ["id2"], ["SY"], 512)
-        ts(T.nak[:], T.S0[:, 0:C], 0.0, None, A.is_le, None, ["S0"], ["nak"], C)
         tt(T.lt[:], T.S0[:, 0:C], T.thr[:], A.is_gt, ["S0", "thr"], ["lt"], C, 1.0)
-        ik = "ivi" if t == 0 else "im"
-        tt(T.jj[:], T.lt[:], T[ik][:], A.add, ["lt", ik], ["jj"], C)
+        below("nak", T.nak[:], T.S0[:, 0:C], -128.0, 1.0, ["S0"])
+        mm([(T.S1[:, 0:C], T.dm[:], T.t0f[:], True, False), (T.S1[:, 0:C], T.rep80[:], T.tauh[:, t * C:t * C + C], False, True)],
+           ["t0f", "dm", "rep80", "tauh0", "tauhr"], ["S1"], 2 * C)
+        tt(T.jj[:], T.S1[:, 0:C], T.lt[:], A.add, ["S1", "lt"], ["jj"], C, 1.0)
         mm([(T.S2[:, 0:C], T.sh[:], T.nak[:], True, True)], ["sh", "nak"], ["S2"], C)
-        ts(T.lv[:], T.S2[:, 0:C], pl, None, A.is_gt, None, ["S2", "pl"], ["lv"], C)
+        if "lv" in CFG["step"]:
+            act(T.lv[:], T.S2[:, 0:C], AF.Sigmoid, ["S2", "pl"], ["lv"], C, bias=pl, scale=400.0)
+        else:
+            ts(T.lv[:], T.S2[:, 0:C], 400.0, pl, A.mult, A.is_gt, ["S2", "pl"], ["lv"], C)
         rtk = ["rt%d" % j for j in range(len(segments()))] + ["rtz"]
         for j, bank in ((2, "S2"), (1, "S1"), (0, "S0")):
             t0, t1 = PARTS[j]
@@ -498,7 +523,7 @@ def build(g, core, T, topo, rank):
                 o = T[bank][:, C * (x - t0):C * (x - t0) + C]
                 lst += [(o, T.rt[:, C * x:C * x + C], T.jj[:], True, False), (o, T.ll[:, C * x:C * x + C], T.lv[:], False, True)]
             mm(lst, rtk + ["jj", "ll%d" % j, "lv"], [bank], 2 * nn)
-            ts(T.fc[:, C * t0:C * t1], T[bank][:, 0:nn], 0.0, 2048.0, A.max, A.min, [bank], ["fc%d" % j], nn)
+            ts(T.fc[:, C * t0:C * t1], T[bank][:, 0:nn], -2048.0, 2048.0, A.max, A.min, [bank], ["fc%d" % j], nn)
         tn = (t + 1) * C
         lst = [(T.S2[:, 0:C], T.rep8[:], T.tauh[:, tn:tn + C], True, False)]
         for h in range(2):
@@ -517,8 +542,8 @@ def build(g, core, T, topo, rank):
         tt(T.dn[64:C, 0:16], T.SY[64:C, 112:C], T.ru[64:C, 112:C], A.add, ["SY", "ru"], ["dn2"], 16, 1.0)
         weights(t)
         for b in range(4):
-            table(CFG["xm"][b], T.xm, "xm", X[t + 1], "x%d" % (t + 1), AX[t + 1], SI[t + 1], "si%d" % (t + 1), AS[t + 1], b, CFG["bm"][b],
-                  t0=M["x1"] if t == 0 else 0.0)
+            table("a", T.xm, "xm", X[t + 1], "x%d" % (t + 1), AX[t + 1], SI[t + 1], "si%d" % (t + 1), AS[t + 1], b, CFG["bm"][b],
+                  t0=M["x1"] if t == 0 else 0.0, plus=V)
             if b == 0:
                 act(T.xm[:, W:W + 1], T.xm[:, 0:1], AF.Copy, ["xm0"], ["xmc"], 1)
         parts(t + 1)
@@ -600,32 +625,47 @@ def schedule(ops):
         start = both_ways(start)
         if length(start) < length(best):
             best = start
-    return improve(ops, pred, succ, fore, first, final, sorted(range(nops), key=lambda i: (best[i], i)))
+    slow = [o["dur"] * M["slow"][o["eng"] == "pe"] for o in ops]
+    fore2 = [[(j, slow[j] + gap(j, i)) for j in pred[i]] for i in range(nops)]
+    return improve(ops, pred, succ, fore, fore2, slow, first, final, sorted(range(nops), key=lambda i: (best[i], i)))
 
 
-def improve(ops, pred, succ, fore, first, final, seq):
+def improve(ops, pred, succ, fore1, fore2, slow, first, final, seq):
     nops = len(ops)
     names = sorted(set(o["eng"] for o in ops))
     eng = [names.index(o["eng"]) for o in ops]
-    dur = [o["dur"] for o in ops]
+    sets = (([o["dur"] for o in ops], fore1, 1.0), (slow, fore2, M["weight"]))
 
-    def play(seq):
-        at, free, prev, last = [0.0] * nops, [0.0] * len(names), [-1] * nops, [-1] * len(names)
-        for i in seq:
+    ends = [i for i in range(nops) if not succ[i]]
+
+    def play(seq, p0, ats, prev0, old):
+        out = [play_one(seq, p0, ats[u], prev0, old, *sets[u]) for u in range(2)]
+        return [x[0] for x in out], out[0][1], [x[2] for x in out], out[0][3] + out[1][3]
+
+    def play_one(seq, p0, at0, prev0, old, dur, fore, weight):
+        at, prev, last = at0[:], prev0[:], [-2] * len(names)
+        for i in old:
+            if last[eng[i]] == -2:
+                last[eng[i]] = prev0[i]
+        for k in range(p0, nops):
+            i = seq[k]
             e = eng[i]
-            s = free[e] if free[e] > first[i] else first[i]
+            p = last[e] if last[e] != -2 else prev0[i]
+            s = at[p] + dur[p] if p >= 0 else 0.0
+            if first[i] > s:
+                s = first[i]
             for j, d in fore[i]:
                 if at[j] + d > s:
                     s = at[j] + d
-            at[i], free[e], prev[i], last[e] = s, s + dur[i], last[e], i
-        end = max(range(nops), key=lambda i: at[i] + dur[i] + final[i])
-        return at, prev, end, at[end] + dur[end] + final[end] + M["mean"] * sum(at) / nops
+            at[i], prev[i], last[e] = s, p, i
+        end = max(ends, key=lambda i: at[i] + dur[i] + final[i])
+        return at, prev, end, weight * (at[end] + dur[end] + final[end] + M["mean"] * sum(at) / nops)
 
-    at, prev, end, cost = play(seq)
-    top, held = (cost, seq, at), None
+    ats, prev, end, cost = play(seq, 0, [[0.0] * nops] * 2, [-1] * nops, [])
+    top, held = (cost, seq, ats[0]), None
     for it, r in enumerate(np.random.default_rng(M["seed"]).random((M["tries"], 6)).tolist()):
         if held is None:
-            held, i = [], end
+            (dur, fore, _), at, held, i = sets[it % 2], ats[it % 2], [], end[it % 2]
             while True:
                 c = [j for j, d in fore[i] if at[j] + d >= at[i] - 0.5]
                 p = prev[i]
@@ -636,29 +676,29 @@ def improve(ops, pred, succ, fore, first, final, seq):
                     break
                 i = c[int(r[0] * 997 + len(held)) % len(c)]
             pos = {x: k for k, x in enumerate(seq)}
-        b = held[int(r[1] * len(held))] if r[2] < 0.6 and held else int(r[1] * nops)
+        b = held[int(r[1] * len(held))] if r[2] < 0.7 and held else int(r[1] * nops)
         a = prev[b]
-        for _ in range(int(r[3] ** 3 * 8)):
+        for _ in range(int(r[3] ** 2 * 20)):
             if a >= 0 and prev[a] >= 0:
                 a = prev[a]
         if a < 0:
             continue
-        part = seq[pos[a]:pos[b] + 1]
+        old = seq[pos[a]:pos[b] + 1]
         ahead = r[4] < 0.5
         move = {b if ahead else a}
-        for x in (part[::-1] if ahead else part):
+        for x in (old[::-1] if ahead else old):
             if x in move:
                 move.update(pred[x] if ahead else succ[x])
         if a in move and b in move:
             continue
-        part = [x for x in part if (x in move) == ahead] + [x for x in part if (x in move) != ahead]
+        part = [x for x in old if (x in move) == ahead] + [x for x in old if (x in move) != ahead]
         new = seq[:pos[a]] + part + seq[pos[b] + 1:]
-        at2, prev2, end2, cost2 = play(new)
+        at2, prev2, end2, cost2 = play(new, pos[a], ats, prev, old)
         if cost2 <= cost - M["temp"] * (1.0 - it / M["tries"]) * math.log(r[5] + 1e-12):
-            seq = [new[k] for k in sorted(range(nops), key=lambda k: (at2[new[k]], k))]
-            at, prev, end, cost, held = at2, prev2, end2, cost2, None
+            seq = sorted(new, key=lambda i: at2[0][i])
+            ats, prev, end, cost, held = at2, prev2, end2, cost2, None
             if cost < top[0]:
-                top = (cost, seq, at)
+                top = (cost, seq, ats[0])
     return top[1], pred, top[2]
 
 
@@ -670,9 +710,9 @@ def rank_program(g, core, T, topo):
     if rank is None:
         return
     ops = build(g, core, T, topo, rank)
-    if len(ops) not in PLAN:
-        PLAN[len(ops)] = schedule(ops)
-    order, pred, start = PLAN[len(ops)]
+    if not PLAN:
+        PLAN["all ranks"] = schedule(ops)
+    order, pred, start = PLAN["all ranks"]
     queue = {"pe": g.tensor, "dve": g.vector, "act": g.scalar, "pool": g, "sp": g.sync}
     know = {q: {} for q in queue}
     count = {"pe": 0, "dve": 0, "act": 0, "pool": 0}

import math
import numpy as np
from concourse.bass import DstId, RemoteDMATransfer
from concourse.mybir import dt, AluOpType, AxisListType, ActivationFunctionType

BF, F32, I32, U16, F16 = "bfloat16", "float32", "int32", "uint16", "float16"
W, C, VI = 2048, 128, 4
V = 131072.0
CS = 85.0 / 64
BIG = 1.5 * 2.0 ** 32
BIG1 = 1.5 * 2.0 ** 23
LOW = math.log(1.0 / 8191)
SHIFT = 16.0
BIG2 = 1.5 * 2.0 ** 34
MID = 1023.5
STEP = 4096.0


def _sb(cols, dtype, rows=128):
    return ("sbuf", [rows, cols], dtype)


SCRATCH = {
    "x0": _sb(2064, BF), "x1": _sb(W, BF), "x2": _sb(W, BF), "x3": _sb(W, BF),
    "g0": _sb(2064, BF), "g1": _sb(2064, BF), "g2": _sb(2064, BF), "g3": _sb(W, BF),
    "xm": _sb(2064, BF), "xt": _sb(2064, BF), "gt": _sb(2064, BF),
    "ga0": _sb(W, BF), "ga1": _sb(W, BF), "ms0": _sb(W, BF), "ms1": _sb(W, BF),
    "xg": _sb(W, BF), "xl": _sb(W, BF), "ab": _sb(W, F32), "al": _sb(W, F32),
    "zz": _sb(W, F32), "za": _sb(W, F32), "zb": _sb(W, F32), "zc": _sb(W, F32), "zs": _sb(W, F32),
    "oha": _sb(4096, BF), "ohb": _sb(4096, BF), "qa": _sb(512, BF), "qb": _sb(576, BF), "less": _sb(512, BF, 8), "fc": _sb(1152, F16),
    "ivi": _sb(C, I32), "pfi": _sb(C, I32), "ivh": _sb(C, F16), "pff": _sb(C, F32),
    "taui": _sb(512, I32, 8), "tauh": _sb(512, F16, 8),
    "tr": _sb(C, BF), "t0f": _sb(C, F16), "off0": _sb(C, U16), "off1": _sb(C, U16),
    "tc": _sb(C, F32), "on": _sb(C, BF), "idv": _sb(C, BF), "ki": _sb(C, I32), "hii": _sb(C, I32), "loi": _sb(C, I32),
    "po0": _sb(C, U16), "po1": _sb(C, U16), "thr": _sb(C, F32),
    "rr": _sb(160, F16), "ff": _sb(160, F16), "mt": _sb(4 * C, BF), "si": _sb(4 * C, BF),
    "nak": _sb(C, BF), "lt": _sb(C, BF), "lv": _sb(C, BF), "jj": _sb(C, F16),
    "ru": _sb(C, F32), "dn": _sb(C, I32), "q0": _sb(2 * C, BF), "q1": _sb(2 * C, BF), "yo": _sb(C, F32),
    "onf": _sb(256, F32), "idw": _sb(256, F32), "id1": _sb(C, BF), "idc": _sb(C, BF), "id2": _sb(C, BF), "id64": _sb(C, BF),
    "idn": _sb(C, BF), "id8p": _sb(C, BF), "id8n": _sb(C, BF),
    "pvi": _sb(1, I32), "pw": _sb(4, I32), "pc": _sb(12, F32), "jr": _sb(160, I32), "jm": _sb(160, I32), "jb": _sb(160, I32),
    "gxb": _sb(160, BF),
    "blk": _sb(144, BF), "tri": _sb(144, BF), "ntri": _sb(144, BF), "c1": _sb(144, BF), "c3": _sb(C, BF), "c4": _sb(C, BF),
    "c5": _sb(C, BF), "c7": _sb(C, F32), "blk18": _sb(C, BF), "blk16": _sb(C, BF),
    "tx": _sb(C, BF), "tz": _sb(C, BF), "tq": _sb(2 * C, BF), "sh": _sb(C, BF), "dm": _sb(C, BF), "bo8": _sb(8, BF),
    "j16": _sb(512, BF), "sx": _sb(512, BF), "rep": _sb(1024, BF), "rep8": _sb(C, BF, 8), "rep80": _sb(C, BF, 8),
    "ones": _sb(512, BF), "fl": _sb(C, BF, 8), "selx": _sb(W, BF), "km": _sb(512, BF),
    "rt": _sb(1152, BF), "qt": _sb(1152, BF), "ll": _sb(1152, BF), "ft": _sb(1296, BF),
    "B0": ("psum", [128, 512], F32), "B1": ("psum", [128, 512], F32), "B2": ("psum", [128, 512], F32),
    "B3": ("psum", [128, 512], F32), "S0": ("psum", [128, 512], F32), "S1": ("psum", [128, 512], F32),
    "S2": ("psum", [128, 512], F32), "SY": ("psum", [128, 512], F32),
}
SEMAPHORES = (["pe", "dve", "act", "pool", "za10", "za11", "za20", "za21"] + ["ld%d" % i for i in range(16)] + ["ax1", "ax2", "ax3", "ag1", "ag2", "ag3",
              "as1", "as2", "as3"] + ["lo%d" % i for i in range(12)])
BANKS = ("B0", "B1", "B2", "B3", "S0", "S1", "S2", "SY")
M = {"cy": 0.9, "pe": 0.45, "hop": 110.0, "gc": 1.56, "vo": 35.0, "ao": 70.0, "po": 4.0, "sil": 3500.0, "x1": 17000.0,
     "bulk": {"x": 15000.0, "g": 13500.0, 1: 11000.0, 2: 11000.0}, "add": 5500.0,
     "rounds": 2, "tries": 200000, "seed": 1, "temp": 60.0, "mean": 0.3, "slow": (1.15, 1.7), "weight": 0.5}
CFG = {"hear": "adaaaaaa", "xt": "dada", "xg": "adad", "xgl": "dada", "scan": 2, "qb": 8, "step": "",
       "bh": "01230123", "bt": "b0c1", "bm": "2301", "bq": "2", "bz": "yyy3", "bg": "0b1c"}
BANK = dict(zip("0123abcy", BANKS))


def segments():
    out = []
    for t in range(4):
        s = t + 1
        out.append((t, 0, 17 - 2 * s, 2 * s - 1, s - 1, 1))
        out.append((t, 17 - 2 * s, 2 * s - 1, 17 - 2 * s, 8 - s, 1))
    for w in range(5):
        out.append((4 + w, 0, 16 - 2 * w, 0, 15 - w, 0))
        if 0 < w < 4:
            out.append((4 + w, 16 - 2 * w, 2 * w, 0, 7 + w, 0))
    return out


def near(topo, a, b):
    return b in topo.cores_of(a)


def routes(topo, cores):
    n, out = len(cores), []
    for s in range(n):
        holders = [s]
        for d in range(1, VI):
            r = (s - d) % n
            same = [h for h in holders if near(topo, cores[h], cores[r])]
            quiet = [h for h in holders if near(topo, cores[h], cores[(h - 1) % n])]
            out.append((s, d, (same or quiet or [s])[0]))
            holders.append(r)
    return out


def build(g, core, T, topo, rank):
    A, AF = AluOpType, ActivationFunctionType
    n = len(T.cores)
    ops = []
    CY = M["cy"]

    def op(eng, calls, r, w, dur, sem=None, inc=0, lat=0.0, ext=(), t0=0.0):
        ops.append({"eng": eng, "calls": calls, "r": list(r), "w": list(w), "dur": dur, "sem": sem, "inc": inc, "lat": lat,
                    "ext": [e for e in ext if e is not None], "t0": t0})

    def vd(n_, c):
        return max(64.0, n_ * c) * CY + M["vo"]

    def ts(out, in0, s1, s2, o0, o1, r, w, n_, c=1.0):
        if o1 is None:
            op("dve", [lambda: g.vector.tensor_scalar(out, in0, s1, None, o0)], r, w, vd(n_, c))
        else:
            op("dve", [lambda: g.vector.tensor_scalar(out, in0, s1, s2, o0, o1)], r, w, vd(n_, c))

    def tt(out, a, b, o, r, w, n_, c=2.0, ext=()):
        op("dve", [lambda: g.vector.tensor_tensor(out, a, b, o)], r, w, vd(n_, c), ext=ext)

    def cp(out, a, r, w, n_, c=1.0):
        op("dve", [lambda: g.vector.tensor_copy(out, a)], r, w, vd(n_, c))

    def ms(out, val, w, n_):
        op("dve", [lambda: g.vector.memset(out, val)], [], w, vd(n_, 0.5))

    def act(out, a, f, r, w, n_, c=1.0, bias=0.0, scale=1.0, extra=0.0):
        op("act", [lambda: g.scalar.activation(out, a, f, bias=bias, scale=scale)], r, w, n_ * c * CY + M["ao"] + extra)

    def below(name, out, a, lim, steep, r):
        if name in CFG["step"]:
            act(out, a, AF.Sigmoid, r, [name], C, bias=steep * lim, scale=-steep)
        else:
            ts(out, a, lim, None, A.is_lt, None, r, [name], C)

    def one_mm(m):
        return lambda: g.tensor.matmul(m[0], m[1], m[2], m[3], m[4])

    def mm(lst, r, w, cyc, ext=(), t0=0.0):
        op("pe", [one_mm(m) for m in lst], r, w, cyc * M["pe"] + M["po"] * len(lst), ext=ext, t0=t0)

    def iota(out, pat, base, cm, w, n_, flag=False):
        if flag:
            op("pool", [lambda: g.iota(out, pat, base, cm, allow_small_or_imprecise_dtypes=True)], [], w, 130 + 2 * n_ * CY)
        else:
            op("pool", [lambda: g.iota(out, pat, base, cm)], [], w, 130 + 2 * n_ * CY)

    def sel(out, src, skey, pat, base, w, n_, cmp=A.is_equal, cm=1, c0=0):
        op("pool", [lambda: g.affine_select(out, src[:, c0:c0 + n_], pat, cmp, 0.0, base, cm)], [skey], w, 170 + 2 * n_ * CY)

    nld = [0]

    def dma(q, out, a, r, w, lat):
        s = "ld%d" % nld[0]
        nld[0] += 1
        eng = g.sync if q == "sp" else g.scalar
        op(q, [lambda: eng.dma_start(out, a)], r, w, 100.0, sem=s, inc=16, lat=lat)

    def engines(src, dst):
        if not near(topo, src, dst):
            return topo.engines(src, dst)
        far = [c for c in T.cores if not near(topo, src, c)][0]
        return [e for e in topo.engines(src, dst) if e not in topo.engines(src, far)]

    nlo = [0]

    def fused(trs, s):
        return lambda: g.remote_dma_fused(trs, local_sem=T.sem[s])

    def send(groups, r, w, dur, lat, ext=()):
        s, calls, inc = "lo%d" % nlo[0], [], 0
        nlo[0] += 1
        for items in groups:
            trs = []
            for dst_rank, out, src, sem in items:
                d = T.cores[dst_rank % n]
                e = engines(core, d)
                rid, pid = topo.addr(d, core)
                trs.append(RemoteDMATransfer(dst_ids=[DstId(rid=rid, pnc=pid)], dma_engine_mask=sum(1 << x for x in e),
                                             remote_sem=T.sem[sem], src=src, dst=out))
                inc += len(e)
            calls.append(fused(trs, s))
        op("pool", calls, r, w, dur, sem=s, inc=inc, lat=lat, ext=ext)

    X = [T.x0, T.x1, T.x2, T.x3]
    G = [T.g0, T.g1, T.g2, T.g3]
    ident = T.idw[:, 0:C]
    ways = routes(topo, T.cores)
    sender = {d: h for s, d, h in ways if (s - d) % n == rank}
    AX = [None] + [("ax%d" % t, len(engines(T.cores[sender[t]], core))) for t in range(1, VI)]
    AG = [None] + [("ag%d" % t, len(engines(T.cores[sender[t]], core))) for t in range(1, VI)]
    AS = [None] + [("as%d" % t, len(engines(T.cores[(rank + 1) % n], core))) for t in range(1, VI)]
    quiet = near(topo, core, T.cores[(rank - 1) % n])

    def bulk(window, names):
        groups, ext = [], []
        for name in names:
            for held in range(VI - 1):
                mine = [(s, d) for s, d, h in ways if h == rank and (s - rank) % n == held]
                when = (0 if name == "x" or quiet else 1) if held == 0 else (1 if name == "x" else 2)
                if mine and when == window:
                    src = T["%s%d" % (name, held)][:, 0:W]
                    groups.append([(s - d, T["%s%d" % (name, d)][:, 0:W], src, "a%s%d" % (name, d)) for s, d in mine])
                    ext.append((AX if name == "x" else AG)[held])
        send(groups, [name + "0" for name in names] + ["sent"], [], 1000.0 * len(names), M["bulk"][window if window else names], ext)

    dma("act", T.x0[:, 0:W], T.xs[:], [], ["x0"], 3300)
    dma("sp", T.ivi[:], T.iv[:], [], ["ivi"], 2200)
    dma("sp", T.taui[:, 0:C], T.tau[:], [], ["taui0"], 2000)
    dma("sp", T.pfi[:], T.pf[:], [], ["pfi"], 2200)
    dma("sp", T.g0[:, 0:W], T.gn[:], [], ["g0"], 4500)
    for t in range(1, VI):
        dma("sp", T.taui[:, t * C:t * C + 64], T.tau[:, 0:64], [], ["taui%da" % t], 2000)
        dma("sp", T.taui[t:8, t * C + 64:t * C + C], T.tau[0:8 - t, 64:C], [], ["taui%db" % t], 2000)
        dma("sp", T.taui[0:t, t * C + 64:t * C + C], T.tau[8 - t:8, 64:C], [], ["taui%dc" % t], 2000)
    bulk(0, "x")
    bulk(0, "g")
    MT = [T.mt[:, C * t:C * t + C] for t in range(VI)]
    SI = [T.si[:, C * t:C * t + C] for t in range(VI)]

    iota(T.pvi[:], [[1, 1]], 0, 1, ["pvi"], 1)
    iota(T.jr[:], [[1, 160]], 96, 0, ["jr"], 160)
    iota(T.j16[:], [[1, 32], [0, 16]], 0, 0, ["j16"], 512, True)
    iota(T.less[:], [[-2, 8], [0, 64]], 0, 0, ["less"], 512, True)
    iota(T.sx[:], [[1, 4], [16, 8], [0, 16]], 0, -1, ["sx"], 512, True)
    ms(T.ones[:], 1.0, ["ones"], 512)
    ms(T.onf[:], 1.0, ["onf"], 512)
    sel(T.idw[:], T.onf, "onf", [[0, 2], [-1, C]], 0, ["idw"], 256)
    act(T.id1[:], ident, AF.Sigmoid, ["idw"], ["id1"], C, bias=-200.0, scale=400.0, extra=1300.0)
    for name, s in (("idc", 32 * CS), ("id64", 64.0), ("idn", -1.0), ("id8p", 8192.0), ("id8n", -8192.0), ("id2", 2.0), ("idv", -V)):
        act(T[name][:], ident, AF.Identity, ["idw"], [name], C, scale=s)
    ts(T.pw[:, 0:1], T.pvi[:], 112, None, A.bitwise_and, None, ["pvi"], ["pw0"], 1)
    ts(T.pw[:, 1:2], T.pvi[:], 15, None, A.bitwise_and, None, ["pvi"], ["pw1"], 1)
    ts(T.pw[:, 2:3], T.pvi[:], 63, None, A.bitwise_and, None, ["pvi"], ["pw2"], 1)
    pp, p16, pg, pl, pk, pn, pr, pa, pb = (T.pc[:, i:i + 1] for i in range(9))
    cp(pp, T.pvi[:], ["pvi"], ["pp"], 1)
    ts(p16, T.pvi[:], 16.0, None, A.mult, None, ["pvi"], ["p16"], 1)
    cp(pg, T.pw[:, 0:1], ["pw0"], ["pg"], 1)
    sg = -1.0 if "lv" in CFG["step"] else 1.0
    ts(T.pc[:, 9:10], T.pw[:, 1:2], 14.5, 400.0 * sg, A.is_lt, A.mult, ["pw1"], ["pl0"], 1)
    ts(pl, T.pc[:, 9:10], -200.0 * sg, None, A.add, None, ["pl0"], ["pl"], 1)
    ts(pk, T.pw[:, 1:2], STEP, None, A.mult, None, ["pw1"], ["pk"], 1)
    ts(pn, T.pw[:, 1:2], -STEP, None, A.mult, None, ["pw1"], ["pn"], 1)
    ts(pr, T.pw[:, 1:2], -STEP, 16 * STEP, A.mult, A.add, ["pw1"], ["pr"], 1)
    cp(pa, T.pw[:, 2:3], ["pw2"], ["pa"], 1)
    ts(pb, T.pw[:, 2:3], -32.0, None, A.add, None, ["pw2"], ["pb"], 1)
    ts(T.jm[:], T.jr[:], 127, None, A.bitwise_and, None, ["jr"], ["jm"], 160)
    ts(T.jb[:], T.jr[:], 112, None, A.bitwise_and, None, ["jr"], ["jb"], 160)
    ts(T.blk[:], T.jb[:, 16:160], pg, None, A.is_equal, None, ["jb", "pg"], ["blk"], 144)
    ts(T.c1[:], T.jm[:, 16:160], pp, None, A.is_ge, None, ["jm", "pp"], ["c1"], 144)
    tt(T.tri[:], T.c1[:], T.blk[:], A.mult, ["c1", "blk"], ["tri"], 144)
    ts(T.rep8[:], T.jb[0:8, 32:160], T.pc[0:8, 1:2], None, A.is_equal, None, ["jb", "p16"], ["rep8"], C)
    ts(T.rep80[:], T.jm[0:8, 32:160], T.pc[0:8, 1:2], -1.0, A.is_equal, A.mult, ["jm", "p16"], ["rep80"], C)
    ts(T.bo8[:], T.jm[:, 32:160:16], pg, 8192.0, A.is_equal, A.mult, ["jm", "pg"], ["bo8"], 8)
    for b, (col, key) in enumerate(((pa, "pa"), (pb, "pb"))):
        ts(T.rep[:, 512 * b:512 * b + 512], T.j16[:], col, -CS, A.is_equal, A.mult, ["j16", key], ["rep%d" % b], 512, 0.5)
    for b in range(4):
        ts(T.selx[:, 512 * b:512 * b + 512], T.sx[:], -4.0 * b, V, A.is_equal, A.mult, ["sx"], ["selx%d" % b], 512, 0.5)
    ts(T.gxb[:], T.jm[:], pg, 2.0 ** -13, A.is_equal, A.mult, ["jm", "pg"], ["gxb"], 160)
    blk = T.blk[:, 16:144]
    act(T.ntri[:], T.tri[:], AF.Identity, ["tri"], ["ntri"], 144, scale=-1.0)
    act(T.blk18[:], blk, AF.Identity, ["blk"], ["blk18"], C, scale=2 * V)
    act(T.blk16[:], blk, AF.Identity, ["blk"], ["blk16"], C, scale=1.0 / 16)
    tt(T.c3[:], blk, T.tri[:, 16:144], A.subtract, ["tri", "blk"], ["c3"], C)
    act(T.tx[:], T.c3[:], AF.Identity, ["c3"], ["tx"], C, scale=STEP)
    tt(T.c4[:], T.c3[:], blk, A.add, ["c3", "blk"], ["c4"], C)
    act(T.tz[:], T.c4[:], AF.Identity, ["c4"], ["tz"], C, scale=-STEP)
    ms(T.tq[:], 0.0, ["tq"], 2 * C)
    last_rows = T.blk[:, 31:144:16]
    ts(T.tx[:, 15:C:16], last_rows, pn, None, A.mult, None, ["blk", "pn"], ["tx"], 8)
    ts(T.tz[:, 15:C:16], last_rows, pk, None, A.mult, None, ["blk", "pk"], ["tz"], 8)
    ts(T.tq[:, 15:C:16], last_rows, pk, None, A.mult, None, ["blk", "pk"], ["tq"], 8)
    ts(T.tq[:, C + 15:2 * C:16], last_rows, pr, None, A.mult, None, ["blk", "pr"], ["tq"], 8)
    tt(T.c5[:], ident, T.idw[:, 1:C + 1], A.subtract, ["idw"], ["c5"], C)
    sel(T.sh[:], T.c5, "c5", [[0, 8], [-1, 16]], 15, ["sh"], C, A.is_gt, 0)
    sel(T.c7[:], T.idw, "idw", [[0, 8], [1, 16]], 0, ["c7"], C, A.is_gt, 0, C - 1)
    tt(T.dm[:], ident, T.c7[:], A.subtract, ["idw", "c7"], ["dm"], C)
    ms(T.rr[:], 0.0, ["rr0", "rr1"], 160)
    ms(T.ff[:], 0.0, ["ff0", "ff1"], 160)
    ms(T.fl[:], -15.0 / 256, ["fl"], C)
    ms(SI[0], 1.0, ["si0"], C)
    ms(T.xt[:, W:2064], -V, ["xtc"], 16)
    ms(T.gt[:, W:2064], 0.0, ["gtc"], 16)
    for t in range(VI - 1):
        ms(G[t][:, W:2064], 0.0, ["gc%d" % t], 16)
    sel(T.km[:], T.ones, "ones", [[0, 32], [1, 16]], 0, ["km"], 512, A.is_gt, 0)
    for name in ("rt", "qt"):
        ms(T[name][:, 1088:1152], 0.0, [name + "z"], 64)
    tk = {}
    for j, (tile, q0, nq, k0, d0, dstep) in enumerate(segments()):
        c0 = C * tile + 8 * q0
        sel(T.rt[:, c0:c0 + 8 * nq], T.ones, "ones", [[-16, 8], [-1, nq]], -k0, ["rt%d" % j], 8 * nq)
        sel(T.qt[:, c0:c0 + 8 * nq], T.ones, "ones", [[-16, 8], [-dstep, nq]], -d0, ["qt%d" % j], 8 * nq)
        tk.setdefault(tile, []).append(j)
    PARTS = ((0, 4), (4, 8), (8, 9))
    late_from = len(ops)
    for j, (t0, t1) in enumerate(PARTS):
        keys = [a + "%d" % x for t in range(t0, t1) for x in tk[t] for a in ("rt", "qt")] + ["rtz", "qtz"]
        nn = C * (t1 - t0)
        u, bk = 0 if j == 0 else C, ("B2", "B3")[j % 2]
        mm([(T[bk][:, 0:nn], (T.tx if j == 0 else T.tz)[:], T.rt[:, C * t0:C * t1], True, False),
            (T[bk][:, 0:nn], T.tq[:, u:u + C], T.qt[:, C * t0:C * t1], False, True)], keys + ["tx", "tz", "tq"], [bk], 2 * nn)
        act(T.ll[:, C * t0:C * t1], T[bk][:, 0:nn], AF.Copy, [bk], ["ll%d" % j], nn)
    for j in range(3):
        lst, bk = [], ("B3", "B2")[j % 2]
        for t in range(3 * j, 3 * j + 3):
            o = T[bk][:, 144 * (t % 3):144 * (t % 3) + 144]
            lst.append((o, T.qt[:, C * t:C * t + C], T.tri[:], True, t >= 4))
            if t < 4:
                lst.append((o, T.rt[:, C * t:C * t + C], T.ntri[:], False, True))
        mm(lst, [a + "%d" % x for t in range(3 * j, 3 * j + 3) for x in tk[t] for a in ("rt", "qt")] + ["qtz", "tri", "ntri"],
           [bk], 144 * len(lst))
        act(T.ft[:, 432 * j:432 * j + 432], T[bk][:, 0:432], AF.Copy, [bk], ["ft%d" % j], 432)
    late = ops[late_from:]
    del ops[late_from:]

    Q = [T.q0, T.q1]

    def parts(t):
        q, k = Q[t % 2], "q%d" % (t % 2)
        cp(q[0:64, 0:C], T.dn[0:64, :], ["dn0"], [k + "a"], C)
        cp(q[64:C, C:2 * C], T.dn[64:C, :], ["dn1", "dn2"], [k + "b"], C)
        tt(q[64:C, 0:C], T.dn[0:64, :], q[0:64, 0:C], A.subtract, ["dn0", k + "a"], [k + "c"], C)
        tt(q[0:64, C:2 * C], T.dn[64:C, :], q[64:C, C:2 * C], A.subtract, ["dn1", "dn2", k + "b"], [k + "d"], C)

    def minus_d(t, b, bk):
        q, k, h = Q[t % 2], "q%d" % (t % 2), b // 2
        mm([(T[bk][:], q[:, C * h:C * h + C], T.rep[:, 512 * (b % 2):512 * (b % 2) + 512], True, False)],
           [k + "ab"[h], k + "cd"[h], "rep%d" % (b % 2)], [bk], 512)

    def times(t):
        ts(T.tr[:], T.S2[:, 0:C], BIG2, -BIG2, A.add, A.add, ["S2"], ["tr"], C)
        tt(T.t0f[:], T.S2[:, 0:C], T.tr[:], A.subtract, ["S2", "tr"], ["t0f"], C, 1.0)
        ts(T.off0[:], T.t0f[:], MID, None, A.add, None, ["t0f"], ["off0"], C)
        ts(T.off1[:], T.t0f[:], MID + 1, None, A.add, None, ["t0f"], ["off1"], C)

    def table(eng, out, okey, src, skey, sext, msk, mkey, mext, b, bank, how=A.subtract, t0=0.0, plus=0.0):
        s, bk = slice(512 * b, 512 * b + 512), BANK[bank]
        with_x = eng == "a"
        if with_x:
            mm([(T[bk][:], T.idn[:], src[:, s], True, False)], [skey, "idn"], [bk], 512, [sext], t0)
        mm([(T[bk][:, C * j:C * j + C], T.selx[:, C * (4 * b + j):C * (4 * b + j) + C], msk, not with_x, (not with_x) or j == 3)
            for j in range(4)], [mkey, "selx%d" % b], [bk], 512, [mext])
        if eng == "a":
            act(out[:, s], T[bk][:], AF.Identity, [bk], [okey + "%d" % b], 512, bias=plus, scale=-1.0)
        else:
            tt(out[:, s], src[:, s], T[bk][:], how, [skey, bk], [okey + "%d" % b], 512, 1.0, ext=[sext])

    def gather(eng, out, win, off, r, w):
        if eng == "a":
            act(out, win.indirect(off), AF.Copy, r, w, 512, M["gc"])
        else:
            cp(out, win.indirect(off), r, w, 512, M["gc"])

    def weights(t):
        xg, ab = ("xg", "ab") if t < VI - 1 else ("xl", "al")
        for b in range(4):
            s, bk = slice(512 * b, 512 * b + 512), BANK[CFG["bz"][t]]
            minus_d(t, b, bk)
            mm([(T[bk][:], T.idc[:], T[xg][:, s], False, True)], [xg + "%d" % b, "idc"], [bk], 512)
            act(T[ab][:, s], T[bk][:], AF.Abs, [bk], [ab + "%d" % b], 512)
            act(T[ab][:, s], T[ab][:, s], AF.Sigmoid, [ab + "%d" % b], [ab + "%d" % b], 512,
                bias=-SHIFT - (math.log(V) if t == VI - 1 else 0.0), scale=-1.0 / (256 * CS))

    def terms(t, win, keys):
        po, ab, zk = "po%d" % (t % 2), "ab" if t < VI - 1 else "al", ("za", "zb", "zc", "zz")[t]
        for b in range(4):
            s = slice(512 * b, 512 * b + 512)
            tt(T[zk][:, s], win[:, 0:2064].indirect(T[po][:, 32 * b:32 * b + 32]), T[ab][:, s], A.mult,
               [ab + "%d" % b, po] + keys, [zk + "%d" % b], 512, M["gc"], ext=[AG[t]])
        if 0 < t < VI - 1:
            u = 16 * t
            pairs = ((T.za[:, 0:1024], T[zk][:, 0:1024]), (T.za[0:C - u, 1024:W], T[zk][u:C, 1024:W]), (T.za[C - u:C, 1024:W], T[zk][0:u, 1024:W]))
            for h, part in enumerate((pairs[:1], pairs[1:])):
                op("pool", [add_dma(o, a) for o, a in part], [zk + "%d" % (2 * h), zk + "%d" % (2 * h + 1)], ["za%d" % (2 * h), "za%d" % (2 * h + 1)],
                   1000.0 * len(part), sem="za%d%d" % (t, h), inc=16 * len(part), lat=M["add"])

    def add_dma(out, a):
        return lambda: g.dma_start(out, a, accum_op=A.add)

    def scan(out, data):
        return lambda: g.vector.tensor_tensor_scan(out, T.km[:], data, 0.0, A.mult, A.add)

    cp(T.ivh[:], T.ivi[:], ["ivi"], ["ivh"], C)
    ts(T.tauh[:, 0:C], T.taui[:, 0:C], -MID, None, A.add, None, ["taui0"], ["tauh0"], C)
    mm([(T.S2[:, 0:C], T.tri[:, 16:144], T.ivh[:], True, False), (T.S2[:, 0:C], T.rep8[:], T.tauh[:, 0:C], False, True)],
       ["tri", "ivh", "rep8", "tauh0"], ["S2"], 2 * C)
    cp(T.pff[:], T.pfi[:], ["pfi"], ["pff"], C)
    mm([(T.S0[:, 0:C], T.pff[:], ident, True, True)], ["pff", "idw"], ["S0"], 512)
    cp(T.dn[:], T.S0[:, 0:C], ["S0"], ["dn0", "dn1", "dn2"], C)
    parts(0)
    act(T.x0[:, W:W + 1], T.x0[:, 0:1], AF.Copy, ["x0"], ["x0c"], 1)
    ts(T.tauh[:, C:4 * C], T.taui[:, C:4 * C], -MID, None, A.add, None, ["taui%d%s" % (t, s) for t in (1, 2, 3) for s in "abc"], ["tauhr"], 3 * C)
    times(0)

    GA, MS, OFF = [T.ga0, T.ga1], [T.ms0, T.ms1], [T.off0, T.off1]
    R = CFG["qb"]
    for t in range(VI):
        last = t == VI - 1
        po = "po%d" % (t % 2)
        xw = T.x0 if t == 0 else T.xm
        xkeys = ["x0", "x0c"] if t == 0 else ["xm0", "xm1", "xm2", "xm3", "xmc"]
        for e in range(2):
            for b in range(4):
                s, bk = slice(512 * b, 512 * b + 512), BANK[CFG["bh"][4 * e + b]]
                gather(CFG["hear"][4 * e + b], GA[e][:, s], xw[:, 0:W + 1], OFF[e][:, 32 * b:32 * b + 32], xkeys + ["off%d" % e],
                       ["ga%d%d" % (e, b)])
                minus_d(t, b, bk)
                mm([(T[bk][:], T.idc[:], GA[e][:, s], False, True)], ["ga%d%d" % (e, b), "idc"], [bk], 512)
                ts(MS[e][:, s], T[bk][:], BIG, BIG, A.add, A.not_equal, [bk], ["ms%d%d" % (e, b)], 512)
            for q in range(2):
                mm([(T.S0[:, C * e + k:C * e + C:16], MS[e][:, k:W:16], T.bo8[:], e == 0, e == 0 or k == 15)
                    for k in range(8 * q, 8 * q + 8)], ["ms%d%d" % (e, b) for b in range(4)] + ["bo8"], ["S0"], 512)
            if e == 0:
                below("on", T.on[:], T.S0[:, 0:C], 36864.0, 0.05, ["S0"])
                mm([(T.S1[:, 0:C], T.t0f[:], T.id1[:], True, False)], ["t0f", "id1"], ["S1"], C)
                mm([(T.S1[:, 0:C], T.idn[:], T.on[:], False, True)], ["idn", "on"], ["S1"], C)
                act(T.tc[:], T.S1[:, 0:C], AF.Identity, ["S1"], ["tc"], C, bias=32769.0 + MID)
                mm([(T.S0[:, C:2 * C], T.idv[:], T.on[:], True, False)], ["idv", "on"], ["S0"], C)
                if not last:
                    mm([(T.S2[:, 0:C], T.on[:], T.id1[:], True, True)], ["id1", "on"], ["S2"], C)
                    act(T.thr[:], T.S2[:, 0:C], AF.Copy, ["S2"], ["thr"], C)
        tt(T.ki[:], T.S0[:, C:2 * C], T.tc[:], A.max, ["S0", "tc"], ["ki"], C, 1.0)
        ts(T.loi[:], T.ki[:], 63, None, A.bitwise_and, None, ["ki"], ["loi"], C)
        ts(T.hii[:], T.ki[:], 6, 0xD9F, A.arith_shift_right, A.bitwise_and, ["ki"], ["hii"], C)
        cp(T.qb[:, 0:C], T.loi[:], ["loi"], ["qb", "qc"], C)
        for h in range(2):
            bk = BANK[CFG["bq"]] if h == 0 else "qc"
            if h == 0:
                mm([(T[bk][:], T.ones[0:1, 0:C], T.less[0:1, :], True, False)], ["ones", "less"], [bk], 512)
                mm([(T[bk][:, 64 * s:64 * s + 64], T.id1[:], T.qb[:, 0:64], False, s == 7) for s in range(8)], ["id1", "qb"], [bk], 512)
            for r in (1, 2, 4)[:3 * h]:
                ts(T.qb[:, 64 + 64 * r:64 + 128 * r], T.qb[:, 64:64 + 64 * r], -2.0 * r, None, A.add, None, ["qb", bk], [bk], 64 * r, 0.5)
            c0, key = 256 * h, "qa%d" % h
            cp(T.qa[:, c0:c0 + 64], T.hii[:, 64 * h:64 * h + 64], ["hii"], [key + "0", key], 64)
            for r in (1, 2):
                ts(T.qa[:, c0 + 64 * r:c0 + 128 * r], T.qa[:, c0:c0 + 64 * r], -1.0 * r, None, A.add, None, [key], [key], 64 * r, 0.5)
            for a in range(8):
                c0 = 2048 * h + 256 * a
                ts(T.oha[:, c0:c0 + 256], T.qa[:, 256 * h:256 * h + 256], 4.0 * a, None, A.is_equal, None,
                   ["qa%d" % h], ["oha%d_%d" % (h, a)], 256, 0.5)
            for b in range(32 // R):
                c0 = 2048 * h + 64 * R * b
                act(T.ohb[:, c0:c0 + 64 * R], T.qb[:, 64:576] if h else T[bk][:], AF.Sigmoid, [bk, "id1"],
                    ["ohb%d_%d" % (h, b)], 64 * R, bias=LOW - 200.0 * R * b, scale=100.0)
        lst = []
        for h in range(2):
            lst.append((T.S0[64 * h:64 * h + 64, 0:C], T.qa[:, 256 * h:256 * h + 64], T.id64[:], True, False))
            lst.append((T.S0[64 * h:64 * h + 64, 0:C], T.qb[:, 64 * h:64 * h + 64], T.id1[:], False, True))
        mm(lst, ["qa00", "qa10", "qb", "id64", "id1"], ["S0"], 4 * C)
        ts(T[po][:], T.S0[:, 0:C], 2048.0, None, A.min, None, ["S0"], [po], C)
        if last:
            for b in range(4):
                gather(CFG["xgl"][b], T.xl[:, 512 * b:512 * b + 512], T.xm[:, 0:W + 1], T[po][:, 32 * b:32 * b + 32],
                       xkeys + [po], ["xl%d" % b])
            weights(t)
            for q in range(8):
                mm([(T.SY[:, 0:C], ident, T.za[:, k:W:16], k == 0, False) for k in (2 * q, 2 * q + 1)],
                   ["za0", "za1", "za2", "za3", "idw"], ["SY"], 1024)
        if t == 0:
            ops.extend(late)
        for h in range(2):
            H, hk = (T.S1, "S1") if h == 0 else (T.S2, "S2")
            for p in range(2):
                c0 = 2048 * h + 16 * p
                for q in range(2):
                    mm([(H[64 * p:64 * p + 64, 0:64], T.oha[:, c0 + k:2048 * h + 2048:32], T.ohb[:, c0 + k:2048 * h + 2048:32],
                         k == 0, k == 15) for k in range(8 * q, 8 * q + 8)],
                       ["oha%d_%d" % (h, a) for a in range(8)] + ["ohb%d_%d" % (h, b) for b in range(32 // R)], [hk], 8 * 64)
            c0 = 80 * h
            ts(T.rr[:, c0:c0 + 64], H[:, 0:64], BIG1, -BIG1, A.add, A.add, [hk], ["rr%d" % h], 64)
            tt(T.ff[:, c0:c0 + 64], H[:, 0:64], T.rr[:, c0:c0 + 64], A.subtract, [hk, "rr%d" % h], ["ff%d" % h], 64, 1.0)
            lst = []
            for u in range(2):
                here, on = slice(c0 + u, c0 + 64, 2), slice(c0 + u + 2, c0 + 66, 2)
                for a in range(2):
                    pick = slice(2 * a + u, C, 4)
                    even, odd = (T.S0[64 * h + 32 * u:64 * h + 32 * u + 32, C + 64 * a + p:C + 64 * a + 64:2] for p in range(2))
                    lst += [(even, T.id8p[:, pick], T.ff[:, here], True, True), (odd, T.id1[:, pick], T.rr[:, here], True, False),
                            (odd, T.idn[:, pick], T.rr[:, on], False, False),
                            (odd, T.id8n[:, pick], T.ff[:, on], False, True)]
            mm(lst, ["rr%d" % h, "ff%d" % h, "id1", "idn", "id8p", "id8n"], ["S0"], 512)
        mk = "mt%d" % t
        tt(MT[t], T.S0[:, C:2 * C], SI[t], A.is_equal if last else A.not_equal, ["S0", "si%d" % t], [mk], C, 1.0, ext=[AS[t]])
        if last:
            for b in range(4):
                table("d", T.gt, "gt", G[t], "g%d" % t, AG[t], MT[t], mk, None, b, CFG["bg"][b], A.mult)
            terms(t, T.gt, ["gt0", "gt1", "gt2", "gt3", "gtc"])
            for q in range(4 if CFG["scan"] == 2 else 0):
                mm([(T.SY[:, 0:64], ident, T.zz[:, k:1024:16], False, False) for k in range(4 * q, 4 * q + 4)],
                   ["zz0", "zz1", "idw"], ["SY"], 1024)
            for b in range(4 - CFG["scan"], 4):
                zs, w0 = T.zs[:, 512 * b:512 * b + 512], 16 * t * (b // 2)
                op("dve", [scan(zs, T.zz[:, 512 * b:512 * b + 512])], ["km", "zz%d" % b], ["zs%d" % b], vd(512, 1.0))
                mm([(T.SY[:, 32 * b:32 * b + 32], T.idw[:, w0:w0 + C], T.zs[:, 512 * b + 15:512 * b + 512:16], False, b == 3)],
                   ["zs%d" % b, "idw"], ["SY"], 256)
            break
        send([[(rank - 1, SI[t + 1], MT[t], "as%d" % (t + 1))]], [mk], ["si%d" % (t + 1), "sent"], 1000.0, M["sil"])
        if t < VI - 2:
            bulk(t + 1, "xg")
        for b in range(4):
            table(CFG["xt"][b], T.xt, "xt", X[t], "x%d" % t, AX[t], MT[t], mk, None, b, CFG["bt"][b])
        for b in range(4):
            gather(CFG["xg"][b], T.xg[:, 512 * b:512 * b + 512], T.xt[:, 0:W + 1], T[po][:, 32 * b:32 * b + 32],
                   ["xt0", "xt1", "xt2", "xt3", "xtc", po], ["xg%d" % b])
        xgk = ["xg0", "xg1", "xg2", "xg3"]
        for h in range(2):
            mm([(T.S0[:, 64 * h:64 * h + 64], T.gxb[:, 32 - k:160 - k], T.xg[:, 1024 * h + k:1024 * h + 1024:16], k == 0, k == 15)
                for k in range(16)], xgk[2 * h:2 * h + 2] + ["gxb"], ["S0"], 1024)
        for q in range(4):
            mm([(T.SY[:, 0:C], T.xg[:, k:W:16], T.id2[:], k == 0, False) for k in range(4 * q, 4 * q + 4)], xgk + ["id2"], ["SY"], 512)
        tt(T.lt[:], T.S0[:, 0:C], T.thr[:], A.is_gt, ["S0", "thr"], ["lt"], C, 1.0)
        below("nak", T.nak[:], T.S0[:, 0:C], -128.0, 1.0, ["S0"])
        mm([(T.S1[:, 0:C], T.dm[:], T.t0f[:], True, False), (T.S1[:, 0:C], T.rep80[:], T.tauh[:, t * C:t * C + C], False, True)],
           ["t0f", "dm", "rep80", "tauh0", "tauhr"], ["S1"], 2 * C)
        tt(T.jj[:], T.S1[:, 0:C], T.lt[:], A.add, ["S1", "lt"], ["jj"], C, 1.0)
        mm([(T.S2[:, 0:C], T.sh[:], T.nak[:], True, True)], ["sh", "nak"], ["S2"], C)
        if "lv" in CFG["step"]:
            act(T.lv[:], T.S2[:, 0:C], AF.Sigmoid, ["S2", "pl"], ["lv"], C, bias=pl, scale=400.0)
        else:
            ts(T.lv[:], T.S2[:, 0:C], 400.0, pl, A.mult, A.is_gt, ["S2", "pl"], ["lv"], C)
        rtk = ["rt%d" % j for j in range(len(segments()))] + ["rtz"]
        for j, bank in ((2, "S2"), (1, "S1"), (0, "S0")):
            t0, t1 = PARTS[j]
            nn = C * (t1 - t0)
            lst = []
            for x in range(t0, t1):
                o = T[bank][:, C * (x - t0):C * (x - t0) + C]
                lst += [(o, T.rt[:, C * x:C * x + C], T.jj[:], True, False), (o, T.ll[:, C * x:C * x + C], T.lv[:], False, True)]
            mm(lst, rtk + ["jj", "ll%d" % j, "lv"], [bank], 2 * nn)
            ts(T.fc[:, C * t0:C * t1], T[bank][:, 0:nn], -2048.0, 2048.0, A.max, A.min, [bank], ["fc%d" % j], nn)
        tn = (t + 1) * C
        lst = [(T.S2[:, 0:C], T.rep8[:], T.tauh[:, tn:tn + C], True, False)]
        for h in range(2):
            lst.append((T.S2[:, 64 * h:64 * h + 64], T.tri[:, 16 - 16 * h:144 - 16 * h], T.jj[:, 64 * h:64 * h + 64], False, False))
        mm(lst, ["rep8", "tauhr", "tri", "jj"], ["S2"], 2 * C)
        for j in (2, 1, 0):
            t0, t1 = PARTS[j]
            mm([(T.S2[:, 64 * h:64 * h + 64], T.ft[:, 144 * x + 16 - 16 * h:144 * x + 144 - 16 * h],
                 T.fc[:, C * x + 64 * h:C * x + 64 * h + 64], False, j == 0 and x == t1 - 1 and h == 1)
                for x in range(t0, t1) for h in range(2)], ["fc%d" % j, "ft0", "ft1", "ft2"], ["S2"], C * (t1 - t0))
        mm([(T.SY[:, 0:C], T.nak[:], T.blk18[:], False, False), (T.SY[:, 0:C], T.ones[0:8, 0:C], T.fl[:], False, True),
            (T.SY[:, C:2 * C], T.nak[:], T.blk16[:], True, True)], ["nak", "blk18", "blk16", "ones", "fl"], ["SY"], 3 * C)
        tt(T.ru[:], T.SY[:, C:2 * C], T.dn[:], A.mult, ["SY", "dn0", "dn1", "dn2"], ["ru"], C, 1.0)
        tt(T.dn[0:64, :], T.SY[0:64, 0:C], T.ru[0:64, :], A.add, ["SY", "ru"], ["dn0"], C, 1.0)
        tt(T.dn[64:C, 16:C], T.SY[64:C, 0:112], T.ru[64:C, 0:112], A.add, ["SY", "ru"], ["dn1"], 112, 1.0)
        tt(T.dn[64:C, 0:16], T.SY[64:C, 112:C], T.ru[64:C, 112:C], A.add, ["SY", "ru"], ["dn2"], 16, 1.0)
        weights(t)
        for b in range(4):
            table("a", T.xm, "xm", X[t + 1], "x%d" % (t + 1), AX[t + 1], SI[t + 1], "si%d" % (t + 1), AS[t + 1], b, CFG["bm"][b],
                  t0=M["x1"] if t == 0 else 0.0, plus=V)
            if b == 0:
                act(T.xm[:, W:W + 1], T.xm[:, 0:1], AF.Copy, ["xm0"], ["xmc"], 1)
        parts(t + 1)
        times(t + 1)
        terms(t, G[t], ["gc%d" % t, "g%d" % t])
    act(T.yo[:], T.SY[:, 0:C], AF.Identity, ["SY"], ["yo"], C, scale=math.exp(SHIFT))
    dma("sp", T.y[:], T.yo[:], ["yo"], [], 2000)
    return ops


def schedule(ops):
    nops = len(ops)
    lastw, readers = {}, {}
    pred = [set() for _ in ops]
    for i, o in enumerate(ops):
        rd, wr = o["r"], o["w"]
        for k in rd:
            if k in lastw:
                pred[i].add(lastw[k])
            if k in BANKS:
                pred[i].update(j for j in readers.get(k, ()) if ops[j]["eng"] != o["eng"])
        for k in wr:
            if k in lastw:
                pred[i].add(lastw[k])
            pred[i].update(readers.get(k, ()))
        for k in rd:
            readers.setdefault(k, []).append(i)
        for k in wr:
            lastw[k] = i
            readers[k] = []
        pred[i].discard(i)
    succ = [[] for _ in ops]
    for i in range(nops):
        for j in pred[i]:
            succ[j].append(i)

    def gap(j, i):
        if "sent" in ops[j]["w"] and "sent" in ops[i]["r"]:
            return 0.0
        return ops[j]["lat"] + (0.0 if ops[j]["eng"] == ops[i]["eng"] == "pe" else M["hop"])

    fore = [[(j, ops[j]["dur"] + gap(j, i)) for j in pred[i]] for i in range(nops)]
    back = [[(k, ops[k]["dur"] + gap(i, k)) for k in succ[i]] for i in range(nops)]
    prio = [0.0] * nops
    for i in range(nops - 1, -1, -1):
        prio[i] = ops[i]["dur"] + max([gap(i, k) + prio[k] for k in succ[i]] + [ops[i]["lat"]])
    first = [o["t0"] for o in ops]
    final = [0.0 if succ[i] else ops[i]["lat"] for i in range(nops)]

    def place(seq, before, low):
        at, busy = [0.0] * nops, {}
        for i in seq:
            s = low[i]
            for j, d in before[i]:
                if at[j] + d > s:
                    s = at[j] + d
            lst = busy.setdefault(ops[i]["eng"], [])
            d = ops[i]["dur"]
            pos = len(lst)
            while pos > 0 and lst[pos - 1][1] > s:
                pos -= 1
            while pos < len(lst) and s + d > lst[pos][0]:
                s = max(s, lst[pos][1])
                pos += 1
            lst.insert(pos, (s, s + d))
            at[i] = s
        return at

    def length(at):
        return max(at[i] + ops[i]["dur"] + final[i] for i in range(nops))

    def both_ways(start):
        rev = place(sorted(range(nops), key=lambda i: (-(start[i] + ops[i]["dur"]), -i)), back, final)
        return place(sorted(range(nops), key=lambda i: (-(rev[i] + ops[i]["dur"]), i)), fore, first)

    start = place(sorted(range(nops), key=lambda i: (-prio[i], i)), fore, first)
    best = start
    for _ in range(M["rounds"]):
        start = both_ways(start)
        if length(start) < length(best):
            best = start
    slow = [o["dur"] * M["slow"][o["eng"] == "pe"] for o in ops]
    fore2 = [[(j, slow[j] + gap(j, i)) for j in pred[i]] for i in range(nops)]
    return improve(ops, pred, succ, fore, fore2, slow, first, final, sorted(range(nops), key=lambda i: (best[i], i)))


def improve(ops, pred, succ, fore1, fore2, slow, first, final, seq):
    nops = len(ops)
    names = sorted(set(o["eng"] for o in ops))
    eng = [names.index(o["eng"]) for o in ops]
    sets = (([o["dur"] for o in ops], fore1, 1.0), (slow, fore2, M["weight"]))

    ends = [i for i in range(nops) if not succ[i]]

    def play(seq, p0, ats, prev0, old):
        out = [play_one(seq, p0, ats[u], prev0, old, *sets[u]) for u in range(2)]
        return [x[0] for x in out], out[0][1], [x[2] for x in out], out[0][3] + out[1][3]

    def play_one(seq, p0, at0, prev0, old, dur, fore, weight):
        at, prev, last = at0[:], prev0[:], [-2] * len(names)
        for i in old:
            if last[eng[i]] == -2:
                last[eng[i]] = prev0[i]
        for k in range(p0, nops):
            i = seq[k]
            e = eng[i]
            p = last[e] if last[e] != -2 else prev0[i]
            s = at[p] + dur[p] if p >= 0 else 0.0
            if first[i] > s:
                s = first[i]
            for j, d in fore[i]:
                if at[j] + d > s:
                    s = at[j] + d
            at[i], prev[i], last[e] = s, p, i
        end = max(ends, key=lambda i: at[i] + dur[i] + final[i])
        return at, prev, end, weight * (at[end] + dur[end] + final[end] + M["mean"] * sum(at) / nops)

    ats, prev, end, cost = play(seq, 0, [[0.0] * nops] * 2, [-1] * nops, [])
    top, held = (cost, seq, ats[0]), None
    for it, r in enumerate(np.random.default_rng(M["seed"]).random((M["tries"], 6)).tolist()):
        if held is None:
            (dur, fore, _), at, held, i = sets[it % 2], ats[it % 2], [], end[it % 2]
            while True:
                c = [j for j, d in fore[i] if at[j] + d >= at[i] - 0.5]
                p = prev[i]
                if p >= 0 and at[p] + dur[p] >= at[i] - 0.5 and p not in pred[i]:
                    held.append(i)
                    c.append(p)
                if not c:
                    break
                i = c[int(r[0] * 997 + len(held)) % len(c)]
            pos = {x: k for k, x in enumerate(seq)}
        b = held[int(r[1] * len(held))] if r[2] < 0.7 and held else int(r[1] * nops)
        a = prev[b]
        for _ in range(int(r[3] ** 2 * 20)):
            if a >= 0 and prev[a] >= 0:
                a = prev[a]
        if a < 0:
            continue
        old = seq[pos[a]:pos[b] + 1]
        ahead = r[4] < 0.5
        move = {b if ahead else a}
        for x in (old[::-1] if ahead else old):
            if x in move:
                move.update(pred[x] if ahead else succ[x])
        if a in move and b in move:
            continue
        part = [x for x in old if (x in move) == ahead] + [x for x in old if (x in move) != ahead]
        new = seq[:pos[a]] + part + seq[pos[b] + 1:]
        at2, prev2, end2, cost2 = play(new, pos[a], ats, prev, old)
        if cost2 <= cost - M["temp"] * (1.0 - it / M["tries"]) * math.log(r[5] + 1e-12):
            seq = sorted(new, key=lambda i: at2[0][i])
            ats, prev, end, cost, held = at2, prev2, end2, cost2, None
            if cost < top[0]:
                top = (cost, seq, ats[0])
    return top[1], pred, top[2]


PLAN = {}


def rank_program(g, core, T, topo):
    rank = T.rank_of(core)
    if rank is None:
        return
    ops = build(g, core, T, topo, rank)
    if not PLAN:
        PLAN["all ranks"] = schedule(ops)
    order, pred, start = PLAN["all ranks"]
    queue = {"pe": g.tensor, "dve": g.vector, "act": g.scalar, "pool": g, "sp": g.sync}
    know = {q: {} for q in queue}
    count = {"pe": 0, "dve": 0, "act": 0, "pool": 0}
    done, snap, total = {}, {}, {}
    for i in order:
        o = ops[i]
        q, kn = o["eng"], know[o["eng"]]
        need = [(e[0], e[1], None) for e in o["ext"]]
        for j in pred[i]:
            pj = ops[j]
            if pj["eng"] == q and q == "pe":
                continue
            if pj["sem"] is not None and pj["sem"].startswith("lo"):
                continue
            if pj["eng"] == q == "pool" and "sent" in o["w"]:
                continue
            need.append((done[j][0], done[j][1], j))
        need.sort(key=lambda x: -(start[x[2]] if x[2] is not None else -1.0))
        for sem, val, j in need:
            if kn.get(sem, 0) < val:
                queue[q].wait_ge(T.sem[sem], val)
                kn[sem] = val
                if j is not None:
                    for s2, v2 in snap[j].items():
                        if kn.get(s2, 0) < v2:
                            kn[s2] = v2
        snap[i] = dict(kn)
        if o["sem"] is None:
            for call in o["calls"]:
                call().then_inc(T.sem[q], 1)
            count[q] += len(o["calls"])
            done[i] = (q, count[q])
        else:
            for call in o["calls"]:
                ins = call()
                if not o["sem"].startswith("lo"):
                    ins.then_inc(T.sem[o["sem"]], 16)
            done[i] = (o["sem"], o["inc"])
        total[done[i][0]] = done[i][1]
        for e in o["ext"]:
            total[e[0]] = e[1]
    for sem, val in total.items():
        if max(know[q].get(sem, 0) for q in know) < val:
            g.wait_ge(T.sem[sem], val)
